import numpy as np, ml_dtypes
CORES = [2,6,10,14,18,22,26,30]
N = 8
BF = ml_dtypes.bfloat16
def gentries(a):
    return np.ascontiguousarray(a.reshape(8, 16, -1).transpose(0, 2, 1)).reshape(8, -1)
def gtable(e):
    e = np.asarray(e); return np.ascontiguousarray(e.reshape(8, -1, 16).transpose(0, 2, 1)).reshape(128, -1).astype(np.int32)
L, E, H, RO = 3, 256, 3, 2
V = L * E; W = (1 + H) * V
def feed(rng, far, void):
    x = rng.integers(V, W, (N, 8, 16, V))
    for l in range(1, L):
        s = slice(l * E, (l + 1) * E); own = rng.integers(0, l * E, (N, 8, 16, E))
        x[..., s] = np.where(rng.random(own.shape) < far, x[..., s], own)
    return np.where(rng.random(x.shape) < void, -1, x)
def edges(rng):
    x = np.zeros((N, 8, 16, V), np.int64)
    for l in range(L):
        few = np.array(([0, l * E - 1, V, W - 1] if l else [V, 2 * V - 1, W - 1]) + ([2 * V, H * V] if H > 1 else []))
        x[..., l * E:(l + 1) * E] = rng.choice(few, (N, 8, 16, E))
    return x
def links(rng):
    return np.argsort(rng.random((N, 8, L, E)), axis=-1).reshape(N, 8, V)
def first(rng, empty):
    cf = rng.integers(V, W, (N, 8, E))
    return np.where(rng.random(cf.shape) < empty, -1, cf), rng.integers(0, 17, (N, 8, E))
def near(rng, base):
    return np.clip(base + rng.integers(-20, 21, (N, 8, 16, V)), 0, 255)
def pack(fd, pw, bs, dl, nx, t0, cf, cw):
    def lanes(a): return np.ascontiguousarray(a.reshape(N, 128, V)).astype(np.float32).astype(BF)
    return {"fd": np.ascontiguousarray(fd.reshape(N, 128, V)).astype(np.int32), "pw": lanes(pw), "bs": lanes(bs), "t0": lanes(t0),
            "dl": dl.astype(np.int32), "nx": np.stack([gtable(a) for a in nx]), "cf": cf.astype(np.int32), "cw": cw.astype(np.int32)}
def setup_inputs(rng):
    base = rng.integers(0, 236, (N, 8, 1, V)); void = rng.choice(np.array([0.0, 0.05, 0.2, 0.7]), (N, 8, 1, V))
    pw = np.minimum((17 * rng.random((N, 8, 16, V)) ** 2).astype(np.int64), 16)
    pw = np.where(rng.random((N, 8, 1, V)) < 0.125, pw[:, :, :1], pw)
    cf, cw = first(rng, 0.25)
    return pack(feed(rng, 0.4, void), pw, near(rng, base), rng.integers(1, 5, (N, 8, V)), links(rng), near(rng, base), cf, cw)
def setup_inputs_spread(rng):
    bs = np.minimum((np.exp2(8 * rng.random((N, 8, 1, V))) * rng.random((N, 8, 16, V))).astype(np.int64), 255)
    t0 = np.minimum((np.exp2(8 * rng.random((N, 8, 1, V))) * rng.random((N, 8, 16, V))).astype(np.int64), 255)
    bs = np.where(rng.random(bs.shape) < 0.02, 255, bs); t0 = np.where(rng.random(t0.shape) < 0.02, 255, t0)
    pw = np.minimum((17 * rng.random((N, 8, 16, V)) ** rng.choice(np.array([0.5, 1.0, 3.0, 8.0]), (N, 8, 1, V))).astype(np.int64), 16)
    x = feed(rng, rng.choice(np.array([0.05, 0.5, 0.95]), (N, 8, 1, 1)), rng.random((N, 8, 1, V)) ** 2)
    crowd = V + ((x - V) * rng.random(x.shape) ** 3).astype(np.int64)
    x = np.where((x >= V) & (np.arange(8)[None, :, None, None] % 2 == 1), crowd, x)
    cf, cw = first(rng, 0.4)
    return pack(x, pw, bs, rng.choice(np.array([1, 1, 1, 2, 3, 4]), (N, 8, V)), links(rng), t0, cf, cw)
def setup_inputs_ends(rng):
    def two():
        m = rng.choice(np.array([0, 1, 2]), (N, 8, 1, V), p=[0.45, 0.2, 0.35])
        return 255 * np.where(m == 2, rng.integers(0, 2, (N, 8, 16, V)), m)
    bs = two(); t0 = two()
    pw = 16 * (rng.random((N, 8, 16, V)) < rng.choice(np.array([0.0, 0.06, 1.0]), (N, 8, 1, V), p=[0.6, 0.3, 0.1])).astype(np.int64)
    u = rng.random((N, 8, 16, V)); x = np.where(u < 0.35, -1, np.where(u < 0.75, W - 1, edges(rng)))
    bs[N - 1, 7, :, V - 1] = 255; t0[N - 1, 7, :, V - 1] = 255; pw[N - 1, 7, :, V - 1] = 0
    t0[N - 1 - H, 7 - H, :, V - 1] = 255; bs[N - 1, 7, :, E - 1] = 0; t0[N - 1, 7, :, E - 1] = 0; pw[N - 1, 7, :, E - 1] = 0; x[N - 1, 7, :, E - 1] = W - 1
    mid = 1 + np.argsort(rng.random((N, 8, L, E - 2)), axis=-1); one = np.ones((N, 8, L, 1), np.int64)
    nx = np.where(rng.random((N, 8, L, 1)) < 0.5, np.arange(E)[::-1], np.concatenate([(E - 1) * one, mid, 0 * one], axis=-1))
    c = rng.random((N, 8, E)); cf = np.where(c < 0.45, -1, np.where(c < 0.85, W - 1, V)); cf[N - 1, 7, E - 1] = W - 1
    return pack(x, pw, bs, 1 + 3 * rng.integers(0, 2, (N, 8, V)), nx.reshape(N, 8, V), t0, cf, 16 * rng.integers(0, 2, (N, 8, E)))
def setup_inputs_corners(rng):
    kd = np.argsort(rng.random((N, 8)), axis=1)[:, :, None, None]; ke = kd[..., 0]
    base = rng.integers(0, 236, (N, 8, 1, V)); bs = near(rng, base); t0 = near(rng, base); e = rng.random((N, 8, 1, V))
    bs = np.where(e < 0.1, 0, np.where(e < 0.15, 255, bs)); t0 = np.where(e < 0.05, 0, np.where((e > 0.12) & (e < 0.2), 255, t0))
    nv = rng.choice(np.array([0, 1, 15, 16]), (N, 8, 1, V))
    for k, n in ((0, 0), (1, 16), (2, 0), (3, 1), (4, 15)): nv = np.where(kd == k, n, nv)
    x = np.where(kd == 5, edges(rng), feed(rng, 0.5, 0.0))
    x = np.where(np.argsort(rng.random((N, 8, 16, V)), axis=2) < nv, -1, x)
    pw = rng.integers(0, 17, (N, 8, 16, V))
    pw = np.where(kd == 3, pw[:, :, :1], np.where(kd == 5, 16 * rng.integers(0, 2, pw.shape), np.where(kd == 0, 16, np.where(kd == 2, 0, pw))))
    cf, cw = first(rng, 0.3); full, heavy = first(rng, 0.0)
    cf = np.where(ke == 1, -1, np.where((ke == 0) | (ke == 2) | (ke == 4), full, cf))
    cw = np.where(ke == 0, rng.choice(np.array([0, 15, 16]), cw.shape), np.where(ke == 2, 0, np.where(ke == 4, 16, cw)))
    return pack(x, pw, bs, rng.integers(1, 5, (N, 8, V)), links(rng), t0, cf, cw)
def setup_inputs_heavy(rng):
    late = np.arange(V) >= E
    bs = rng.integers(0, 201, (N, 8, 16, V)); t0 = rng.integers(1, 151, (N, 8, 16, V))
    low = late & (rng.random((N, 8, 1, V)) < 0.4); bs = np.where(low, 0, bs); t0 = np.where(low, 0, t0)
    n15 = rng.choice(np.array([0, 0, 1, 1, 2, 16]), (N, 8, 1, V))
    pw = np.where(np.argsort(rng.random((N, 8, 16, V)), axis=2) < n15, 15, 16)
    light = late & (rng.random((N, 8, 1, V)) < 0.75); pw = np.where(light, rng.integers(0, 15, pw.shape), pw)
    x = feed(rng, 0.5, np.where(light, 0.2, 0.0))
    cf, cw = first(rng, 0.1); cw = rng.choice(np.array([16, 16, 16, 15]), cw.shape)
    return pack(x, pw, bs, rng.integers(1, 5, (N, 8, V)), links(rng), t0, cf, cw)
def setup_inputs_ties(rng):
    lv = 3 * np.repeat(np.arange(L), E)
    bs = 60 + lv + rng.integers(0, 4, (N, 8, 16, V)); t0 = 60 + lv + rng.integers(0, 4, (N, 8, 16, V))
    lift = (rng.random((N, 8, 16, V)) < 0.3) & (rng.random((N, 8, 1, V)) < 0.5)
    pw = rng.choice(np.array([4, 8, 8, 9, 12, 15]), (N, 8, 1, V)) + lift.astype(np.int64)
    x = feed(rng, 0.5, rng.choice(np.array([0.0, 0.0, 0.1]), (N, 8, 1, V)))
    cf, cw = first(rng, 0.1); cw = rng.choice(np.array([4, 8, 9, 12]), cw.shape)
    return pack(x, pw, bs, 1 + 3 * (rng.random((N, 8, V)) < 0.2).astype(np.int64), links(rng), t0, cf, cw)
def check_inputs(d):
    bad = []
    for k, lo, hi in (("fd", -1, W - 1), ("pw", 0, 16), ("bs", 0, 255), ("t0", 0, 255), ("dl", 1, 4), ("nx", 0, E - 1), ("cf", -1, W - 1), ("cw", 0, 16)):
        a = np.asarray(d[k]).astype(np.float64)
        if not (np.all(a >= lo) and np.all(a <= hi) and np.all(a == np.floor(a))): bad.append("range of " + k)
    x = d["fd"].reshape(N, 128, L, E); c = d["cf"]
    if np.any((x < V) & (x >= (np.arange(L) * E)[None, None, :, None])): bad.append("own feeders of fd lie in earlier levels")
    if np.any((c >= 0) & (c < V)): bad.append("first carried feeders of cf are foreign")
    n = np.stack([gentries(a) for a in d["nx"]]).reshape(N, 8, L, E)
    if np.any(np.sort(n, axis=-1) != np.arange(E)): bad.append("nx is a permutation in each level")
    return bad
def reference(fd, pw, bs, t0, dl, nx, cf, cw):
    fe = fd.astype(np.int64).reshape(N, 8, 16, V); wt = np.where(fe < 0, -1, pw.astype(np.float32).astype(np.int64).reshape(N, 8, 16, V))
    base = bs.astype(np.float32).astype(np.int32).reshape(N, 8, 16, V); T = t0.astype(np.float32).astype(np.int32).reshape(N, 8, 16, V)
    to = np.stack([gentries(a) for a in nx]).astype(np.int64); dd = dl.astype(np.int32)[:, :, None, :]
    inf = cf.astype(np.int64); inw = np.where(inf < 0, -1, cw.astype(np.int64))
    rows = np.arange(16)[None, None, :, None]
    for q in range(RO):
        old = T.copy()
        win = np.concatenate([T] + [np.roll(old, (h, h), (0, 1)) for h in range(1, H + 1)], axis=3)
        for l in range(L):
            s = slice(l * E, (l + 1) * E); f = fe[..., s]; w = wt[..., s]
            m = np.argmin(w, axis=2)[:, :, None]
            lf = np.take_along_axis(f, m, 2)[:, :, 0]; lw = np.take_along_axis(w, m, 2)[:, :, 0]
            enter = inw > lw; put = enter[:, :, None] & (rows == m)
            hf = np.where(enter, lf, inf); hw = np.where(enter, lw, inw)
            f = np.where(put, inf[:, :, None], f); w = np.where(put, inw[:, :, None], w)
            b = (base[..., s] + old[..., s]) >> 1
            a = np.take_along_axis(win, np.maximum(f, 0).reshape(N, 8, 1, 16 * E), 3).reshape(N, 8, 16, 16, E)
            c = np.add.reduce(a > b[:, :, :, None], axis=2, dtype=np.int64)
            drop = c > w
            t = np.max(np.where(drop[:, :, None], 0, a), axis=3)
            T[..., s] = np.minimum(255, np.maximum(b, t) + dd[..., s]); win[..., s] = T[..., s]
            v = np.where(drop, w, -1); m = np.argmax(v, axis=2)[:, :, None]
            gf = np.take_along_axis(f, m, 2)[:, :, 0]; gw = np.take_along_axis(v, m, 2)[:, :, 0]
            take = gw > hw; gone = take[:, :, None] & (rows == m)
            outf = np.where(take, gf, hf); outw = np.where(take, gw, hw)
            fe[..., s] = np.where(gone, -1, f); wt[..., s] = np.where(gone, -1, w)
            if l == L - 1: outf = np.where(outw < 0, -1, V + l * E + np.arange(E))
            inf = np.zeros_like(outf); inw = np.zeros_like(outw)
            np.put_along_axis(inf, to[..., s], outf, 2); np.put_along_axis(inw, to[..., s], outw, 2)
            if l == L - 1: inf = np.roll(inf, (1, 1), (0, 1)); inw = np.roll(inw, (1, 1), (0, 1))
    return {"yt": np.ascontiguousarray(T.reshape(N, 128, V)).astype(np.float32).astype(BF)}

@@ -1,0 +1,696 @@
+import numpy as np
+from concourse.bass import DstId, RemoteDMATransfer
+from concourse.mybir import AluOpType, ActivationFunctionType
+
+N = 8
+E = 256
+V = 768
+WIN = 16 + 4 * V
+SL = 272
+GROUPS = [(0, 4, "V"), (4, 8, "A"), (8, 12, "V"), (12, 17, "V")]
+NXA = 11
+WROWS = [13, 14]
+ZROWS = [k for k in range(17) if k not in WROWS]
+NXB = 2 + len(ZROWS) - NXA + 1
+PB = ["P0", "P1", "P2", "P3"]
+DB = ["D0", "D1"]
+REP = 4
+U = 131072.0
+S = 64 * U
+MG = 1.5 * 2.0 ** 40
+M1 = 1.5 * 2.0 ** 23
+
+SCRATCH = {}
+
+
+def _b(name, cols, dtype, rows=128, where="sbuf"):
+    SCRATCH[name] = (where, [rows, cols], dtype)
+
+
+for _n, _c in (("winA", WIN), ("winB", WIN), ("pwb", V), ("bsb", V), ("bb", REP * V), ("dB", V), ("cmp", 17 * E), ("Ab", 17 * E),
+               ("XA", NXA * E), ("XB", NXB * E), ("SA", NXA * E), ("SB", NXB * E), ("dA0", NXA * E), ("dB0", NXB * E),
+               ("dK", 128), ("c15", E), ("acc", 2 * E),
+               ("dS", E), ("NHb", 3 * SL), ("eqb", V), ("cst", SL), ("Jb", E), ("Cb", E), ("Zs", V), ("msk", V),
+               ("WS", 144), ("WH", 144), ("iB", 128), ("inB", 128), ("i16", 128), ("i64", 128), ("i2", 128), ("ieq", 128),
+               ("inq", 128), ("Gd", 384), ("dlb", E), ("oneB", 384)):
+    _b(_n, _c, "bfloat16")
+for _n, _c in (("lo", V), ("uu", V), ("kn", V), ("kt", V), ("sc", V), ("W0", 512), ("W1", 512), ("W2", 512), ("kp", 3 * SL),
+               ("keyF", 3 * SL), ("nk0", 3 * SL), ("nk", SL), ("o2f", SL), ("tmpA", 3 * SL), ("tmpb", E), ("Y", E), ("oneF", 128),
+               ("idF", 128), ("J0", 256), ("J1", 256), ("Wd", 144), ("Wg", 144), ("cF", 512), ("col", 16), ("io8", 32),
+               ("sm", 1024), ("ein", 16), ("eout", 16), ("tr", 256), ("Zb", E), ("Zf", V)):
+    _b(_n, _c, "float32")
+for _n, _c in (("fdi", V), ("qi", V), ("nxi", 48), ("keyI", 3 * SL), ("fI", 3 * SL), ("smi", 256), ("pci", 16)):
+    _b(_n, _c, "int32")
+for _n, _c in (("off", 3 * SL), ("off2", SL), ("nxu", 48), ("inv", 48), ("lP", 18), ("lE", 16)):
+    _b(_n, _c, "uint16")
+for _n in ("P0", "P1", "P2", "P3", "D0", "D1", "M0", "Mb"):
+    _b(_n, 512, "float32", where="psum")
+
+NDMA = 24
+SEMAPHORES = ["cV", "cA", "cP", "cG", "arrA", "arrB", "arrE"] + ["d%d" % i for i in range(NDMA)]
+ENG_SEM = {"V": "cV", "A": "cA", "P": "cP", "G": "cG"}
+OP = AluOpType
+AF = ActivationFunctionType
+CY = 0.83 * 1.2
+PCY = 0.42 * 1.2
+GC = 1.56
+LAT = 120.0
+SLACK = [40.0, 80.0, 120.0, 160.0]
+NOISE = [0.0, 50.0, 200.0, 500.0]
+PASSES = 100
+MOVES = 8000
+HEAT = 50.0
+ORDER = {}
+SEED = 1
+VARIANTS = [(1.0, 1.0, LAT), (0.8, 1.3, 80.0), (1.2, 1.0, 200.0)]
+
+
+def R(name, a, b, step=1, p0=0, p1=128):
+    return (name, a, b, step, p0, p1)
+
+
+def ncols(x):
+    return len(range(x[1], x[2], x[3]))
+
+
+def bits(x):
+    if x[3] == 1:
+        return ((1 << (x[2] - x[1])) - 1) << x[1]
+    m = 0
+    for j in range(x[1], x[2], x[3]):
+        m |= 1 << j
+    return m
+
+
+def is2(x):
+    return SCRATCH[x[0]][2] in ("bfloat16", "uint16")
+
+
+def insb(x):
+    return SCRATCH[x[0]][0] == "sbuf"
+
+
+def plan(r, core, T, topo, g):
+    tasks = []
+    queue = {"V": g.vector, "A": g.scalar, "P": g.tensor, "G": g, "S": g.sync}
+
+    def ap(x):
+        if len(x) == 2:
+            return ap(x[0]).indirect(ap(x[1]))
+        return T[x[0]][x[4]:x[5], x[1]:x[2]:x[3]]
+
+    def flat(xs):
+        out = []
+        for x in xs:
+            if isinstance(x, tuple):
+                out.extend(list(x) if len(x) == 2 else [x])
+        return out
+
+    def add(eng, fn, reads, writes, cost, lat=0.0, sem=None, ext=None):
+        tasks.append({"eng": eng, "fn": fn, "r": flat(reads), "w": flat(writes), "cost": cost, "lat": lat, "sem": sem, "ext": ext,
+                      "ind": any(isinstance(x, tuple) and len(x) == 2 for x in reads)})
+
+    def vcost(out, ins, per):
+        x = ins[0]
+        if len(x) == 2:
+            return 50 + ncols(out) * GC * CY
+        if len(out) == 2:
+            return 50 + ncols(x) * 3.8 * CY
+        return 20 + max(64, ncols(out) * per) * CY
+
+    def sc(s):
+        return ap(s) if isinstance(s, tuple) else s
+
+    def tt(out, a, b, op, ext=None):
+        per = 2 if len(a) == 2 or (insb(a) and insb(b)) else 1
+        add("V", lambda: g.vector.tensor_tensor(ap(out), ap(a), ap(b), op), [a, b], [out], vcost(out, [a], per), ext=ext)
+
+    def ts(out, a, s1, op0, s2=None, op1=None, ext=None):
+        per = 0.5 if is2(out) and is2(a) else 1
+        if op1 is None:
+            fn = lambda: g.vector.tensor_scalar(ap(out), ap(a), sc(s1), None, op0)
+        else:
+            fn = lambda: g.vector.tensor_scalar(ap(out), ap(a), sc(s1), sc(s2), op0, op1)
+        add("V", fn, [a, s1, s2], [out], vcost(out, [a], per), ext=ext)
+
+    def cp(out, a):
+        per = 0.5 if len(out) > 2 and is2(out) and is2(a) else 1
+        rd = [a] + ([out[1]] if len(out) == 2 else [])
+        add("V", lambda: g.vector.tensor_copy(ap(out), ap(a)), rd, [out[0] if len(out) == 2 else out], vcost(out, [a], per))
+
+    def ms(out, val):
+        add("V", lambda: g.vector.memset(ap(out), val), [], [out], vcost(out, [out], 0.5 if is2(out) else 1))
+
+    def scan(out, d0, d1, op0, op1):
+        per = 0.5 if is2(out) and is2(d0) and is2(d1) else 1
+        add("V", lambda: g.vector.tensor_tensor_scan(ap(out), ap(d0), ap(d1), 0.0, op0, op1), [d0, d1], [out], vcost(out, [d1], per))
+
+    def act(out, a, func=AF.Identity, bias=0.0, scale=1.0, ext=None):
+        cost = 65 + ncols(out) * GC * CY if len(a) == 2 else 40 + max(64, ncols(out)) * CY
+        add("A", lambda: g.scalar.activation(ap(out), ap(a), func, bias=sc(bias), scale=sc(scale)), [a, bias, scale], [out], cost, ext=ext)
+
+    def mm(items, parts=1):
+        step = len(items) // parts
+        for p in range(0, len(items), step):
+            def fn(p=p):
+                ins = None
+                for i in range(p, p + step):
+                    o, l, x = items[i]
+                    ins = g.tensor.matmul(ap(o), ap(l), ap(x), i == 0, i == len(items) - 1)
+                return ins
+            its = items[p:p + step]
+            cost = 40 + sum(max(64, ncols(x)) * (1 if is2(x) else 4) for o, l, x in its) * PCY
+            add("P", fn, [l for o, l, x in its] + [x for o, l, x in its], [items[0][0]], cost)
+
+    def move(out, a):
+        add("G", lambda: g.affine_select(ap(out), ap(a), [[0, ncols(a)]], OP.is_equal, 0.0, 0, 0), [a], [out], 170 + 2 * ncols(out) * CY)
+
+    nbank = [0]
+
+    def iota(out, pat, base, cm=0):
+        if SCRATCH[out[0]][2] == "int32":
+            fn = lambda: g.iota(ap(out), pat, base, cm)
+        else:
+            fn = lambda: g.iota(ap(out), pat, base, cm, allow_small_or_imprecise_dtypes=True)
+        add("G", fn, [], [out], 130 + 2 * ncols(out) * CY)
+
+    def sel(out, a, pat, base):
+        add("G", lambda: g.affine_select(ap(out), ap(a), pat, OP.is_equal, 0.0, base, 1), [a], [out], 170 + 2 * ncols(out) * CY)
+
+    nd = [0]
+
+    def dsem():
+        nd[0] += 1
+        return "d%d" % (nd[0] - 1)
+
+    def dma(eng, pairs, reads, writes, nbytes):
+        s = dsem()
+
+        def fn():
+            for o, i in pairs:
+                queue[eng].dma_start(o(), i()).then_inc(T.sem[s], 16)
+            return None
+        add(eng, fn, reads, writes, 60.0 * len(pairs), lat=2000 + nbytes / 150.0, sem=(s, 16 * len(pairs)))
+
+    def rot(eng, name, dst, rows, nbytes):
+        a, b = rows
+        d = lambda p0, p1: (lambda: ap(dst[:4] + (p0, p1)))
+        pairs = [(d(0, (N - r) * b), lambda: T[name][r * a:N * a, :])]
+        if r:
+            pairs.append((d((N - r) * b, N * b), lambda: T[name][0:r * a, :]))
+        dma(eng, pairs, [], [dst], nbytes)
+
+    def send(src, dsts, rsem):
+        s = dsem()
+        far = [(T.cores[k], x) for k, x in dsts if topo.chip(T.cores[k]) != topo.chip(core)]
+        near = [(T.cores[k], x) for k, x in dsts if topo.chip(T.cores[k]) == topo.chip(core)]
+        out = topo.engines(core, T.cores[(r + 2) % N])
+        sets = []
+        if far:
+            sets.append((far, out))
+        if near:
+            sets.append((near, [e for e in topo.engines(core, near[0][0]) if e not in out]))
+
+        def fn():
+            tr = []
+            for ds, es in sets:
+                ids = [DstId(rid=topo.addr(c)[0], pnc=topo.addr(c)[1]) for c, x in ds]
+                tr.append(RemoteDMATransfer(dst_ids=ids, dma_engine_mask=sum(1 << e for e in es), remote_sem=T.sem[rsem],
+                                            srcs=[ap(src)], dsts=[ap(x) for c, x in ds]))
+            g.remote_dma_fused(tr, local_sem=T.sem[s])
+            return None
+        add("G", fn, [src], [], 500.0, lat=2500 + ncols(src) * 256 * 3 / 60.0, sem=(s, sum(len(es) for ds, es in sets)))
+        return len(tasks) - 1
+
+    def landed(k):
+        c = T.cores[k % N]
+        out = topo.engines(c, T.cores[(k + 2) % N])
+        return len(out) if topo.chip(c) != topo.chip(core) else len(topo.engines(c, core)) - len(out)
+
+    three = sum(landed(r - h) for h in (1, 2, 3))
+    smn = [0]
+
+    def sm(n=16):
+        smn[0] += n
+        return R("sm", smn[0] - n, smn[0])
+
+    def part(x, l):
+        return R(x[0], x[1] + 16 * l, x[1] + 16 * l + 16)
+
+    def slot(name, l, k, k1=None):
+        return R(name, l * SL + 16 * k, l * SL + 16 * (k + 1 if k1 is None else k1))
+
+    def full(name):
+        return R(name, 0, SCRATCH[name][1][1])
+
+    def lev(name, l, o=0):
+        return R(name, o + l * E, o + (l + 1) * E)
+
+    rot("S", "t0", R("winA", 16, 16 + V), (16, 16), 196608)
+    for l in range(3):
+        c0, c1 = l * E, (l + 1) * E
+        dma("A", [(lambda c0=c0, c1=c1: T.fdi[:, c0:c1], lambda c0=c0, c1=c1: T.fd[:, c0:c1])], [], [lev("fdi", l)], 196608 * (l + 1))
+        dma("A", [(lambda c0=c0, c1=c1: T.pwb[:, c0:c1], lambda c0=c0, c1=c1: T.pw[:, c0:c1])], [], [lev("pwb", l)], 196608 * (l + 1) + 65536)
+    rot("S", "bs", full("bsb"), (16, 16), 196608)
+    dma("S", [(lambda: T.qi[0:8, 256:512], lambda: T.cf[:, :]), (lambda: T.qi[0:8, 512:768], lambda: T.cw[:, :])], [], [R("qi", 256, 768)], 16384)
+    rot("A", "nx", full("nxi"), (16, 16), 24576)
+    rot("S", "dl", R("qi", 0, 256), (1, 3), 24576)
+    s0 = send(R("winA", 16, 16 + V), [((r + h) % N, R("winA", 16 + h * V, 16 + (h + 1) * V)) for h in (1, 2, 3)], "arrA")
+    extA = ("arrA", three, [s0])
+
+    col = lambda j: R("col", j, j + 1)
+    pf, pg, par1, par0, kc, uc, p16x = [col(j) for j in range(7)]
+    iota(R("pci", 0, 1), [[0, 1]], 0, 1)
+    ts(R("pci", 4, 5), R("pci", 0, 1), 15, OP.bitwise_and)
+    ts(R("pci", 5, 6), R("pci", 0, 1), 4, OP.logical_shift_right)
+    ts(R("pci", 6, 7), R("pci", 0, 1), 4, OP.logical_shift_right, 1, OP.bitwise_and)
+    cp(R("col", 0, 3), R("pci", 4, 7))
+    ts(par0, par1, -1.0, OP.mult, 1.0, OP.add)
+    ts(kc, pf, 4096.0, OP.mult, 2 * U - 32768, OP.add)
+    ts(uc, pf, 4096.0, OP.mult, U - 32768 + 15, OP.add)
+    ts(p16x, pf, 16.0, OP.mult)
+    ms(full("oneF"), 1.0)
+    ms(full("oneB"), 1.0)
+    sel(full("idF"), full("oneF"), [[-1, 128]], 0)
+    for nm, val in (("i16", U), ("iB", 1.0), ("inB", -1.0), ("i64", -64.0), ("i2", 2.0), ("ieq", -32 * S), ("inq", S)):
+        act(full(nm), full("idF"), scale=val)
+    for nm, c in (("J0", par0), ("J1", par1)):
+        act(R(nm, 0, 128), full("idF"), scale=c)
+        act(R(nm, 128, 256), full("idF"), scale=c)
+    iota(R("io8", 0, 18), [[1, 18]], 0)
+    ms(full("Wd"), 0.0)
+    ts(R("Wd", 16, 144, 16), R("io8", 0, 8), pg, OP.is_equal)
+    act(full("WS"), full("Wd"), scale=-S)
+    act(full("WH"), full("Wd"), scale=-S / 2)
+    ms(R("Wg", 0, 144, 1, 0, 32), 0.0)
+    cut = N - r if r else N // 2
+    sel(R("Wg", 16, 16 + 16 * cut, 16, 0, 8), R("oneF", 0, cut, 1, 0, 8), [[-1, cut]], -r)
+    sel(R("Wg", 16 + 16 * cut, 144, 16, 0, 8), R("oneF", 0, N - cut, 1, 0, 8), [[-1, N - cut]], -((cut + r) % N))
+    sel(R("Gd", 0, 384, 1, 0, 24), R("oneB", 0, 384, 1, 0, 24), [[-1, 3], [-3, 8], [0, 16]], 0)
+    iota(full("Jb"), [[0, 16], [1, 16]], 0)
+    iota(full("Cb"), [[32, 16], [0, 16]], 32)
+    ts(full("Jb"), full("Jb"), pf, OP.is_equal)
+    tt(full("Zb"), full("Jb"), full("Cb"), OP.mult)
+    ts(R("lP", 0, 16), R("io8", 0, 16), p16x, OP.add)
+    ts(R("lP", 16, 17), p16x, 256.0 + 14, OP.add)
+    ts(full("lE"), R("oneF", 0, 16), pf, OP.mult)
+    cf2 = sm()
+    ts(cf2, R("io8", 0, 16), 16.0, OP.mult, pf, OP.add)
+    ts(cf2, cf2, 16.0 + V + 2 * E, OP.add)
+    ms(full("dS"), 0.0)
+    ms(R("dS", 0, E, 16), S)
+    ms(full("dA0"), 0.0)
+    ms(R("dA0", 0, NXA * E, NXA), -512.0)
+    ms(full("dB0"), 0.0)
+    ms(R("dB0", 0, NXB * E, NXB), -512.0)
+    ms(R("XB", NXB - 2, NXB * E, NXB), 0.0)
+    ms(R("XB", NXB - 1, NXB * E, NXB), 0.0)
+    ms(full("cst"), 1.5 * U)
+    for ka, kb, who in GROUPS:
+        if who != "V":
+            ms(R("cst", 16 * ka, 16 * kb), 9.5 * U)
+    ms(R("winA", 0, 16), 0.0)
+    ms(R("winB", 0, 16 + V), 0.0)
+    ms(full("c15"), 15.0)
+    act(full("dK"), full("idF"), scale=kc)
+
+    def Lm(name, a, p1=128):
+        return R(name, 16 - a, 144 - a, 1, 0, p1)
+
+    def bcalc(l):
+        mm([(R("Mb", 0, E), full("iB"), lev("bsb", l)), (R("Mb", 0, E), full("iB"), lev("winA", l, 16))])
+        act(full("tmpb"), R("Mb", 0, E), scale=0.5 - 2.0 ** -11, bias=M1)
+        act(brep(l, 0, 1), full("tmpb"), bias=-M1)
+        for j in range(1, REP):
+            move(brep(l, j, j + 1), brep(l, 0, 1))
+
+    def brep(l, j, j1):
+        return R("bb", (l * REP + j) * E, (l * REP + j1) * E)
+
+    def nkcalc(l, with_eq):
+        n = 16
+        o = R("Mb", 0, 16 * n)
+        it = [(o, full("idF"), slot("keyF", l, 0, n)), (o, full("i2"), slot("NHb", l, 0, n))]
+        if with_eq:
+            it.append((o, full("inq"), lev("eqb", l)))
+        mm(it)
+        act(slot("nk0", l, 0, n), o)
+
+    ktm, thr, mne, fm = sm(48), sm(48), sm(48), R("smi", 0, 48)
+    for l in range(3):
+        bank, bank2, W = "P%d" % l, ("P3", "D0", "D1")[l], "W%d" % l
+        ts(lev("lo", l), lev("fdi", l), 1.0, OP.add)
+        act(lev("uu", l), lev("lo", l), scale=32 * U, bias=uc)
+        mm([(R(bank, 0, E), full("idF"), lev("lo", l)), (R(bank, 0, E), full("i16"), lev("pwb", l)),
+            (R(bank, 0, E), full("dK"), R("oneB", 0, E)), (R(bank, 0, E), full("iB"), full("c15"))])
+        tt(lev("kn", l), R(bank, 0, E), lev("uu", l), OP.min)
+        add("V", lambda l=l: g.vector.transpose(ap(lev("kt", l)), ap(lev("kn", l))), [lev("kn", l)], [lev("kt", l)], 20 + E * CY)
+        scan(lev("sc", l), full("dS"), lev("kt", l), OP.add, OP.min)
+        tt(R(W, 0, E - 1), R("sc", l * E, l * E + E - 1), R("kt", l * E + 1, l * E + E), OP.max)
+        cp(R(W, 15, E, 16), R("sc", l * E + 15, l * E + E, 16))
+        scan(R(W, E, 2 * E), full("dS"), R(W, 0, E), OP.add, OP.min)
+        act(slot("kp", l, 0, 17), (full(W), R("lP", 0, 17)))
+        for x1 in (0, 1):
+            it = []
+            for g0 in (0, 1):
+                o = (16 * (x1 + r - g0)) % 128
+                it.append((R(bank2, x1, SL, 2), R("J%d" % x1, o, o + 128), R("kp", l * SL + g0, (l + 1) * SL, 2)))
+            mm(it)
+        cp(slot("keyI", l, 0, 16), R(bank2, 0, E))
+        act(slot("keyF", l, 0, 17), R(bank2, 0, SL))
+        act(slot("tmpA", l, 0, 16), R(bank2, 0, E), scale=-1.0, bias=MG)
+        act(slot("NHb", l, 0, 16), slot("tmpA", l, 0, 16), bias=-MG)
+        ts(slot("fI", l, 0, 16), slot("keyI", l, 0, 16), 4095, OP.bitwise_and)
+        cp(slot("off", l, 0, 15), slot("fI", l, 0, 15))
+        tt(part(ktm, l), slot("keyF", l, 15), slot("fI", l, 15), OP.subtract)
+        tt(part(ktm, l), part(ktm, l), slot("NHb", l, 15), OP.add)
+        act(part(thr, l), slot("NHb", l, 15), bias=-U / 2)
+        nkcalc(l, False)
+        bcalc(l)
+
+    cp(R("cF", 0, 512, 1, 0, 8), R("qi", 256, 768, 1, 0, 8))
+    mm([(R("M0", 0, 32), Lm("Wg", a, 8), R("cF", a, 512, 16, 0, 8)) for a in range(16)], 4)
+    e0, t1, t2 = sm(), sm(), sm()
+    act(t1, R("M0", 0, 16), scale=-32 * U, bias=16 - 33 * U)
+    act(t2, R("M0", 16, 32), scale=-U, bias=16 - 2 * U)
+    tt(t1, t1, t2, OP.max)
+    tt(e0, R("M0", 0, 16), t1, OP.add)
+    cp(R("dlb", 0, E, 1, 0, 24), R("qi", 0, E, 1, 0, 24))
+    for l in range(3):
+        mm([(R("Mb", 0, E), R("Gd", 128 * l, 128 * l + 128, 1, 0, 24), R("dlb", 0, E, 1, 0, 24))])
+        act(lev("dB", l), R("Mb", 0, E))
+    cp(full("nxu"), full("nxi"))
+    for l in range(3):
+        nxl = R("nxu", 16 * l, 16 * l + 16)
+        add("A", lambda l=l, nxl=nxl: g.scalar.activation(ap((lev("Zf", l), nxl)), ap(full("Zb")), AF.Silu), [full("Zb"), nxl], [lev("Zf", l)],
+            65 + E * 3.8 * CY + (1300 if l == 0 else 0))
+        act(lev("Zs", l), lev("Zf", l))
+        act(lev("msk", l), lev("Zf", l), func=AF.Sign)
+        mm([(R("M0", 0, 16), Lm("WS", a), R("Zs", l * E + a, (l + 1) * E, 16)) for a in range(16)])
+        ts(R("inv", 16 * l, 16 * l + 16), R("M0", 0, 16), -1.0 / (32 * S), OP.mult, -1.0, OP.add)
+
+    en, df, new, home, kf, d2, ne = [sm() for _ in range(7)]
+    Mn, nhi, tk, mk, selk, kg, vk, him, low = [sm(48) for _ in range(9)]
+    lowm, lown = R("smi", 48, 96), R("smi", 96, 112)
+    sends = []
+    extB = ("arrB", 3 * three, sends)
+    esend = []
+    extE = ("arrE", landed(r - 1), esend)
+
+    for q in range(2):
+        win = "winA" if q == 0 else "winB"
+        ext = extA if q == 0 else extB
+        nrow = 16 + q
+        for l in range(3):
+            last = q == 1 and l == 2
+            k0 = 15 + q
+            src = R("M0", 0, 16) if l > 0 else full("ein") if q else e0
+            ex = extE if q and not l else None
+            m = slot("nk0", l, 15) if q == 0 else part(mne, l)
+            tt(en, src, part(thr, l), OP.is_lt, ext=ex)
+            tt(df, src, m, OP.subtract, ext=ex)
+            tt(df, df, en, OP.mult)
+            tt(new, df, m, OP.add)
+            if not last:
+                tt(home, src, df, OP.subtract, ext=ex)
+            ts(slot("NHb", l, k0), new, MG, OP.add, -MG, OP.add)
+            tt(lown, new, slot("NHb", l, k0), OP.subtract)
+            ts(slot("fI", l, k0), lown, 4095, OP.bitwise_and)
+            cp(slot("off", l, k0), slot("fI", l, k0))
+            if not last:
+                tt(kf, part(ktm, l), slot("fI", l, k0), OP.add)
+                tt(slot("nk0", l, k0), kf, slot("NHb", l, k0), OP.add)
+                if q == 0:
+                    tt(slot("keyF", l, 15), kf, slot("NHb", l, 15), OP.subtract)
+                    tt(part(mk, l), slot("keyF", l, 15), slot("keyF", l, 16), OP.min)
+            xb = lambda j: R("XB", j, NXB * E, NXB)
+            move(R("dB0", NXB - 1, NXB * E, NXB), lev("dB", l))
+            for gi, (ka, kb, who) in enumerate(GROUPS):
+                kb = min(kb, nrow)
+                if who == "A":
+                    for j in range(ka, kb, 2):
+                        n2 = min(2, kb - j)
+                        bk = R(DB[nbank[0] % len(DB)], 0, n2 * E)
+                        nbank[0] += 1
+                        Ab = R("Ab", j * E, (j + n2) * E)
+                        act(Ab, (full(win), slot("off", l, j, j + n2)), ext=ext)
+                        mm([(bk, full("iB"), Ab), (bk, full("inB"), brep(l, 0, n2))])
+                        act(R("cmp", j * E, (j + n2) * E), bk, func=AF.Sign, bias=-0.5)
+                else:
+                    cuts = sorted(set(list(range(ka, min(kb, k0), REP)) + [min(kb, k0), kb]))
+                    for k, k1 in zip(cuts, cuts[1:]):
+                        tt(R("cmp", k * E, k1 * E), (full(win), slot("off", l, k, k1)), brep(l, 0, k1 - k), OP.is_gt, ext=ext)
+                P = R(PB[gi % len(PB)], 0, 16 * (kb - ka))
+                it = [(P, full("i64"), slot("NHb", l, ka, kb)), (P, full("i64"), R("cst", 16 * ka, 16 * kb))]
+                if q == 1:
+                    ke = min(kb, 16)
+                    it.append((R(P[0], 0, 16 * (ke - ka)), full("ieq"), R("eqb", l * E + 16 * ka, l * E + 16 * ke)))
+                it += [(P, Lm("WS" if who == "V" else "WH", a), R("cmp", ka * E + a, kb * E, 16)) for a in range(16)]
+                mm(it)
+                tt(R("o2f", 16 * ka, 16 * kb), P, slot("fI", l, ka, kb), OP.min)
+                cp(R("off2", 16 * ka, 16 * kb), R("o2f", 16 * ka, 16 * kb))
+                if not last:
+                    tt(R("nk", 16 * ka, 16 * kb), P, slot("nk0", l, ka, kb), OP.max)
+                for k in range(ka, kb):
+                    again = (full(win), R("off2", 16 * k, 16 * k + 16))
+                    if k in WROWS:
+                        j = WROWS.index(k)
+                        tt(xb(1) if k == WROWS[-1] else lev("acc", j % 2), again, lev("acc", 1 - j % 2) if j else brep(l, 0, 1), OP.max, ext=ext)
+                    else:
+                        j = ZROWS.index(k)
+                        act(R("XA", j, NXA * E, NXA) if j < NXA else xb(2 + j - NXA), again, ext=ext)
+            scan(full("SA"), full("dA0"), full("XA"), OP.add, OP.max)
+            cp(xb(0), R("SA", NXA - 1, NXA * E, NXA))
+            scan(full("SB"), full("dB0"), full("XB"), OP.add, OP.max)
+            ts(lev(win, l, 16), R("SB", NXB - 1, NXB * E, NXB), 255.0, OP.min)
+            if q == 0:
+                sends.append(send(lev("winA", l, 16), [((r + h) % N, lev("winB", l, 16 + h * V)) for h in (1, 2, 3)], "arrB"))
+                bcalc(l)
+            else:
+                y = lambda p0, p1, l=l: (lambda: T.yt[p0:p1, l * E:(l + 1) * E])
+                w = lambda p0, p1, l=l: (lambda: T.winB[p0:p1, 16 + l * E:16 + (l + 1) * E])
+                pairs = [(y(16 * r, 128), w(0, 128 - 16 * r))] + ([(y(0, 16 * r), w(128 - 16 * r, 128))] if r else [])
+                dma("S", pairs, [lev("winB", l, 16)], [], 65536)
+            if last:
+                continue
+            tt(R("tr", 0, 128), R("nk", 0, 128), R("nk", 128, 256), OP.min)
+            tt(R("tr", 128, 192), R("tr", 0, 64), R("tr", 64, 128), OP.min)
+            tt(R("tr", 192, 224), R("tr", 128, 160), R("tr", 160, 192), OP.min)
+            tt(part(Mn, l), R("tr", 192, 208), R("tr", 208, 224), OP.min)
+            if q == 1:
+                tt(part(Mn, l), part(Mn, l), R("nk", 256, SL), OP.min)
+            tt(d2, part(Mn, l), home, OP.subtract)
+            ts(part(tk, l), d2, -U / 2, OP.is_lt)
+            tt(d2, d2, part(tk, l), OP.mult)
+            tt(ne, d2, home, OP.add)
+            if l == 2:
+                ts(ne, ne, MG, OP.add, -MG, OP.add)
+                tt(ne, ne, cf2, OP.add)
+            tt(full("Y"), (ne, R("inv", 16 * l, 16 * l + 16)), lev("msk", l), OP.mult)
+            mm([(R("M0", 0, 16), Lm("Wd", a), R("Y", a, E, 16)) for a in range(16)], 4)
+            if l == 2:
+                act(full("eout"), R("M0", 0, 16))
+                esend.append(send(full("eout"), [((r + 1) % N, full("ein"))], "arrE"))
+        if q == 0:
+            ts(nhi, Mn, MG, OP.add, -MG, OP.add)
+            tt(low, Mn, nhi, OP.subtract)
+            tt(kg, low, nhi, OP.subtract)
+            act(vk, tk, scale=-S, bias=S + U)
+            tt(kg, kg, tk, OP.mult)
+            tt(vk, vk, low, OP.add)
+            tt(selk, kg, mk, OP.max)
+            tt(mk, mk, vk, OP.min)
+            ts(him, mk, MG, OP.add, -MG, OP.add)
+            tt(lowm, mk, him, OP.subtract)
+            act(thr, him, scale=-1.0, bias=-U / 2)
+            tt(mne, lowm, him, OP.subtract)
+            ts(fm, lowm, 4095, OP.bitwise_and)
+            tt(ktm, lowm, fm, OP.subtract)
+            for l in range(3):
+                tt(lev("eqb", l), (part(selk, l), full("lE")), slot("keyF", l, 0, 16), OP.is_equal)
+                if l < 2:
+                    nkcalc(l, True)
+    return tasks, queue, [extA, extB, extE]
+
+
+def depend(tasks):
+    hist = {}
+    deps = []
+    for i, t in enumerate(tasks):
+        d = set()
+        acc = [(x[0], bits(x), False) for x in t["r"]] + [(x[0], bits(x), True) for x in t["w"]]
+        for name, m, wr in acc:
+            ps = SCRATCH[name][0] == "psum"
+            for j, m2, wr2 in hist.get(name, []):
+                if j != i and ((ps and tasks[j]["eng"] != t["eng"]) or ((m & m2) and (wr or wr2))):
+                    d.add(j)
+        for name, m, wr in acc:
+            h = hist.setdefault(name, [])
+            if wr:
+                ps = SCRATCH[name][0] == "psum"
+                h[:] = [(j, m2 & ~m, w2) for j, m2, w2 in h if j == i or ((m2 & ~m) and not (ps and tasks[j]["eng"] != t["eng"]))]
+            h.append((i, m, wr))
+        deps.append(d)
+    return deps
+
+
+def schedule(tasks, deps):
+    n = len(tasks)
+    pre = [set(d) | set(t["ext"][2] if t["ext"] else []) for d, t in zip(deps, tasks)]
+    succ = [[] for _ in range(n)]
+    for i in range(n):
+        for j in pre[i]:
+            succ[j].append(i)
+    prio = [0.0] * n
+    for i in range(n - 1, -1, -1):
+        prio[i] = tasks[i]["cost"] + tasks[i]["lat"] + max([prio[k] + LAT for k in succ[i]] + [0.0])
+    best = None
+    rng = np.random.default_rng(SEED)
+    for it in range(PASSES):
+        slack = float(rng.choice(np.array(SLACK)))
+        order, start = sweep(tasks, pre, succ, prio, False, slack)
+        end = sum(replay(tasks, pre, order, v) for v in range(len(VARIANTS)))
+        if best is None or end < best[0]:
+            best = (end, order, start)
+        if it % 2:
+            start = best[2]
+        noise = rng.normal(0.0, float(rng.choice(np.array(NOISE))), n)
+        o2, s2 = sweep(tasks, succ, pre, [start[i] + tasks[i]["cost"] + noise[i] for i in range(n)], True, slack)
+        prio = [s2[i] + tasks[i]["cost"] for i in range(n)]
+    cur, order = best[0], best[1]
+    best = (cur, order)
+    pre = [list(p) for p in pre]
+    chain = None
+    for it in range(MOVES):
+        if chain is None or it % 8 == 0:
+            why = [None] * n
+            replay(tasks, pre, order, int(rng.integers(len(VARIANTS))), why)
+            chain, i = [], why[n - 1][2]
+            while why[i][0] is not None:
+                if why[i][1]:
+                    chain.append((i, why[i][0]))
+                i = why[i][0]
+        i, j = chain[int(rng.integers(len(chain)))]
+        a, b = order.index(j), order.index(i)
+        if rng.random() < 0.3:
+            e = tasks[i]["eng"]
+            back = [k for k in range(max(0, a - 12), a) if tasks[order[k]]["eng"] == e]
+            if back:
+                a = back[int(rng.integers(len(back)))]
+        mid = order[a:b]
+        need, front = set(pre[i]), []
+        for k in reversed(mid):
+            if k in need:
+                front.append(k)
+                need.update(pre[k])
+        if order[a] in need:
+            continue
+        fs = set(front)
+        cand = order[:a] + front[::-1] + [i] + [k for k in mid if k not in fs] + order[b + 1:]
+        end = sum(replay(tasks, pre, cand, v) for v in range(len(VARIANTS)))
+        if end < cur + HEAT * (1.0 - it / MOVES) * rng.exponential():
+            cur, order, chain = end, cand, None
+            if end < best[0]:
+                best = (end, cand)
+    return best[1]
+
+
+def replay(tasks, pre, order, v, why=None):
+    fg, fp, lat = VARIANTS[v]
+    free = {e: 0.0 for e in "VAPGS"}
+    prev = {e: None for e in "VAPGS"}
+    fin = [0.0] * len(tasks)
+    for i in order:
+        t = tasks[i]
+        e = t["eng"]
+        s = free[e]
+        w = None
+        for j in pre[i]:
+            if fin[j] + lat > s:
+                s = fin[j] + lat
+                w = j
+        if why is not None:
+            why[i] = [prev[e], True, None] if w is None else [w, False, None]
+            prev[e] = i
+        s += t["cost"] * (fp if e == "P" else fg if t["ind"] else 1.0)
+        free[e] = s
+        fin[i] = s + t["lat"]
+    end = max(fin)
+    if why is not None:
+        why[len(tasks) - 1][2] = fin.index(end)
+    return end
+
+
+def sweep(tasks, pre, succ, prio, back, slack):
+    n = len(tasks)
+    left = [len(p) for p in pre]
+    ready = {e: [] for e in "VAPGS"}
+    at = [tasks[i]["lat"] if back else 0.0 for i in range(n)]
+    for i in range(n):
+        if not left[i]:
+            ready[tasks[i]["eng"]].append(i)
+    free = {e: 0.0 for e in "VAPGS"}
+    order, start = [], [0.0] * n
+    while len(order) < n:
+        best = None
+        for e in "VAPGS":
+            if ready[e]:
+                t0 = max(free[e], min(at[i] for i in ready[e]))
+                if best is None or t0 < best[0]:
+                    best = (t0, e)
+        t0, e = best
+        i = max((k for k in ready[e] if at[k] <= t0 + slack), key=lambda k: (prio[k], -k))
+        t0 = max(t0, at[i])
+        ready[e].remove(i)
+        order.append(i)
+        start[i] = t0
+        free[e] = t0 + tasks[i]["cost"]
+        for k in succ[i]:
+            at[k] = max(at[k], free[e] + tasks[k if back else i]["lat"] + LAT)
+            left[k] -= 1
+            if not left[k]:
+                ready[tasks[k]["eng"]].append(k)
+    return order, start
+
+
+def rank_program(g, core, T, topo):
+    r = T.rank_of(core)
+    if r is None:
+        return
+    tasks, queue, exts = plan(r, core, T, topo, g)
+    deps = depend(tasks)
+    if "all" not in ORDER:
+        ORDER["all"] = schedule(*[(t, depend(t)) for t in [plan(1, T.cores[1], T, topo, g)[0]]][0])
+    order = ORDER["all"]
+    needed = set(j for d in deps for j in d)
+    count = {e: 0 for e in ENG_SEM}
+    mark = {}
+    for i in order:
+        t = tasks[i]
+        if t["sem"] is not None:
+            mark[i] = t["sem"]
+        elif i in needed:
+            count[t["eng"]] += 1
+            mark[i] = (ENG_SEM[t["eng"]], count[t["eng"]])
+    seen = {e: {} for e in queue}
+    for i in order:
+        t = tasks[i]
+        e = t["eng"]
+        want = {}
+        for j in deps[i]:
+            want[mark[j][0]] = max(want.get(mark[j][0], 0), mark[j][1])
+        if t["ext"]:
+            want[t["ext"][0]] = t["ext"][1]
+        for s, v in want.items():
+            if seen[e].get(s, 0) < v:
+                queue[e].wait_ge(T.sem[s], v)
+                seen[e][s] = v
+        ins = t["fn"]()
+        if t["sem"] is None and i in mark:
+            ins.then_inc(T.sem[mark[i][0]], 1)
+    ends = {}
+    for s, v in list(mark.values()) + [(x[0], x[1]) for x in exts]:
+        ends[s] = max(ends.get(s, 0), v)
+    for s, v in ends.items():
+        if max(seen[e].get(s, 0) for e in seen) < v:
+            g.wait_ge(T.sem[s], v)

@@ -7,18 +7,33 @@ E = 256
 V = 768
 WIN = 16 + 4 * V
 SL = 272
-GROUPS = [(0, 4, "V"), (4, 8, "A"), (8, 12, "V"), (12, 17, "V")]
-NXA = 11
-WROWS = [13, 14]
-ZROWS = [k for k in range(17) if k not in WROWS]
-NXB = 2 + len(ZROWS) - NXA + 1
-PB = ["P0", "P1", "P2", "P3"]
+GROUPS = [[(0, 4, "V"), (4, 8, "V"), (8, 12, "A"), (12, 16, "V")],
+          [(0, 4, "V"), (4, 8, "V"), (8, 13, "A"), (13, 17, "V")]]
+SCANS = [[([0], [1, 2, 3, 4, 5, 6, 8, 9, 10]), ([7], [11, 12, 13, 14, 15])],
+         [([0], [1, 2, 3, 4, 5, 6, 8, 9, 10]), ([7], [11, 12, 13, 14, 15, 16])]]
+ROWS = [2700.0, 3900.0, 5100.0]
+ONTO = [6500.0, 9000.0, 14000.0]
+BASE = [11000, 22500, 34000, 49500, 61000, 72500]
+_D = {"cmp": [0, 1650, 2900, 4000, 5300, 6200], "o2f": [2600, 4900, 5900, 7300], "off2": [2700, 5000, 6000, 7400],
+      "nk": [3850, 5100, 6100, 7500], "acc": [0, 5950, 7350, 7600], "entry": [2620, 2720, 3800, 3900, 3950, 4950],
+      "gather": [0, 860, 2270], "sub": [980, 2480, 3040], "sign": [1720, 3400, 3950], "count": [1760, 3900, 4600, 6400],
+      "again": [2950, 4250, 4700] + [5200 + 460 * j for j in range(12)], "W": [6700, 8800, 9300, 9800], "tree": [7700, 8750, 9250, 9350],
+      "Y": 9900, "route": 10000, "scan": [7750, 11000, 11100], "end": 11400}
+DUE = [_D, _D]
+KCV = 4
+CUT = [4, 2, 2, 2, 2, 2]
+PB = ["P0", "P1"]
 DB = ["D0", "D1"]
 REP = 4
-U = 131072.0
-S = 64 * U
-MG = 1.5 * 2.0 ** 40
+TIE = 16384
+U = 32 * TIE
+S = 128.0 * U
+BIG = 32.0 * U
+HIGH = 31 * U
+MG = 1.5 * 2.0 ** 23 * 2 * U
 M1 = 1.5 * 2.0 ** 23
+MID = 1520
+KC = {"mid": MID + 16.0, "q": -0.25, "M1": M1, "c0": 18.5 * U, "MG": MG, "nMG": -MG, "n18": -18.0 * U, "V": 17.75 * S, "A": 9.75 * S}
 
 SCRATCH = {}
 
@@ -27,25 +42,37 @@ def _b(name, cols, dtype, rows=128, where="sbuf"):
     SCRATCH[name] = (where, [rows, cols], dtype)
 
 
-for _n, _c in (("winA", WIN), ("winB", WIN), ("pwb", V), ("bsb", V), ("bb", REP * V), ("dB", V), ("cmp", 17 * E), ("Ab", 17 * E),
-               ("XA", NXA * E), ("XB", NXB * E), ("SA", NXA * E), ("SB", NXB * E), ("dA0", NXA * E), ("dB0", NXB * E),
-               ("dK", 128), ("c15", E), ("acc", 2 * E),
-               ("dS", E), ("NHb", 3 * SL), ("eqb", V), ("cst", SL), ("Jb", E), ("Cb", E), ("Zs", V), ("msk", V),
-               ("WS", 144), ("WH", 144), ("iB", 128), ("inB", 128), ("i16", 128), ("i64", 128), ("i2", 128), ("ieq", 128),
-               ("inq", 128), ("Gd", 384), ("dlb", E), ("oneB", 384)):
+for _n, _c in (("winA", WIN), ("winB", WIN), ("pwb", V), ("bsb", V), ("bb", REP * V), ("cmp", 17 * E), ("Ab", 17 * E),
+               ("dK", 128), ("acc", 2 * E), ("dB", V), ("dS", E), ("rl", V), ("eqb", V), ("Jb", 128), ("Cb", E),
+               ("WS", 144), ("WH", 144), ("iB", 128), ("inB", 128), ("iH", 128), ("iU", 128), ("inU", 128), ("i32", 128), ("Wg", 144), ("iq", 128),
+               ("Gd", 384), ("dlb", E), ("oneB", 384), ("kc", 128 * len(KC)), ("tjb", 48)):
     _b(_n, _c, "bfloat16")
-for _n, _c in (("lo", V), ("uu", V), ("kn", V), ("kt", V), ("sc", V), ("W0", 512), ("W1", 512), ("W2", 512), ("kp", 3 * SL),
-               ("keyF", 3 * SL), ("nk0", 3 * SL), ("nk", SL), ("o2f", SL), ("tmpA", 3 * SL), ("tmpb", E), ("Y", E), ("oneF", 128),
-               ("idF", 128), ("J0", 256), ("J1", 256), ("Wd", 144), ("Wg", 144), ("cF", 512), ("col", 16), ("io8", 32),
-               ("sm", 1024), ("ein", 16), ("eout", 16), ("tr", 256), ("Zb", E), ("Zf", V)):
+for _n, _c in (("lo", V), ("cF", 512)):
+    _b(_n, _c, "float16")
+for _n, _c in (("W0", V), ("W1", V), ("W2", V), ("kp", 3 * SL), ("nk0", 3 * SL), ("nk", SL), ("o2f", SL), ("Y", E),
+               ("oneF", 128), ("idF", 128), ("iS", 128), ("J0", 256), ("J1", 256), ("K0", 256), ("K1", 256),
+               ("Wd", 144), ("col", 16), ("io8", 32), ("sm", 512), ("ein", 16), ("eout", 16), ("Zb", E), ("Zs", V)):
     _b(_n, _c, "float32")
-for _n, _c in (("fdi", V), ("qi", V), ("nxi", 48), ("keyI", 3 * SL), ("fI", 3 * SL), ("smi", 256), ("pci", 16)):
+for _n, _c in (("fdi", V), ("qi", V), ("nxi", 48), ("keyI", V), ("fI", 3 * SL), ("smi", 512), ("pci", 16)):
     _b(_n, _c, "int32")
 for _n, _c in (("off", 3 * SL), ("off2", SL), ("nxu", 48), ("inv", 48), ("lP", 18), ("lE", 16)):
     _b(_n, _c, "uint16")
-for _n in ("P0", "P1", "P2", "P3", "D0", "D1", "M0", "Mb"):
+for _n in ("P0", "P1", "D0", "D1", "Q0", "Q1", "M0", "Mb"):
     _b(_n, 512, "float32", where="psum")
 
+
+def scans(q):
+    out = []
+    for s, (w, a) in enumerate(SCANS[q]):
+        end = s == len(SCANS[q]) - 1
+        n = 1 + len(a) + end
+        out.append((n, end) + tuple("%s%d%s" % (c, n, "e" if end else "s" + str(s)) for c in ("X", "d", "S")))
+        for nm in out[-1][2:]:
+            _b(nm, n * E, "bfloat16")
+    return out
+
+
+TILES = [scans(0), scans(1)]
 NDMA = 24
 SEMAPHORES = ["cV", "cA", "cP", "cG", "arrA", "arrB", "arrE"] + ["d%d" % i for i in range(NDMA)]
 ENG_SEM = {"V": "cV", "A": "cA", "P": "cP", "G": "cG"}
@@ -55,14 +82,17 @@ CY = 0.83 * 1.2
 PCY = 0.42 * 1.2
 GC = 1.56
 LAT = 120.0
+RATE = 100.0
 SLACK = [40.0, 80.0, 120.0, 160.0]
 NOISE = [0.0, 50.0, 200.0, 500.0]
 PASSES = 100
 MOVES = 8000
 HEAT = 50.0
+FIT, BLIND = 100.0, 500.0
+REFINE = [(120, 60, 12000, 30.0), (200, 100, 8000, 15.0)]
 ORDER = {}
 SEED = 1
-VARIANTS = [(1.0, 1.0, LAT), (0.8, 1.3, 80.0), (1.2, 1.0, 200.0)]
+VARIANTS = [(1.0, 1.0, LAT, 1.0), (0.8, 1.3, 80.0, 0.7), (1.2, 1.0, 200.0, 1.5)]
 
 
 def R(name, a, b, step=1, p0=0, p1=128):
@@ -83,7 +113,7 @@ def bits(x):
 
 
 def is2(x):
-    return SCRATCH[x[0]][2] in ("bfloat16", "uint16")
+    return SCRATCH[x[0]][2] in ("bfloat16", "uint16", "float16")
 
 
 def insb(x):
@@ -92,6 +122,7 @@ def insb(x):
 
 def plan(r, core, T, topo, g):
     tasks = []
+    due, step, loop = [None], [], []
     queue = {"V": g.vector, "A": g.scalar, "P": g.tensor, "G": g, "S": g.sync}
 
     def ap(x):
@@ -106,8 +137,13 @@ def plan(r, core, T, topo, g):
                 out.extend(list(x) if len(x) == 2 else [x])
         return out
 
-    def add(eng, fn, reads, writes, cost, lat=0.0, sem=None, ext=None):
-        tasks.append({"eng": eng, "fn": fn, "r": flat(reads), "w": flat(writes), "cost": cost, "lat": lat, "sem": sem, "ext": ext,
+    def add(eng, fn, reads, writes, cost, lat=0.0, sem=None, ext=None, grp=None):
+        if step:
+            due[0] = step[0]
+            step[0] += step[1]
+        elif not loop:
+            due[0] = None
+        tasks.append({"grp": grp, "eng": eng, "fn": fn, "r": flat(reads), "w": flat(writes), "cost": cost, "lat": lat, "sem": sem, "ext": ext, "due": due[0],
                       "ind": any(isinstance(x, tuple) and len(x) == 2 for x in reads)})
 
     def vcost(out, ins, per):
@@ -149,18 +185,23 @@ def plan(r, core, T, topo, g):
         cost = 65 + ncols(out) * GC * CY if len(a) == 2 else 40 + max(64, ncols(out)) * CY
         add("A", lambda: g.scalar.activation(ap(out), ap(a), func, bias=sc(bias), scale=sc(scale)), [a, bias, scale], [out], cost, ext=ext)
 
-    def mm(items, parts=1):
-        step = len(items) // parts
-        for p in range(0, len(items), step):
-            def fn(p=p):
+    def mm(items, cuts=(), ext=None):
+        cuts = [0] + list(cuts) + [len(items)]
+        grp = len(tasks)
+        for p, p1 in zip(cuts, cuts[1:]):
+            def fn(p=p, p1=p1):
                 ins = None
-                for i in range(p, p + step):
+                for i in range(p, p1):
                     o, l, x = items[i]
                     ins = g.tensor.matmul(ap(o), ap(l), ap(x), i == 0, i == len(items) - 1)
                 return ins
-            its = items[p:p + step]
+            its = items[p:p1]
             cost = 40 + sum(max(64, ncols(x)) * (1 if is2(x) else 4) for o, l, x in its) * PCY
-            add("P", fn, [l for o, l, x in its] + [x for o, l, x in its], [items[0][0]], cost)
+            add("P", fn, [l for o, l, x in its] + [x for o, l, x in its], [o for o, l, x in items], cost, ext=ext, grp=grp)
+
+    def const(o, name):
+        j = list(KC).index(name)
+        return (o, R("kc", 128 * j, 128 * j + 128, 1, 0, 1), R("oneB", 0, ncols(o), 1, 0, 1))
 
     def move(out, a):
         add("G", lambda: g.affine_select(ap(out), ap(a), [[0, ncols(a)]], OP.is_equal, 0.0, 0, 0), [a], [out], 170 + 2 * ncols(out) * CY)
@@ -190,7 +231,7 @@ def plan(r, core, T, topo, g):
             for o, i in pairs:
                 queue[eng].dma_start(o(), i()).then_inc(T.sem[s], 16)
             return None
-        add(eng, fn, reads, writes, 60.0 * len(pairs), lat=2000 + nbytes / 150.0, sem=(s, 16 * len(pairs)))
+        add(eng, fn, reads, writes, 60.0 * len(pairs), lat=1500 + nbytes / 200.0, sem=(s, 16 * len(pairs)))
 
     def rot(eng, name, dst, rows, nbytes):
         a, b = rows
@@ -219,7 +260,7 @@ def plan(r, core, T, topo, g):
                                             srcs=[ap(src)], dsts=[ap(x) for c, x in ds]))
             g.remote_dma_fused(tr, local_sem=T.sem[s])
             return None
-        add("G", fn, [src], [], 500.0, lat=2500 + ncols(src) * 256 * 3 / 60.0, sem=(s, sum(len(es) for ds, es in sets)))
+        add("G", fn, [src], [], 500.0, lat=2000 + ncols(src) * 256 * len(dsts) / RATE, sem=(s, sum(len(es) for ds, es in sets)))
         return len(tasks) - 1
 
     def landed(k):
@@ -228,11 +269,14 @@ def plan(r, core, T, topo, g):
         return len(out) if topo.chip(c) != topo.chip(core) else len(topo.engines(c, core)) - len(out)
 
     three = sum(landed(r - h) for h in (1, 2, 3))
-    smn = [0]
+    used = {"sm": 0, "smi": 0}
 
-    def sm(n=16):
-        smn[0] += n
-        return R("sm", smn[0] - n, smn[0])
+    def sm(n=16, name="sm"):
+        used[name] += n
+        return R(name, used[name] - n, used[name])
+
+    def smi(n=16):
+        return sm(n, "smi")
 
     def part(x, l):
         return R(x[0], x[1] + 16 * l, x[1] + 16 * l + 16)
@@ -246,6 +290,7 @@ def plan(r, core, T, topo, g):
     def lev(name, l, o=0):
         return R(name, o + l * E, o + (l + 1) * E)
 
+    step[:] = [0.0, 10.0]
     rot("S", "t0", R("winA", 16, 16 + V), (16, 16), 196608)
     for l in range(3):
         c0, c1 = l * E, (l + 1) * E
@@ -253,28 +298,36 @@ def plan(r, core, T, topo, g):
         dma("A", [(lambda c0=c0, c1=c1: T.pwb[:, c0:c1], lambda c0=c0, c1=c1: T.pw[:, c0:c1])], [], [lev("pwb", l)], 196608 * (l + 1) + 65536)
     rot("S", "bs", full("bsb"), (16, 16), 196608)
     dma("S", [(lambda: T.qi[0:8, 256:512], lambda: T.cf[:, :]), (lambda: T.qi[0:8, 512:768], lambda: T.cw[:, :])], [], [R("qi", 256, 768)], 16384)
-    rot("A", "nx", full("nxi"), (16, 16), 24576)
+    rot("S", "nx", full("nxi"), (16, 16), 24576)
     rot("S", "dl", R("qi", 0, 256), (1, 3), 24576)
+    step[:] = [2500.0, 0.0]
     s0 = send(R("winA", 16, 16 + V), [((r + h) % N, R("winA", 16 + h * V, 16 + (h + 1) * V)) for h in (1, 2, 3)], "arrA")
+    step[:] = []
     extA = ("arrA", three, [s0])
 
     col = lambda j: R("col", j, j + 1)
-    pf, pg, par1, par0, kc, uc, p16x = [col(j) for j in range(7)]
+    pf, pg, par1, par0, kc, p16x, par1n, par0n = [col(j) for j in range(8)]
     iota(R("pci", 0, 1), [[0, 1]], 0, 1)
     ts(R("pci", 4, 5), R("pci", 0, 1), 15, OP.bitwise_and)
     ts(R("pci", 5, 6), R("pci", 0, 1), 4, OP.logical_shift_right)
     ts(R("pci", 6, 7), R("pci", 0, 1), 4, OP.logical_shift_right, 1, OP.bitwise_and)
     cp(R("col", 0, 3), R("pci", 4, 7))
     ts(par0, par1, -1.0, OP.mult, 1.0, OP.add)
-    ts(kc, pf, 4096.0, OP.mult, 2 * U - 32768, OP.add)
-    ts(uc, pf, 4096.0, OP.mult, U - 32768 + 15, OP.add)
+    ts(kc, pf, float(TIE), OP.mult, float(TIE + U), OP.add)
     ts(p16x, pf, 16.0, OP.mult)
+    ts(R("col", 6, 8), R("col", 2, 4), -2.0, OP.mult)
     ms(full("oneF"), 1.0)
     ms(full("oneB"), 1.0)
+    for j, nm in enumerate(KC):
+        if j < KCV:
+            ms(R("kc", 128 * j, 128 * j + 128, 1, 0, 1), KC[nm])
+        else:
+            act(R("kc", 128 * j, 128 * j + 128, 1, 0, 1), R("oneF", 0, 128, 1, 0, 1), scale=KC[nm])
     sel(full("idF"), full("oneF"), [[-1, 128]], 0)
-    for nm, val in (("i16", U), ("iB", 1.0), ("inB", -1.0), ("i64", -64.0), ("i2", 2.0), ("ieq", -32 * S), ("inq", S)):
+    for nm, val in (("i32", -32.0), ("iB", 1.0), ("iU", float(U)), ("inU", -float(U)), ("iH", 0.5), ("inB", -1.0), ("iS", -S / U), ("iq", BIG)):
         act(full(nm), full("idF"), scale=val)
-    for nm, c in (("J0", par0), ("J1", par1)):
+    act(full("dK"), full("idF"), scale=kc)
+    for nm, c in (("K0", par0n), ("K1", par1n), ("J0", par0), ("J1", par1)):
         act(R(nm, 0, 128), full("idF"), scale=c)
         act(R(nm, 128, 256), full("idF"), scale=c)
     iota(R("io8", 0, 18), [[1, 18]], 0)
@@ -284,185 +337,225 @@ def plan(r, core, T, topo, g):
     act(full("WH"), full("Wd"), scale=-S / 2)
     ms(R("Wg", 0, 144, 1, 0, 32), 0.0)
     cut = N - r if r else N // 2
-    sel(R("Wg", 16, 16 + 16 * cut, 16, 0, 8), R("oneF", 0, cut, 1, 0, 8), [[-1, cut]], -r)
-    sel(R("Wg", 16 + 16 * cut, 144, 16, 0, 8), R("oneF", 0, N - cut, 1, 0, 8), [[-1, N - cut]], -((cut + r) % N))
+    sel(R("Wg", 16, 16 + 16 * cut, 16, 0, 8), R("oneB", 0, cut, 1, 0, 8), [[-1, cut]], -r)
+    sel(R("Wg", 16 + 16 * cut, 144, 16, 0, 8), R("oneB", 0, N - cut, 1, 0, 8), [[-1, N - cut]], -((cut + r) % N))
     sel(R("Gd", 0, 384, 1, 0, 24), R("oneB", 0, 384, 1, 0, 24), [[-1, 3], [-3, 8], [0, 16]], 0)
-    iota(full("Jb"), [[0, 16], [1, 16]], 0)
-    iota(full("Cb"), [[32, 16], [0, 16]], 32)
-    ts(full("Jb"), full("Jb"), pf, OP.is_equal)
-    tt(full("Zb"), full("Jb"), full("Cb"), OP.mult)
-    ts(R("lP", 0, 16), R("io8", 0, 16), p16x, OP.add)
-    ts(R("lP", 16, 17), p16x, 256.0 + 14, OP.add)
+    sel(R("Jb", 0, 128, 1, 0, 16), R("oneB", 0, 128, 1, 0, 16), [[0, 8], [-1, 16]], 0)
+    iota(R("Cb", 0, E, 1, 0, 16), [[1, 16], [0, 16]], 1)
+    sel(R("Cb", 0, E, 1, 0, 16), R("Cb", 0, E, 1, 0, 16), [[0, 16], [-1, 16]], 0)
+    mm([(R("D1", 0, E), R("Jb", 0, 128, 1, 0, 16), R("Cb", 0, E, 1, 0, 16))])
+    act(full("Zb"), R("D1", 0, E), scale=BIG)
+    ts(R("lP", 0, 15), R("io8", 0, 15), p16x, OP.add, 256.0, OP.add)
+    ts(R("lP", 15, 16), p16x, 15.0, OP.add)
+    ts(R("lP", 16, 17), p16x, 512.0 + 14, OP.add)
     ts(full("lE"), R("oneF", 0, 16), pf, OP.mult)
     cf2 = sm()
     ts(cf2, R("io8", 0, 16), 16.0, OP.mult, pf, OP.add)
     ts(cf2, cf2, 16.0 + V + 2 * E, OP.add)
     ms(full("dS"), 0.0)
-    ms(R("dS", 0, E, 16), S)
-    ms(full("dA0"), 0.0)
-    ms(R("dA0", 0, NXA * E, NXA), -512.0)
-    ms(full("dB0"), 0.0)
-    ms(R("dB0", 0, NXB * E, NXB), -512.0)
-    ms(R("XB", NXB - 2, NXB * E, NXB), 0.0)
-    ms(R("XB", NXB - 1, NXB * E, NXB), 0.0)
-    ms(full("cst"), 1.5 * U)
-    for ka, kb, who in GROUPS:
-        if who != "V":
-            ms(R("cst", 16 * ka, 16 * kb), 9.5 * U)
+    ms(R("dS", 0, E, 16), BIG)
+    for n, end, X, d, Sc in sorted(set(TILES[0] + TILES[1])):
+        if d in [t[3] for t in TILES[0]]:
+            ms(full(d), 0.0)
+            ms(R(d, 0, n * E, n), -512.0)
+        else:
+            for h in range(4):
+                iota(R(d, h * 64 * n, (h + 1) * 64 * n), [[0, 64 * n]], 0)
+            iota(R(d, 0, n * E, n), [[0, E]], -512)
+        if end:
+            iota(R(X, n - 1, n * E, n), [[0, E]], 0)
     ms(R("winA", 0, 16), 0.0)
-    ms(R("winB", 0, 16 + V), 0.0)
-    ms(full("c15"), 15.0)
-    act(full("dK"), full("idF"), scale=kc)
+    iota(R("winB", 0, 16 + V), [[0, 16 + V]], 0)
 
     def Lm(name, a, p1=128):
         return R(name, 16 - a, 144 - a, 1, 0, p1)
 
     def bcalc(l):
-        mm([(R("Mb", 0, E), full("iB"), lev("bsb", l)), (R("Mb", 0, E), full("iB"), lev("winA", l, 16))])
-        act(full("tmpb"), R("Mb", 0, E), scale=0.5 - 2.0 ** -11, bias=M1)
-        act(brep(l, 0, 1), full("tmpb"), bias=-M1)
+        o = R("Mb", 0, E)
+        mm([(o, full("iH"), lev("bsb", l)), (o, full("iH"), lev("winA", l, 16)), const(o, "q"), const(o, "M1")])
+        act(brep(l, 0, 1), o, bias=-M1)
         for j in range(1, REP):
             move(brep(l, j, j + 1), brep(l, 0, 1))
 
     def brep(l, j, j1):
         return R("bb", (l * REP + j) * E, (l * REP + j1) * E)
 
-    def nkcalc(l, with_eq):
-        n = 16
-        o = R("Mb", 0, 16 * n)
-        it = [(o, full("idF"), slot("keyF", l, 0, n)), (o, full("i2"), slot("NHb", l, 0, n))]
-        if with_eq:
-            it.append((o, full("inq"), lev("eqb", l)))
-        mm(it)
-        act(slot("nk0", l, 0, n), o)
+    Ms, tjI = sm(48), smi(48)
 
-    ktm, thr, mne, fm = sm(48), sm(48), sm(48), R("smi", 0, 48)
-    for l in range(3):
-        bank, bank2, W = "P%d" % l, ("P3", "D0", "D1")[l], "W%d" % l
-        ts(lev("lo", l), lev("fdi", l), 1.0, OP.add)
-        act(lev("uu", l), lev("lo", l), scale=32 * U, bias=uc)
-        mm([(R(bank, 0, E), full("idF"), lev("lo", l)), (R(bank, 0, E), full("i16"), lev("pwb", l)),
-            (R(bank, 0, E), full("dK"), R("oneB", 0, E)), (R(bank, 0, E), full("iB"), full("c15"))])
-        tt(lev("kn", l), R(bank, 0, E), lev("uu", l), OP.min)
-        add("V", lambda l=l: g.vector.transpose(ap(lev("kt", l)), ap(lev("kn", l))), [lev("kn", l)], [lev("kt", l)], 20 + E * CY)
-        scan(lev("sc", l), full("dS"), lev("kt", l), OP.add, OP.min)
-        tt(R(W, 0, E - 1), R("sc", l * E, l * E + E - 1), R("kt", l * E + 1, l * E + E), OP.max)
-        cp(R(W, 15, E, 16), R("sc", l * E + 15, l * E + E, 16))
-        scan(R(W, E, 2 * E), full("dS"), R(W, 0, E), OP.add, OP.min)
+    def rows(l, kb, tb):
+        W = "W%d" % l
+        x = R(kb, 0, E)
+        step[:] = [ROWS[l], 400.0]
+        ts(lev("lo", l), lev("fdi", l), -float(MID), OP.add)
+        mm([(x, full("iB"), lev("pwb", l)), (x, full("i32"), lev("lo", l))])
+        act(lev("rl", l), x, func=AF.Relu, bias=nmid)
+        mm([(x, full("iB"), lev("lo", l)), (x, full("iU"), lev("pwb", l)), (x, full("dK"), R("oneB", 0, E)), const(x, "mid"),
+            (x, full("inU"), lev("rl", l))], [4])
+        add("V", lambda: g.vector.transpose(ap(R(tb, 0, E)), ap(x)), [x], [R(tb, 0, E)], 20 + E * CY)
+        scan(R(W, 0, E), full("dS"), R(tb, 0, E), OP.add, OP.min)
+        tt(R(W, E, 2 * E - 1), R(W, 0, E - 1), R(tb, 1, E), OP.max)
+        scan(R(W, 2 * E, 3 * E), full("dS"), R(W, E, 2 * E), OP.add, OP.min)
         act(slot("kp", l, 0, 17), (full(W), R("lP", 0, 17)))
-        for x1 in (0, 1):
-            it = []
-            for g0 in (0, 1):
-                o = (16 * (x1 + r - g0)) % 128
-                it.append((R(bank2, x1, SL, 2), R("J%d" % x1, o, o + 128), R("kp", l * SL + g0, (l + 1) * SL, 2)))
-            mm(it)
-        cp(slot("keyI", l, 0, 16), R(bank2, 0, E))
-        act(slot("keyF", l, 0, 17), R(bank2, 0, SL))
-        act(slot("tmpA", l, 0, 16), R(bank2, 0, E), scale=-1.0, bias=MG)
-        act(slot("NHb", l, 0, 16), slot("tmpA", l, 0, 16), bias=-MG)
-        ts(slot("fI", l, 0, 16), slot("keyI", l, 0, 16), 4095, OP.bitwise_and)
-        cp(slot("off", l, 0, 15), slot("fI", l, 0, 15))
-        tt(part(ktm, l), slot("keyF", l, 15), slot("fI", l, 15), OP.subtract)
-        tt(part(ktm, l), part(ktm, l), slot("NHb", l, 15), OP.add)
-        act(part(thr, l), slot("NHb", l, 15), bias=-U / 2)
-        nkcalc(l, False)
-        bcalc(l)
+        step[:] = []
 
-    cp(R("cF", 0, 512, 1, 0, 8), R("qi", 256, 768, 1, 0, 8))
-    mm([(R("M0", 0, 32), Lm("Wg", a, 8), R("cF", a, 512, 16, 0, 8)) for a in range(16)], 4)
-    e0, t1, t2 = sm(), sm(), sm()
-    act(t1, R("M0", 0, 16), scale=-32 * U, bias=16 - 33 * U)
-    act(t2, R("M0", 16, 32), scale=-U, bias=16 - 2 * U)
+    def onto(l, nb):
+        it = [const(R(nb, 0, SL), "c0")]
+        for nm, n in (("K", E), ("J", SL)):
+            for x1 in (0, 1):
+                for g0 in (0, 1):
+                    o = (16 * (x1 + r - g0)) % 128
+                    it.append((R(nb, x1, n, 2), R(nm + str(x1), o, o + 128), R("kp", l * SL + g0, l * SL + n, 2)))
+            if nm == "K":
+                it += [const(R(nb, 0, SL), "MG"), const(R(nb, 0, SL), "nMG"), const(R(nb, E, SL), "n18")]
+        step[:] = [ONTO[l], 600.0]
+        mm(it, [3, 5, 10])
+        step[:] = [step[0], 300.0] if l == 0 else []
+        cp(lev("keyI", l), R(nb, 0, E))
+        ts(slot("fI", l, 0, 16), lev("keyI", l), 4095, OP.bitwise_and)
+        cp(slot("off", l, 0, 15), slot("fI", l, 0, 15))
+        step[:] = []
+        act(slot("nk0", l, 0, 16), R(nb, 0, E))
+        act(part(Ms, l), R(nb, E, SL))
+        ts(part(tjI, l), R("keyI", l * E + 240, (l + 1) * E), 31 * TIE, OP.bitwise_and)
+        ts(part(full("tjb"), l), part(tjI, l), 4096.0, OP.add)
+
+    def inverse(l):
+        nxl = R("nxu", 16 * l, 16 * l + 16)
+        add("A", lambda: g.scalar.activation(ap((lev("Zs", l), nxl)), ap(full("Zb")), AF.Silu), [full("Zb"), nxl] + ([lev("Zs", 0)] if l else []), [lev("Zs", l)],
+            65 + E * 3.8 * CY + (1300 if l == 0 else 0))
+        mm([(R("Mb", 0, 16), Lm("Wd", a), R("Zs", l * E + a, (l + 1) * E, 16)) for a in range(16)], [4, 8, 12])
+        ts(R("inv", 16 * l, 16 * l + 16), R("Mb", 0, 16), 1.0 / BIG, OP.mult, -1.0, OP.add)
+
+    for l in range(3):
+        ms(R("W%d" % l, 2 * E - 1, 2 * E), 0.0)
+    nmid = -32.0 * MID - 31
+    rows(0, "P0", "P1")
+    rows(1, "Q0", "Q1")
+    rows(2, "D1", "P0")
+    onto(0, "D0")
+    onto(1, "Q0")
+    onto(2, "Q1")
+    bcalc(0)
+    ts(R("cF", 0, 512, 1, 0, 8), R("qi", 256, 768, 1, 0, 8), -float(MID), OP.add)
+    mm([(R("M0", 32, 64), Lm("Wg", a, 8), R("cF", a, 512, 16, 0, 8)) for a in range(16)])
+    e0, t1, t2, t3 = sm(), sm(), sm(), sm()
+    act(t3, R("M0", 32, 48), func=AF.Relu, scale=-1.0, bias=-float(MID))
+    act(t1, t3, scale=18.0 * U + 16 + MID)
+    act(t2, R("M0", 48, 64), scale=-float(U), bias=(17.0 - MID) * U)
+    ts(t2, t2, 16.0 + MID, OP.add)
     tt(t1, t1, t2, OP.max)
-    tt(e0, R("M0", 0, 16), t1, OP.add)
+    tt(e0, R("M0", 32, 48), t1, OP.add)
     cp(R("dlb", 0, E, 1, 0, 24), R("qi", 0, E, 1, 0, 24))
+    cp(full("nxu"), full("nxi"))
     for l in range(3):
         mm([(R("Mb", 0, E), R("Gd", 128 * l, 128 * l + 128, 1, 0, 24), R("dlb", 0, E, 1, 0, 24))])
         act(lev("dB", l), R("Mb", 0, E))
-    cp(full("nxu"), full("nxi"))
-    for l in range(3):
-        nxl = R("nxu", 16 * l, 16 * l + 16)
-        add("A", lambda l=l, nxl=nxl: g.scalar.activation(ap((lev("Zf", l), nxl)), ap(full("Zb")), AF.Silu), [full("Zb"), nxl], [lev("Zf", l)],
-            65 + E * 3.8 * CY + (1300 if l == 0 else 0))
-        act(lev("Zs", l), lev("Zf", l))
-        act(lev("msk", l), lev("Zf", l), func=AF.Sign)
-        mm([(R("M0", 0, 16), Lm("WS", a), R("Zs", l * E + a, (l + 1) * E, 16)) for a in range(16)])
-        ts(R("inv", 16 * l, 16 * l + 16), R("M0", 0, 16), -1.0 / (32 * S), OP.mult, -1.0, OP.add)
+        inverse(l)
+        if l < 2:
+            bcalc(l + 1)
 
-    en, df, new, home, kf, d2, ne = [sm() for _ in range(7)]
-    Mn, nhi, tk, mk, selk, kg, vk, him, low = [sm(48) for _ in range(9)]
-    lowm, lown = R("smi", 48, 96), R("smi", 96, 112)
+    loop.append(1)
+    due[0] = None
+    ej = R("M0", 0, 16)
+    homeI, homeN, neI, ne2 = [smi() for _ in range(4)]
+    nI, cI, tie, lowa, kI, low, mjI = [smi(48) for _ in range(7)]
+    ntk, Mv, Ma, l2, tsel, selk = [sm(48) for _ in range(6)]
     sends = []
     extB = ("arrB", 3 * three, sends)
     esend = []
     extE = ("arrE", landed(r - 1), esend)
+    tj = lambda l: (ej, full("iB"), part(full("tjb"), l))
 
     for q in range(2):
         win = "winA" if q == 0 else "winB"
         ext = extA if q == 0 else extB
-        nrow = 16 + q
+        where = {k: R(t[2], 1 + j, t[0] * E, t[0]) for t, (w, a) in zip(TILES[q], SCANS[q]) for j, k in enumerate(a)}
+        ne, dE, SE = TILES[q][-1][0], TILES[q][-1][3], TILES[q][-1][4]
         for l in range(3):
             last = q == 1 and l == 2
             k0 = 15 + q
-            src = R("M0", 0, 16) if l > 0 else full("ein") if q else e0
-            ex = extE if q and not l else None
-            m = slot("nk0", l, 15) if q == 0 else part(mne, l)
-            tt(en, src, part(thr, l), OP.is_lt, ext=ex)
-            tt(df, src, m, OP.subtract, ext=ex)
-            tt(df, df, en, OP.mult)
-            tt(new, df, m, OP.add)
-            if not last:
-                tt(home, src, df, OP.subtract, ext=ex)
-            ts(slot("NHb", l, k0), new, MG, OP.add, -MG, OP.add)
-            tt(lown, new, slot("NHb", l, k0), OP.subtract)
-            ts(slot("fI", l, k0), lown, 4095, OP.bitwise_and)
+            base = BASE[3 * q + l]
+            D = DUE[q]
+
+            def at(name, j=0):
+                due[0] = None if name is None else base + (D[name][j] if isinstance(D[name], list) else D[name])
+            if l == 0:
+                mm([tj(0), (ej, full("idF"), full("ein") if q else e0)], ext=extE if q else None)
+            m = part(mjI, l) if q else R("keyI", l * E + 240, (l + 1) * E)
+            at("entry", 0)
+            tt(part(nI, l), ej, m, OP.min)
+            at("entry", 1)
+            tt(slot("nk0", l, k0), ej, m, OP.min)
+            at("entry", 2)
+            ts(slot("fI", l, k0), part(nI, l), 4095, OP.bitwise_and)
+            at("entry", 3)
             cp(slot("off", l, k0), slot("fI", l, k0))
             if not last:
-                tt(kf, part(ktm, l), slot("fI", l, k0), OP.add)
-                tt(slot("nk0", l, k0), kf, slot("NHb", l, k0), OP.add)
-                if q == 0:
-                    tt(slot("keyF", l, 15), kf, slot("NHb", l, 15), OP.subtract)
-                    tt(part(mk, l), slot("keyF", l, 15), slot("keyF", l, 16), OP.min)
-            xb = lambda j: R("XB", j, NXB * E, NXB)
-            move(R("dB0", NXB - 1, NXB * E, NXB), lev("dB", l))
-            for gi, (ka, kb, who) in enumerate(GROUPS):
-                kb = min(kb, nrow)
+                at("entry", 4)
+                tt(homeI, ej, m, OP.max)
+                at("entry", 5)
+                ts(homeN, homeI, HIGH + 4095, OP.bitwise_and)
+            at(None)
+            move(R(dE, ne - 1, ne * E, ne), lev("dB", l))
+            nv, na, ng = 0, 0, 0
+            for gi, (ka, kb, who) in enumerate(GROUPS[q]):
                 if who == "A":
                     for j in range(ka, kb, 2):
                         n2 = min(2, kb - j)
                         bk = R(DB[nbank[0] % len(DB)], 0, n2 * E)
                         nbank[0] += 1
                         Ab = R("Ab", j * E, (j + n2) * E)
+                        at("gather", na)
                         act(Ab, (full(win), slot("off", l, j, j + n2)), ext=ext)
+                        at("sub", na)
                         mm([(bk, full("iB"), Ab), (bk, full("inB"), brep(l, 0, n2))])
+                        at("sign", na)
                         act(R("cmp", j * E, (j + n2) * E), bk, func=AF.Sign, bias=-0.5)
+                        na += 1
                 else:
-                    cuts = sorted(set(list(range(ka, min(kb, k0), REP)) + [min(kb, k0), kb]))
+                    cuts = sorted(set(list(range(ka, min(kb, k0), CUT[gi])) + [min(kb, k0), kb]))
                     for k, k1 in zip(cuts, cuts[1:]):
+                        at("cmp", nv)
+                        nv += 1
                         tt(R("cmp", k * E, k1 * E), (full(win), slot("off", l, k, k1)), brep(l, 0, k1 - k), OP.is_gt, ext=ext)
-                P = R(PB[gi % len(PB)], 0, 16 * (kb - ka))
-                it = [(P, full("i64"), slot("NHb", l, ka, kb)), (P, full("i64"), R("cst", 16 * ka, 16 * kb))]
-                if q == 1:
-                    ke = min(kb, 16)
-                    it.append((R(P[0], 0, 16 * (ke - ka)), full("ieq"), R("eqb", l * E + 16 * ka, l * E + 16 * ke)))
-                it += [(P, Lm("WS" if who == "V" else "WH", a), R("cmp", ka * E + a, kb * E, 16)) for a in range(16)]
-                mm(it)
+                c0 = 96 * (gi // len(PB))
+                P = R(PB[gi % len(PB)], c0, c0 + 16 * (kb - ka))
+                it = [const(P, who)] + [(P, Lm("WS" if who == "V" else "WH", a), R("cmp", ka * E + a, kb * E, 16)) for a in range(16)]
+                at("count", gi)
+                mm(it[:1] + [(P, full("iS"), slot("nk0", l, ka, kb))] + it[1:])
+                at("o2f", gi)
                 tt(R("o2f", 16 * ka, 16 * kb), P, slot("fI", l, ka, kb), OP.min)
+                at("off2", gi)
                 cp(R("off2", 16 * ka, 16 * kb), R("o2f", 16 * ka, 16 * kb))
-                if not last:
-                    tt(R("nk", 16 * ka, 16 * kb), P, slot("nk0", l, ka, kb), OP.max)
+                at("nk", gi)
+                if not last and gi == 0:
+                    tt(R("nk", 0, 16 * (kb - ka)), P, slot("nk0", l, ka, kb), OP.max)
+                    wide = kb - ka
+                elif not last:
+                    tt(P, P, slot("nk0", l, ka, kb), OP.max)
+                    at("acc", gi)
+                    for j in range(0, kb - ka, wide):
+                        n = 16 * min(wide, kb - ka - j)
+                        tt(R("nk", 0, n), R(P[0], P[1] + 16 * j, P[1] + 16 * j + n), R("nk", 0, n), OP.min)
                 for k in range(ka, kb):
-                    again = (full(win), R("off2", 16 * k, 16 * k + 16))
-                    if k in WROWS:
-                        j = WROWS.index(k)
-                        tt(xb(1) if k == WROWS[-1] else lev("acc", j % 2), again, lev("acc", 1 - j % 2) if j else brep(l, 0, 1), OP.max, ext=ext)
-                    else:
-                        j = ZROWS.index(k)
-                        act(R("XA", j, NXA * E, NXA) if j < NXA else xb(2 + j - NXA), again, ext=ext)
-            scan(full("SA"), full("dA0"), full("XA"), OP.add, OP.max)
-            cp(xb(0), R("SA", NXA - 1, NXA * E, NXA))
-            scan(full("SB"), full("dB0"), full("XB"), OP.add, OP.max)
-            ts(lev(win, l, 16), R("SB", NXB - 1, NXB * E, NXB), 255.0, OP.min)
+                    if k in where:
+                        at("again", ng)
+                        ng += 1
+                        act(where[k], (full(win), R("off2", 16 * k, 16 * k + 16)), ext=ext)
+            run, nw = brep(l, 0, 1), 0
+            for s, ((n, end, X, d, Sc), (ws, a)) in enumerate(zip(TILES[q], SCANS[q])):
+                for j, k in enumerate(ws):
+                    o = R(X, 0, n * E, n) if k == ws[-1] else lev("acc", j % 2)
+                    at("W", nw)
+                    nw += 1
+                    tt(o, (full(win), R("off2", 16 * k, 16 * k + 16)), run, OP.max, ext=ext)
+                    run = o
+                at("scan", s)
+                scan(full(Sc), full(d), full(X), OP.add, OP.max)
+                run = R(Sc, n - 1, n * E, n)
+            at("end")
+            ts(lev(win, l, 16), run, 255.0, OP.min)
+            at(None)
             if q == 0:
                 sends.append(send(lev("winA", l, 16), [((r + h) % N, lev("winB", l, 16 + h * V)) for h in (1, 2, 3)], "arrB"))
                 bcalc(l)
@@ -473,43 +566,54 @@ def plan(r, core, T, topo, g):
                 dma("S", pairs, [lev("winB", l, 16)], [], 65536)
             if last:
                 continue
-            tt(R("tr", 0, 128), R("nk", 0, 128), R("nk", 128, 256), OP.min)
-            tt(R("tr", 128, 192), R("tr", 0, 64), R("tr", 64, 128), OP.min)
-            tt(R("tr", 192, 224), R("tr", 128, 160), R("tr", 160, 192), OP.min)
-            tt(part(Mn, l), R("tr", 192, 208), R("tr", 208, 224), OP.min)
-            if q == 1:
-                tt(part(Mn, l), part(Mn, l), R("nk", 256, SL), OP.min)
-            tt(d2, part(Mn, l), home, OP.subtract)
-            ts(part(tk, l), d2, -U / 2, OP.is_lt)
-            tt(d2, d2, part(tk, l), OP.mult)
-            tt(ne, d2, home, OP.add)
-            if l == 2:
-                ts(ne, ne, MG, OP.add, -MG, OP.add)
-                tt(ne, ne, cf2, OP.add)
-            tt(full("Y"), (ne, R("inv", 16 * l, 16 * l + 16)), lev("msk", l), OP.mult)
-            mm([(R("M0", 0, 16), Lm("Wd", a), R("Y", a, E, 16)) for a in range(16)], 4)
-            if l == 2:
-                act(full("eout"), R("M0", 0, 16))
+            nt = 0
+            while wide > 1:
+                h = wide // 2
+                wide -= h
+                at("tree", nt)
+                nt += 1
+                tt(R("nk", 0, 16 * h), R("nk", 0, 16 * h), R("nk", 16 * wide, 16 * (wide + h)), OP.min)
+            at("tree", 2)
+            tt(part(cI, l), R("nk", 0, 16), homeN, OP.min)
+            at("tree", 3)
+            if l < 2:
+                ts(neI, part(cI, l), HIGH + 4095, OP.bitwise_and)
+            else:
+                ts(ne2, part(cI, l), HIGH, OP.bitwise_and)
+                tt(neI, ne2, cf2, OP.add)
+            at("Y")
+            tt(full("Y"), (neI, R("inv", 16 * l, 16 * l + 16)), lev("Zs", l), OP.min)
+            it = [(ej, Lm("Wd", a), R("Y", a, E, 16)) for a in range(16)]
+            at("route")
+            if l < 2:
+                mm([tj(l + 1)] + it, [5, 9, 13])
+                at(None)
+            else:
+                mm(it, [4, 8, 12])
+                at(None)
+                act(full("eout"), ej)
                 esend.append(send(full("eout"), [((r + 1) % N, full("ein"))], "arrE"))
         if q == 0:
-            ts(nhi, Mn, MG, OP.add, -MG, OP.add)
-            tt(low, Mn, nhi, OP.subtract)
-            tt(kg, low, nhi, OP.subtract)
-            act(vk, tk, scale=-S, bias=S + U)
-            tt(kg, kg, tk, OP.mult)
-            tt(vk, vk, low, OP.add)
-            tt(selk, kg, mk, OP.max)
-            tt(mk, mk, vk, OP.min)
-            ts(him, mk, MG, OP.add, -MG, OP.add)
-            tt(lowm, mk, him, OP.subtract)
-            act(thr, him, scale=-1.0, bias=-U / 2)
-            tt(mne, lowm, him, OP.subtract)
-            ts(fm, lowm, 4095, OP.bitwise_and)
-            tt(ktm, lowm, fm, OP.subtract)
+            ts(tie, cI, 31 * TIE, OP.bitwise_and)
+            ts(ntk, tie, 0.0, OP.is_equal, BIG, OP.mult)
+            tt(Mv, tie, ntk, OP.add)
+            ts(lowa, nI, U - 1, OP.bitwise_and)
+            ts(l2, lowa, 2.0, OP.mult, 18.0 * U, OP.add)
+            tt(Ma, l2, nI, OP.subtract)
+            tt(Ma, Ma, Ms, OP.min)
+            tt(kI, Ma, Mv, OP.min)
+            ts(low, kI, U - 1, OP.bitwise_and)
+            ts(l2, low, 2.0, OP.mult, 18.0 * U, OP.add)
+            tt(mjI, l2, kI, OP.subtract)
+            ts(tjI, kI, 31 * TIE, OP.bitwise_and)
+            ts(full("tjb"), tjI, 8192.0, OP.add)
+            tt(tsel, cI, ntk, OP.add)
+            tt(selk, mjI, tsel, OP.min)
             for l in range(3):
-                tt(lev("eqb", l), (part(selk, l), full("lE")), slot("keyF", l, 0, 16), OP.is_equal)
-                if l < 2:
-                    nkcalc(l, True)
+                tt(lev("eqb", l), (part(selk, l), full("lE")), slot("nk0", l, 0, 16), OP.is_equal)
+                o = R("Q%d" % (l % 2), 0, E)
+                mm([(o, full("idF"), slot("nk0", l, 0, 16)), (o, full("iq"), lev("eqb", l))])
+                act(slot("nk0", l, 0, 16), o)
     return tasks, queue, [extA, extB, extE]
 
 
@@ -596,7 +700,7 @@ def schedule(tasks, deps):
 
 
 def replay(tasks, pre, order, v, why=None):
-    fg, fp, lat = VARIANTS[v]
+    fg, fp, lat, fl = VARIANTS[v]
     free = {e: 0.0 for e in "VAPGS"}
     prev = {e: None for e in "VAPGS"}
     fin = [0.0] * len(tasks)
@@ -614,7 +718,7 @@ def replay(tasks, pre, order, v, why=None):
             prev[e] = i
         s += t["cost"] * (fp if e == "P" else fg if t["ind"] else 1.0)
         free[e] = s
-        fin[i] = s + t["lat"]
+        fin[i] = s + t["lat"] * fl
     end = max(fin)
     if why is not None:
         why[len(tasks) - 1][2] = fin.index(end)
@@ -653,6 +757,124 @@ def sweep(tasks, pre, succ, prio, back, slack):
     return order, start
 
 
+def schedule(tasks, deps):
+    pre = [set(d) | set(t["ext"][2] if t["ext"] else []) for d, t in zip(deps, tasks)]
+    order = bydue(tasks, pre)
+    for span, stride, moves, heat in REFINE:
+        order = refine(tasks, pre, order, span, stride, moves, heat)
+    return order
+
+
+def bydue(tasks, pre):
+    n = len(tasks)
+    succ = [[] for _ in range(n)]
+    for i in range(n):
+        for j in pre[i]:
+            succ[j].append(i)
+    due = [0.0] * n
+    for i in range(n - 1, -1, -1):
+        t = tasks[i]
+        d = min([due[k] - t["cost"] - t["lat"] - LAT for k in succ[i]] + [1e9])
+        due[i] = d if t["due"] is None else min([t["due"]] + [due[k] - 1.0 for k in succ[i]])
+    todo = {e: sorted((i for i in range(n) if tasks[i]["eng"] == e), key=lambda i: (due[i], i)) for e in "VAPGS"}
+    left = [len(p) for p in pre]
+    at = [0.0] * n
+    free = {e: 0.0 for e in "VAPGS"}
+    order = []
+    while len(order) < n:
+        best = None
+        for e in "VAPGS":
+            if not todo[e]:
+                continue
+            m = todo[e][0]
+            pick = m if not left[m] else None
+            if left[m] or at[m] > free[e] + FIT:
+                room = at[m] + FIT if not left[m] else max(at[m], free[e]) + BLIND
+                fill = [k for k in todo[e] if not left[k] and tasks[k]["due"] is None and max(at[k], free[e]) + tasks[k]["cost"] <= room]
+                if fill:
+                    pick = fill[0]
+            if pick is not None:
+                s = max(free[e], at[pick])
+                if best is None or s < best[0]:
+                    best = (s, e, pick)
+        s, e, i = best
+        todo[e].remove(i)
+        order.append(i)
+        free[e] = s + tasks[i]["cost"]
+        for k in succ[i]:
+            at[k] = max(at[k], free[e] + tasks[i]["lat"] + LAT)
+            left[k] -= 1
+    return order
+
+
+def refine(tasks, pre, order, span, stride, moves, heat):
+    n = len(tasks)
+    rng = np.random.default_rng(SEED)
+    eng = ["VAPGS".index(t["eng"]) for t in tasks]
+    hard = [[j for j in d if t["grp"] is None or tasks[j]["grp"] != t["grp"]] for d, t in zip(pre, tasks)]
+    cost = [[t["cost"] * (fp if t["eng"] == "P" else fg if t["ind"] else 1.0) for t in tasks] for fg, fp, lat, fl in VARIANTS]
+    late = [[t["lat"] * fl + lat for t in tasks] for fg, fp, lat, fl in VARIANTS]
+    fin = [[0.0] * n for v in VARIANTS]
+    free0 = [[0.0] * 5 for v in VARIANTS]
+    order = list(order)
+
+    def run(seq, keep=False):
+        tot = 0.0
+        for f, c, la, fr in zip(fin, cost, late, free0):
+            free = fr if keep else fr[:]
+            end = 0.0
+            for i in seq:
+                e = eng[i]
+                s = free[e]
+                for j in hard[i]:
+                    if f[j] > s:
+                        s = f[j]
+                s += c[i]
+                free[e] = s
+                s += la[i]
+                f[i] = s
+                if s > end:
+                    end = s
+            tot += end + 0.1 * (free[0] + free[1] + free[2])
+        return tot
+    for a0 in range(0, max(n - span, 0) + stride, stride):
+        seq = order[a0:a0 + span]
+        m = len(seq)
+        cur = run(seq)
+        best = (cur, seq)
+        pos, far, way, warm = rng.integers(m, size=moves).tolist(), rng.exponential(1.4, moves).tolist(), rng.random(moves).tolist(), rng.exponential(1.0, moves).tolist()
+        for it in range(moves):
+            a = b = pos[it]
+            i = seq[b]
+            hops, d = 1 + int(far[it]), -1 if way[it] < 0.5 else 1
+            while hops and 0 <= a + d < m:
+                a += d
+                hops -= eng[seq[a]] == eng[i]
+            if hops:
+                continue
+            tied, along, rest = set(pre[i]) if d < 0 else {i}, [], []
+            for k in seq[b + d:a:d]:
+                if (k in tied) if d < 0 else (pre[k] & tied):
+                    along.append(k)
+                    tied.update(pre[k] if d < 0 else [k])
+                else:
+                    rest.append(k)
+            if (seq[a] in tied) if d < 0 else (pre[seq[a]] & tied):
+                continue
+            if d < 0:
+                cand = seq[:a] + along[::-1] + [i, seq[a]] + rest[::-1] + seq[b + 1:]
+            else:
+                cand = seq[:b] + rest + [seq[a], i] + along + seq[a + 1:]
+            c = run(cand)
+            if c < cur + heat * (1.0 - it / moves) * warm[it]:
+                cur, seq = c, cand
+                if c < best[0]:
+                    best = (c, cand)
+        order[a0:a0 + span] = best[1]
+        run(best[1][:stride], True)
+    return order
+
+
 def rank_program(g, core, T, topo):
     r = T.rank_of(core)
     if r is None:
@@ -662,7 +884,8 @@ def rank_program(g, core, T, topo):
     if "all" not in ORDER:
         ORDER["all"] = schedule(*[(t, depend(t)) for t in [plan(1, T.cores[1], T, topo, g)[0]]][0])
     order = ORDER["all"]
-    needed = set(j for d in deps for j in d)
+    hard = [[j for j in d if t["grp"] is None or tasks[j]["grp"] != t["grp"]] for d, t in zip(deps, tasks)]
+    needed = set(j for d in hard for j in d)
     count = {e: 0 for e in ENG_SEM}
     mark = {}
     for i in order:
@@ -677,7 +900,7 @@ def rank_program(g, core, T, topo):
         t = tasks[i]
         e = t["eng"]
         want = {}
-        for j in deps[i]:
+        for j in hard[i]:
             want[mark[j][0]] = max(want.get(mark[j][0], 0), mark[j][1])
         if t["ext"]:
             want[t["ext"][0]] = t["ext"][1]

@@ -7,21 +7,29 @@ E = 256
 V = 768
 WIN = 16 + 4 * V
 SL = 272
+KIND = [0, 0, 0, 0, 0, 1]
 GROUPS = [[(0, 4, "V"), (4, 8, "V"), (8, 12, "A"), (12, 16, "V")],
-          [(0, 4, "V"), (4, 8, "V"), (8, 13, "A"), (13, 17, "V")]]
-SCANS = [[([0], [1, 2, 3, 4, 5, 6, 8, 9, 10]), ([7], [11, 12, 13, 14, 15])],
-         [([0], [1, 2, 3, 4, 5, 6, 8, 9, 10]), ([7], [11, 12, 13, 14, 15, 16])]]
+          [(0, 4, "V"), (4, 8, "V"), (8, 12, "A"), (12, 16, "V")]]
+SCANS = [[([7], [0, 1, 2, 3, 4]), ([6], [5, 8, 9, 10, 11]), ([15], [12, 13, 14])],
+         [([7], [0, 1, 2, 3, 4]), ([6], [5, 8, 9, 10, 11]), ([15], [12, 13, 14])]]
 ROWS = [2700.0, 3900.0, 5100.0]
-ONTO = [6500.0, 9000.0, 14000.0]
+ONTO = [6500.0, 9500.0, 14000.0]
+INV = [7600.0, 9000.0, 22000.0]
 BASE = [11000, 22500, 34000, 49500, 61000, 72500]
 _D = {"cmp": [0, 1650, 2900, 4000, 5300, 6200], "o2f": [2600, 4900, 5900, 7300], "off2": [2700, 5000, 6000, 7400],
       "nk": [3850, 5100, 6100, 7500], "acc": [0, 5950, 7350, 7600], "entry": [2620, 2720, 3800, 3900, 3950, 4950],
       "gather": [0, 860, 2270], "sub": [980, 2480, 3040], "sign": [1720, 3400, 3950], "count": [1760, 3900, 4600, 6400],
-      "again": [2950, 4250, 4700] + [5200 + 460 * j for j in range(12)], "W": [6700, 8800, 9300, 9800], "tree": [7700, 8750, 9250, 9350],
-      "Y": 9900, "route": 10000, "scan": [7750, 11000, 11100], "end": 11400}
-DUE = [_D, _D]
+      "again": [2950, 4250, 4700] + [5200 + 460 * j for j in range(12)], "W": [5500, 8000, 10300, 10400, 10500],
+      "tree": [7700, 8750, 9250, 9350], "Y": 9900, "route": [10000, 10700, 11000], "scan": [7000, 9300, 11000], "end": 11400}
+_E = {"cmp": [0, 1640, 2740, 3670, 5200], "gather": [0, 1040], "count": [1760, 3700, 4700, 6050], "route": [11400, 12080, 13520],
+      "sub": [980, 2720], "sign": [1910, 4030], "o2f": [2490, 4910, 5730, 7170], "nk": [2570, 5110, 6260, 7370],
+      "entry": [2650, 2990, 3580, 3790, 4990, 7450], "off2": [2690, 5110, 5930, 7370],
+      "again": [3110, 3570, 4580, 5050, 5530, 5990, 6460, 6920, 7380, 7850, 8310, 8770, 9230], "W": [5810, 7860, 9330],
+      "acc": [0, 5650, 7250, 7570], "scan": [6380, 8430, 9900], "tree": [7780, 8310, 9210, 9780], "Y": 10560, "end": 11010}
+DUE = [_E, _E]
 KCV = 4
-CUT = [4, 2, 2, 2, 2, 2]
+QUICK = 0
+CUT = [4, 2, 2, 3, 2, 2]
 PB = ["P0", "P1"]
 DB = ["D0", "D1"]
 REP = 4
@@ -43,13 +51,14 @@ def _b(name, cols, dtype, rows=128, where="sbuf"):
 
 
 for _n, _c in (("winA", WIN), ("winB", WIN), ("pwb", V), ("bsb", V), ("bb", REP * V), ("cmp", 17 * E), ("Ab", 17 * E),
-               ("dK", 128), ("acc", 2 * E), ("dB", V), ("dS", E), ("rl", V), ("eqb", V), ("Jb", 128), ("Cb", E),
-               ("WS", 144), ("WH", 144), ("iB", 128), ("inB", 128), ("iH", 128), ("iU", 128), ("inU", 128), ("i32", 128), ("Wg", 144), ("iq", 128),
+               ("dK", 128), ("acc", 2 * E), ("dB", V), ("dS", E), ("rl", V), ("Zh", V), ("eqb", V), ("Jb", 128), ("Cb", E),
+               ("WS", 144), ("WH", 144), ("iB", 128), ("inB", 128), ("iH", 128), ("iU", 128), ("inU", 128), ("i32", 128), ("Wg", 144),
+               ("Jg", 128), ("bo", 128), ("Bm", 2048), ("mk", E), ("qa", 2 * E),
                ("Gd", 384), ("dlb", E), ("oneB", 384), ("kc", 128 * len(KC)), ("tjb", 48)):
     _b(_n, _c, "bfloat16")
 for _n, _c in (("lo", V), ("cF", 512)):
     _b(_n, _c, "float16")
-for _n, _c in (("W0", V), ("W1", V), ("W2", V), ("kp", 3 * SL), ("nk0", 3 * SL), ("nk", SL), ("o2f", SL), ("Y", E),
+for _n, _c in (("W0", V), ("W1", V), ("W2", V), ("kp", 3 * SL), ("nk0", 3 * SL), ("nk", SL), ("o2f", SL), ("Y", E), ("Yt", 128),
                ("oneF", 128), ("idF", 128), ("iS", 128), ("J0", 256), ("J1", 256), ("K0", 256), ("K1", 256),
                ("Wd", 144), ("col", 16), ("io8", 32), ("sm", 512), ("ein", 16), ("eout", 16), ("Zb", E), ("Zs", V)):
     _b(_n, _c, "float32")
@@ -65,8 +74,8 @@ def scans(q):
     out = []
     for s, (w, a) in enumerate(SCANS[q]):
         end = s == len(SCANS[q]) - 1
-        n = 1 + len(a) + end
-        out.append((n, end) + tuple("%s%d%s" % (c, n, "e" if end else "s" + str(s)) for c in ("X", "d", "S")))
+        n = (w is not None) + len(a) + end
+        out.append((n, end) + tuple("%s%d%s" % (c, n, "e" if end else "s" + str(s) * (c != "d")) for c in ("X", "d", "S")))
         for nm in out[-1][2:]:
             _b(nm, n * E, "bfloat16")
     return out
@@ -88,8 +97,8 @@ NOISE = [0.0, 50.0, 200.0, 500.0]
 PASSES = 100
 MOVES = 8000
 HEAT = 50.0
-FIT, BLIND = 100.0, 500.0
-REFINE = [(120, 60, 12000, 30.0), (200, 100, 8000, 15.0)]
+FIT, BLIND, EPS, EPS2 = 100.0, 500.0, 0.0003, 0.001
+REFINE = [(120, 60, 10000, 120.0), (130, 50, 8000, 60.0), (120, 60, 8000, 20.0)]
 ORDER = {}
 SEED = 1
 VARIANTS = [(1.0, 1.0, LAT, 1.0), (0.8, 1.3, 80.0, 0.7), (1.2, 1.0, 200.0, 1.5)]
@@ -143,7 +152,7 @@ def plan(r, core, T, topo, g):
             step[0] += step[1]
         elif not loop:
             due[0] = None
-        tasks.append({"grp": grp, "eng": eng, "fn": fn, "r": flat(reads), "w": flat(writes), "cost": cost, "lat": lat, "sem": sem, "ext": ext, "due": due[0],
+        tasks.append({"tag": loop[0] if loop else None, "grp": grp, "eng": eng, "fn": fn, "r": flat(reads), "w": flat(writes), "cost": cost, "lat": lat, "sem": sem, "ext": ext, "due": due[0],
                       "ind": any(isinstance(x, tuple) and len(x) == 2 for x in reads)})
 
     def vcost(out, ins, per):
@@ -185,7 +194,7 @@ def plan(r, core, T, topo, g):
         cost = 65 + ncols(out) * GC * CY if len(a) == 2 else 40 + max(64, ncols(out)) * CY
         add("A", lambda: g.scalar.activation(ap(out), ap(a), func, bias=sc(bias), scale=sc(scale)), [a, bias, scale], [out], cost, ext=ext)
 
-    def mm(items, cuts=(), ext=None):
+    def mm(items, cuts=(), ext=None, more=False, each=False):
         cuts = [0] + list(cuts) + [len(items)]
         grp = len(tasks)
         for p, p1 in zip(cuts, cuts[1:]):
@@ -193,10 +202,10 @@ def plan(r, core, T, topo, g):
                 ins = None
                 for i in range(p, p1):
                     o, l, x = items[i]
-                    ins = g.tensor.matmul(ap(o), ap(l), ap(x), i == 0, i == len(items) - 1)
+                    ins = g.tensor.matmul(ap(o), ap(l), ap(x), each or (i == 0 and not more), each or i == len(items) - 1)
                 return ins
             its = items[p:p1]
-            cost = 40 + sum(max(64, ncols(x)) * (1 if is2(x) else 4) for o, l, x in its) * PCY
+            cost = 40 + sum(max(min(64, ncols(l)), ncols(x)) * (1 if is2(x) else 4) for o, l, x in its) * PCY
             add("P", fn, [l for o, l, x in its] + [x for o, l, x in its], [o for o, l, x in items], cost, ext=ext, grp=grp)
 
     def const(o, name):
@@ -224,14 +233,14 @@ def plan(r, core, T, topo, g):
         nd[0] += 1
         return "d%d" % (nd[0] - 1)
 
-    def dma(eng, pairs, reads, writes, nbytes):
+    def dma(eng, pairs, reads, writes, nbytes, ext=None):
         s = dsem()
 
         def fn():
             for o, i in pairs:
                 queue[eng].dma_start(o(), i()).then_inc(T.sem[s], 16)
             return None
-        add(eng, fn, reads, writes, 60.0 * len(pairs), lat=1500 + nbytes / 200.0, sem=(s, 16 * len(pairs)))
+        add(eng, fn, reads, writes, 60.0 * len(pairs), lat=1500 + nbytes / 200.0, sem=(s, 16 * len(pairs)), ext=ext)
 
     def rot(eng, name, dst, rows, nbytes):
         a, b = rows
@@ -324,7 +333,7 @@ def plan(r, core, T, topo, g):
         else:
             act(R("kc", 128 * j, 128 * j + 128, 1, 0, 1), R("oneF", 0, 128, 1, 0, 1), scale=KC[nm])
     sel(full("idF"), full("oneF"), [[-1, 128]], 0)
-    for nm, val in (("i32", -32.0), ("iB", 1.0), ("iU", float(U)), ("inU", -float(U)), ("iH", 0.5), ("inB", -1.0), ("iS", -S / U), ("iq", BIG)):
+    for nm, val in (("i32", -32.0), ("iB", 1.0), ("iU", float(U)), ("inU", -float(U)), ("iH", 0.5), ("inB", -1.0), ("iS", -S / U)):
         act(full(nm), full("idF"), scale=val)
     act(full("dK"), full("idF"), scale=kc)
     for nm, c in (("K0", par0n), ("K1", par1n), ("J0", par0), ("J1", par1)):
@@ -354,18 +363,26 @@ def plan(r, core, T, topo, g):
     ts(cf2, cf2, 16.0 + V + 2 * E, OP.add)
     ms(full("dS"), 0.0)
     ms(R("dS", 0, E, 16), BIG)
-    for n, end, X, d, Sc in sorted(set(TILES[0] + TILES[1])):
-        if d in [t[3] for t in TILES[0]]:
-            ms(full(d), 0.0)
-            ms(R(d, 0, n * E, n), -512.0)
-        else:
-            for h in range(4):
-                iota(R(d, h * 64 * n, (h + 1) * 64 * n), [[0, 64 * n]], 0)
-            iota(R(d, 0, n * E, n), [[0, E]], -512)
+    for n, end, X, d, Sc in {t[3]: t for t in TILES[0] + TILES[1]}.values():
+        for h in range(2):
+            ms(R(d, h * 128 * n, (h + 1) * 128 * n), 0.0)
+        ms(R(d, 0, n * E, n), -512.0)
         if end:
-            iota(R(X, n - 1, n * E, n), [[0, E]], 0)
+            ms(R(X, n - 1, n * E, n), 0.0)
+    if any(x[2] == "Q" for gr in GROUPS for x in gr):
+        sel(R("Jg", 0, 128, 1, 0, 8), R("oneB", 0, 128, 1, 0, 8), [[-1, 8], [0, 16]], 0)
+        mm([(R("D0", 0, 128), R("Jg", 0, 128, 1, 0, 8), R("Jg", 0, 128, 1, 0, 8))])
+        act(full("bo"), R("D0", 0, 128))
+        am = sm()
+        ts(am, R("io8", 0, 16), pf, OP.is_equal, -512.0, OP.mult)
+        for a in range(16):
+            if a % 2:
+                ts(R("Bm", 128 * a, 128 * a + 128), full("bo"), R("sm", am[1] + a, am[1] + a + 1), OP.mult)
+            else:
+                act(R("Bm", 128 * a, 128 * a + 128), full("bo"), scale=R("sm", am[1] + a, am[1] + a + 1))
     ms(R("winA", 0, 16), 0.0)
-    iota(R("winB", 0, 16 + V), [[0, 16 + V]], 0)
+    ms(R("winB", 0, 16), 0.0)
+    dma("S", [(lambda: T.winB[:, 16:16 + V], lambda: T.bsb[:, :])], [full("bsb")], [R("winB", 16, 16 + V)], 196608, extA)
 
     def Lm(name, a, p1=128):
         return R(name, 16 - a, 144 - a, 1, 0, p1)
@@ -380,7 +397,7 @@ def plan(r, core, T, topo, g):
     def brep(l, j, j1):
         return R("bb", (l * REP + j) * E, (l * REP + j1) * E)
 
-    Ms, tjI = sm(48), smi(48)
+    Ms, tjI, mjI = sm(48), smi(48), smi(48)
 
     def rows(l, kb, tb):
         W = "W%d" % l
@@ -399,32 +416,38 @@ def plan(r, core, T, topo, g):
         step[:] = []
 
     def onto(l, nb):
-        it = [const(R(nb, 0, SL), "c0")]
-        for nm, n in (("K", E), ("J", SL)):
-            for x1 in (0, 1):
-                for g0 in (0, 1):
-                    o = (16 * (x1 + r - g0)) % 128
-                    it.append((R(nb, x1, n, 2), R(nm + str(x1), o, o + 128), R("kp", l * SL + g0, l * SL + n, 2)))
-            if nm == "K":
-                it += [const(R(nb, 0, SL), "MG"), const(R(nb, 0, SL), "nMG"), const(R(nb, E, SL), "n18")]
+        def fix(nm, bank, n):
+            return [(R(bank, x1, n, 2), R(nm + str(x1), (16 * (x1 + r - g0)) % 128, (16 * (x1 + r - g0)) % 128 + 128),
+                     R("kp", l * SL + g0, l * SL + n, 2)) for x1 in (0, 1) for g0 in (0, 1)]
+        kl = R("keyI", l * E, l * E + 240)
         step[:] = [ONTO[l], 600.0]
-        mm(it, [3, 5, 10])
-        step[:] = [step[0], 300.0] if l == 0 else []
-        cp(lev("keyI", l), R(nb, 0, E))
-        ts(slot("fI", l, 0, 16), lev("keyI", l), 4095, OP.bitwise_and)
-        cp(slot("off", l, 0, 15), slot("fI", l, 0, 15))
+        mm([const(R(nb, 0, SL), "c0")] + fix("K", nb, E) + [const(R(nb, 0, SL), "MG"), const(R(nb, 0, SL), "nMG"), const(R(nb, E, SL), "n18")]
+           + fix("J", nb, SL), [3, 5, 10])
+        if l == 0:
+            step[1] = 300.0
+            cp(kl, R(nb, 0, 240))
+            ts(slot("fI", l, 0, 15), kl, 4095, OP.bitwise_and)
+            cp(slot("off", l, 0, 15), slot("fI", l, 0, 15))
         step[:] = []
         act(slot("nk0", l, 0, 16), R(nb, 0, E))
         act(part(Ms, l), R(nb, E, SL))
-        ts(part(tjI, l), R("keyI", l * E + 240, (l + 1) * E), 31 * TIE, OP.bitwise_and)
+        if l:
+            move(kl, slot("nk0", l, 0, 15))
+            ts(slot("fI", l, 0, 15), kl, 4095, OP.bitwise_and)
+            move(slot("off", l, 0, 15), slot("fI", l, 0, 15))
+        move(part(mjI, l), slot("nk0", l, 15))
+        ts(part(tjI, l), part(mjI, l), 31 * TIE, OP.bitwise_and)
         ts(part(full("tjb"), l), part(tjI, l), 4096.0, OP.add)
 
     def inverse(l):
         nxl = R("nxu", 16 * l, 16 * l + 16)
+        step[:] = [INV[l], 0.0]
         add("A", lambda: g.scalar.activation(ap((lev("Zs", l), nxl)), ap(full("Zb")), AF.Silu), [full("Zb"), nxl] + ([lev("Zs", 0)] if l else []), [lev("Zs", l)],
             65 + E * 3.8 * CY + (1300 if l == 0 else 0))
-        mm([(R("Mb", 0, 16), Lm("Wd", a), R("Zs", l * E + a, (l + 1) * E, 16)) for a in range(16)], [4, 8, 12])
-        ts(R("inv", 16 * l, 16 * l + 16), R("Mb", 0, 16), 1.0 / BIG, OP.mult, -1.0, OP.add)
+        step[:] = []
+        move(lev("Zh", l), lev("Zs", l))
+        mm([(R("Mb", 0, 16), Lm("WS", a), R("Zh", l * E + a, (l + 1) * E, 16)) for a in range(16)])
+        ts(R("inv", 16 * l, 16 * l + 16), R("Mb", 0, 16), -1.0 / (BIG * S), OP.mult, -1.0, OP.add)
 
     for l in range(3):
         ms(R("W%d" % l, 2 * E - 1, 2 * E), 0.0)
@@ -445,8 +468,8 @@ def plan(r, core, T, topo, g):
     ts(t2, t2, 16.0 + MID, OP.add)
     tt(t1, t1, t2, OP.max)
     tt(e0, R("M0", 32, 48), t1, OP.add)
-    cp(R("dlb", 0, E, 1, 0, 24), R("qi", 0, E, 1, 0, 24))
-    cp(full("nxu"), full("nxi"))
+    move(R("dlb", 0, E, 1, 0, 24), R("qi", 0, E, 1, 0, 24))
+    move(full("nxu"), full("nxi"))
     for l in range(3):
         mm([(R("Mb", 0, E), R("Gd", 128 * l, 128 * l + 128, 1, 0, 24), R("dlb", 0, E, 1, 0, 24))])
         act(lev("dB", l), R("Mb", 0, E))
@@ -454,11 +477,11 @@ def plan(r, core, T, topo, g):
         if l < 2:
             bcalc(l + 1)
 
-    loop.append(1)
+    loop.append(None)
     due[0] = None
     ej = R("M0", 0, 16)
     homeI, homeN, neI, ne2 = [smi() for _ in range(4)]
-    nI, cI, tie, lowa, kI, low, mjI = [smi(48) for _ in range(7)]
+    nI, cI, tie, lowa, kI, low = [smi(48) for _ in range(6)]
     ntk, Mv, Ma, l2, tsel, selk = [sm(48) for _ in range(6)]
     sends = []
     extB = ("arrB", 3 * three, sends)
@@ -469,27 +492,29 @@ def plan(r, core, T, topo, g):
     for q in range(2):
         win = "winA" if q == 0 else "winB"
         ext = extA if q == 0 else extB
-        where = {k: R(t[2], 1 + j, t[0] * E, t[0]) for t, (w, a) in zip(TILES[q], SCANS[q]) for j, k in enumerate(a)}
-        ne, dE, SE = TILES[q][-1][0], TILES[q][-1][3], TILES[q][-1][4]
         for l in range(3):
             last = q == 1 and l == 2
-            k0 = 15 + q
+            k0 = 15
+            c = KIND[3 * q + l]
+            where = {k: R(t[2], (w is not None) + j, t[0] * E, t[0]) for t, (w, a) in zip(TILES[c], SCANS[c]) for j, k in enumerate(a)}
+            ne, dE = TILES[c][-1][0], TILES[c][-1][3]
             base = BASE[3 * q + l]
-            D = DUE[q]
+            D = DUE[c]
 
             def at(name, j=0):
                 due[0] = None if name is None else base + (D[name][j] if isinstance(D[name], list) else D[name])
+                loop[0] = name and (c, base, name, j)
             if l == 0:
                 mm([tj(0), (ej, full("idF"), full("ein") if q else e0)], ext=extE if q else None)
-            m = part(mjI, l) if q else R("keyI", l * E + 240, (l + 1) * E)
+            m = part(mjI, l)
             at("entry", 0)
-            tt(part(nI, l), ej, m, OP.min)
-            at("entry", 1)
             tt(slot("nk0", l, k0), ej, m, OP.min)
+            at("entry", 1)
+            move(part(nI, l), slot("nk0", l, k0))
             at("entry", 2)
             ts(slot("fI", l, k0), part(nI, l), 4095, OP.bitwise_and)
             at("entry", 3)
-            cp(slot("off", l, k0), slot("fI", l, k0))
+            move(slot("off", l, k0), slot("fI", l, k0))
             if not last:
                 at("entry", 4)
                 tt(homeI, ej, m, OP.max)
@@ -497,12 +522,14 @@ def plan(r, core, T, topo, g):
                 ts(homeN, homeI, HIGH + 4095, OP.bitwise_and)
             at(None)
             move(R(dE, ne - 1, ne * E, ne), lev("dB", l))
-            nv, na, ng = 0, 0, 0
-            for gi, (ka, kb, who) in enumerate(GROUPS[q]):
-                if who == "A":
+            nv, na, ng, nq = 0, 0, 0, 0
+            for gi, (ka, kb, who) in enumerate(GROUPS[c]):
+                banks = []
+                if who != "V":
                     for j in range(ka, kb, 2):
                         n2 = min(2, kb - j)
                         bk = R(DB[nbank[0] % len(DB)], 0, n2 * E)
+                        banks.append((j, n2, bk))
                         nbank[0] += 1
                         Ab = R("Ab", j * E, (j + n2) * E)
                         at("gather", na)
@@ -520,13 +547,33 @@ def plan(r, core, T, topo, g):
                         tt(R("cmp", k * E, k1 * E), (full(win), slot("off", l, k, k1)), brep(l, 0, k1 - k), OP.is_gt, ext=ext)
                 c0 = 96 * (gi // len(PB))
                 P = R(PB[gi % len(PB)], c0, c0 + 16 * (kb - ka))
-                it = [const(P, who)] + [(P, Lm("WS" if who == "V" else "WH", a), R("cmp", ka * E + a, kb * E, 16)) for a in range(16)]
+                it = [const(P, "V" if who == "V" else "A")] + [(P, Lm("WS" if who == "V" else "WH", a), R("cmp", ka * E + a, kb * E, 16)) for a in range(16)]
                 at("count", gi)
-                mm(it[:1] + [(P, full("iS"), slot("nk0", l, ka, kb))] + it[1:])
+                mm(it[:1] + [(P, full("iS"), slot("nk0", l, ka, kb))] + it[1:], [2])
                 at("o2f", gi)
-                tt(R("o2f", 16 * ka, 16 * kb), P, slot("fI", l, ka, kb), OP.min)
-                at("off2", gi)
-                cp(R("off2", 16 * ka, 16 * kb), R("o2f", 16 * ka, 16 * kb))
+                if who == "Q":
+                    ts(R("mk", 16 * ka, 16 * kb), P, 0.0, OP.is_lt)
+                    for j, n2, bk in banks:
+                        at("bcast", nq // 2)
+                        mm([(R(bk[0], a, n2 * E, 16), R("Bm", 128 * a, 128 * a + 128), R("mk", 16 * j, 16 * (j + n2))) for a in range(16)], more=True)
+                        for h in range(n2):
+                            at("qmax", nq)
+                            x = R(bk[0], h * E, (h + 1) * E)
+                            if nq:
+                                tt(lev("qa", nq % 2), x, lev("qa", 1 - nq % 2), OP.max)
+                            else:
+                                ts(lev("qa", 0), x, 0.0, OP.max)
+                            nq += 1
+                    if kb == max(x[1] for x in GROUPS[c] if x[2] == "Q"):
+                        x = R(bk[0], 0, E)
+                        at("qend", 0)
+                        mm([(x, full("iB"), brep(l, 0, 1)), (x, full("iB"), lev("qa", 1 - nq % 2))])
+                        at("qend", 1)
+                        act(where["Q"], x)
+                else:
+                    tt(R("o2f", 16 * ka, 16 * kb), P, slot("fI", l, ka, kb), OP.min)
+                    at("off2", gi)
+                    (move if gi >= QUICK else cp)(R("off2", 16 * ka, 16 * kb), R("o2f", 16 * ka, 16 * kb))
                 at("nk", gi)
                 if not last and gi == 0:
                     tt(R("nk", 0, 16 * (kb - ka)), P, slot("nk0", l, ka, kb), OP.max)
@@ -543,13 +590,17 @@ def plan(r, core, T, topo, g):
                         ng += 1
                         act(where[k], (full(win), R("off2", 16 * k, 16 * k + 16)), ext=ext)
             run, nw = brep(l, 0, 1), 0
-            for s, ((n, end, X, d, Sc), (ws, a)) in enumerate(zip(TILES[q], SCANS[q])):
-                for j, k in enumerate(ws):
+            for s, ((n, end, X, d, Sc), (ws, a)) in enumerate(zip(TILES[c], SCANS[c])):
+                for j, k in enumerate(ws or []):
                     o = R(X, 0, n * E, n) if k == ws[-1] else lev("acc", j % 2)
                     at("W", nw)
                     nw += 1
                     tt(o, (full(win), R("off2", 16 * k, 16 * k + 16)), run, OP.max, ext=ext)
                     run = o
+                if ws == []:
+                    at("W" if s else None, nw)
+                    nw += 1
+                    move(R(X, 0, n * E, n), run)
                 at("scan", s)
                 scan(full(Sc), full(d), full(X), OP.add, OP.max)
                 run = R(Sc, n - 1, n * E, n)
@@ -583,14 +634,14 @@ def plan(r, core, T, topo, g):
                 tt(neI, ne2, cf2, OP.add)
             at("Y")
             tt(full("Y"), (neI, R("inv", 16 * l, 16 * l + 16)), lev("Zs", l), OP.min)
-            it = [(ej, Lm("Wd", a), R("Y", a, E, 16)) for a in range(16)]
-            at("route")
-            if l < 2:
-                mm([tj(l + 1)] + it, [5, 9, 13])
-                at(None)
-            else:
-                mm(it, [4, 8, 12])
-                at(None)
+            at("route", 0)
+            mm([(R("M0", 64 + a, 192, 16, 0, 16), R("Y", a, E, 16), R("Wd", 16, 144, 16)) for a in range(16)], each=True)
+            at("route", 1)
+            act(R("Yt", 0, 128, 1, 0, 16), R("M0", 64, 192, 1, 0, 16))
+            at("route", 2)
+            mm(([tj(l + 1)] if l < 2 else []) + [(ej, R("Yt", 0, 128, 1, 0, 16), R("idF", 0, 16, 1, 0, 16))])
+            at(None)
+            if l == 2:
                 act(full("eout"), ej)
                 esend.append(send(full("eout"), [((r + 1) % N, full("ein"))], "arrE"))
         if q == 0:
@@ -609,11 +660,18 @@ def plan(r, core, T, topo, g):
             ts(full("tjb"), tjI, 8192.0, OP.add)
             tt(tsel, cI, ntk, OP.add)
             tt(selk, mjI, tsel, OP.min)
+            tt(Mv, nI, selk, OP.subtract)
             for l in range(3):
-                tt(lev("eqb", l), (part(selk, l), full("lE")), slot("nk0", l, 0, 16), OP.is_equal)
-                o = R("Q%d" % (l % 2), 0, E)
-                mm([(o, full("idF"), slot("nk0", l, 0, 16)), (o, full("iq"), lev("eqb", l))])
-                act(slot("nk0", l, 0, 16), o)
+                n = R("lE", 0, 15)
+                eq, dk, kl = [R(nm, l * E, l * E + 240) for nm in ("eqb", "W0", "keyI")]
+                tt(eq, (part(selk, l), n), slot("nk0", l, 0, 15), OP.is_equal)
+                tt(dk, (part(Mv, l), n), eq, OP.mult)
+                o = R("Q%d" % (l % 2), 0, 240)
+                mm([(o, full("idF"), slot("nk0", l, 0, 15)), (o, full("idF"), dk)], [1])
+                act(slot("nk0", l, 0, 15), o)
+                (move if l else cp)(kl, slot("nk0", l, 0, 15) if l else o)
+                ts(slot("fI", l, 0, 15), kl, 4095, OP.bitwise_and)
+                (move if l else cp)(slot("off", l, 0, 15), slot("fI", l, 0, 15))
     return tasks, queue, [extA, extB, extE]
 
 
@@ -814,13 +872,14 @@ def refine(tasks, pre, order, span, stride, moves, heat):
     hard = [[j for j in d if t["grp"] is None or tasks[j]["grp"] != t["grp"]] for d, t in zip(pre, tasks)]
     cost = [[t["cost"] * (fp if t["eng"] == "P" else fg if t["ind"] else 1.0) for t in tasks] for fg, fp, lat, fl in VARIANTS]
     late = [[t["lat"] * fl + lat for t in tasks] for fg, fp, lat, fl in VARIANTS]
+    eps = [0.3 if t["sem"] and t["eng"] == "G" else EPS if t["tag"] is None else EPS2 for t in tasks]
     fin = [[0.0] * n for v in VARIANTS]
     free0 = [[0.0] * 5 for v in VARIANTS]
     order = list(order)
 
     def run(seq, keep=False):
         tot = 0.0
-        for f, c, la, fr in zip(fin, cost, late, free0):
+        for f, c, la, fr, tl, te in zip(fin, cost, late, free0, tail, tend):
             free = fr if keep else fr[:]
             end = 0.0
             for i in seq:
@@ -833,13 +892,21 @@ def refine(tasks, pre, order, span, stride, moves, heat):
                 free[e] = s
                 s += la[i]
                 f[i] = s
+                tot += eps[i] * s
+                s += tl[i]
                 if s > end:
                     end = s
-            tot += end + 0.1 * (free[0] + free[1] + free[2])
+            tot += max([end] + [x + y for x, y in zip(free, te)])
         return tot
     for a0 in range(0, max(n - span, 0) + stride, stride):
         seq = order[a0:a0 + span]
         m = len(seq)
+        tail, tend = [[0.0] * n for v in VARIANTS], [[0.0] * 5 for v in VARIANTS]
+        for c, la, tl, te in zip(cost, late, tail, tend):
+            for i in order[:a0 + span - 1:-1]:
+                te[eng[i]] = c[i] + max(la[i] + tl[i], te[eng[i]])
+                for j in hard[i]:
+                    tl[j] = max(tl[j], te[eng[i]])
         cur = run(seq)
         best = (cur, seq)
         pos, far, way, warm = rng.integers(m, size=moves).tolist(), rng.exponential(1.4, moves).tolist(), rng.random(moves).tolist(), rng.exponential(1.0, moves).tolist()

@@ -7,31 +7,32 @@ E = 256
 V = 768
 WIN = 16 + 4 * V
 SL = 272
-KIND = [0, 0, 0, 0, 0, 1]
-GROUPS = [[(0, 4, "V"), (4, 8, "V"), (8, 12, "A"), (12, 16, "V")],
-          [(0, 4, "V"), (4, 8, "V"), (8, 12, "A"), (12, 16, "V")]]
-SCANS = [[([7], [0, 1, 2, 3, 4]), ([6], [5, 8, 9, 10, 11]), ([15], [12, 13, 14])],
-         [([7], [0, 1, 2, 3, 4]), ([6], [5, 8, 9, 10, 11]), ([15], [12, 13, 14])]]
-ROWS = [2700.0, 3900.0, 5100.0]
-ONTO = [6500.0, 9500.0, 14000.0]
-INV = [7600.0, 9000.0, 22000.0]
-BASE = [11000, 22500, 34000, 49500, 61000, 72500]
-_D = {"cmp": [0, 1650, 2900, 4000, 5300, 6200], "o2f": [2600, 4900, 5900, 7300], "off2": [2700, 5000, 6000, 7400],
-      "nk": [3850, 5100, 6100, 7500], "acc": [0, 5950, 7350, 7600], "entry": [2620, 2720, 3800, 3900, 3950, 4950],
-      "gather": [0, 860, 2270], "sub": [980, 2480, 3040], "sign": [1720, 3400, 3950], "count": [1760, 3900, 4600, 6400],
-      "again": [2950, 4250, 4700] + [5200 + 460 * j for j in range(12)], "W": [5500, 8000, 10300, 10400, 10500],
-      "tree": [7700, 8750, 9250, 9350], "Y": 9900, "route": [10000, 10700, 11000], "scan": [7000, 9300, 11000], "end": 11400}
-_E = {"cmp": [0, 1640, 2740, 3670, 5200], "gather": [0, 1040], "count": [1760, 3700, 4700, 6050], "route": [11400, 12080, 13520],
-      "sub": [980, 2720], "sign": [1910, 4030], "o2f": [2490, 4910, 5730, 7170], "nk": [2570, 5110, 6260, 7370],
-      "entry": [2650, 2990, 3580, 3790, 4990, 7450], "off2": [2690, 5110, 5930, 7370],
-      "again": [3110, 3570, 4580, 5050, 5530, 5990, 6460, 6920, 7380, 7850, 8310, 8770, 9230], "W": [5810, 7860, 9330],
-      "acc": [0, 5650, 7250, 7570], "scan": [6380, 8430, 9900], "tree": [7780, 8310, 9210, 9780], "Y": 10560, "end": 11010}
-DUE = [_E, _E]
-KCV = 4
-QUICK = 0
-CUT = [4, 2, 2, 3, 2, 2]
+GROUPS = [[(0, 4, "V")], [(4, 6, "V"), (6, 8, "V")], [(8, 10, "Y"), (10, 12, "Y")], [(12, 14, "V"), (14, 15, "V"), (15, 16, "V")]]
+SCANS = [[-7, 0, 1, 2, 3, 4], [-6, 5, 8, 9, 10, 11], [-15, 12, 13, 14, "fin"]]
+QUICK = False
+ISSUE = ["|ne c0 |Y c4 o0 c6 n0 c12 o4 e0 c14 e1 n4 o8 w7 a4 c15 n8 S0 a8 o12 w6 n12 S1' a12 S1 t2 w15' t1 w15 S2' S2 t0 en end",
+         "g8 g10 s8 s10 |Yt x0 x1 x2 x3 x4 x5 x8 x9 x10 x11 x12 x13 x14",
+         "v8' k0' k0'' v10' |r |r' k4' k4'' |ej k8 k8' k8'' +v10 +v8 k12 k12' k12'' h +k0 +k4",
+         "dd f0 f4 e4 e2 f8 f12"]
+PREP = ["R0 R1 R0' R0'' R2 R0''' R0'''' R1' R1'' R1''' R2' R1'''' R2'' O0 R2''' O0' R2'''' O0''", "R0 R1 R2 R0' R1' O0 R2'",
+        "R0 R0' R0'' R1 R2 R1' R1'' R2' R2'' O0 O0' O0'' O0'''", ""]
+WIDE = GROUPS[0][-1][1] - GROUPS[0][0][0]
+YB = ["D0", "D1"]
+IDV = 8
+STEP = [min(j for j, y in enumerate(SCANS) if j == s or (len(x) == len(y) and "fin" not in x + y)) for s, x in enumerate(SCANS)]
+WAYS = ["VGG", "VGG"]
+HALVED = ["S1", "w15", "S2", "end"]
+EQV = 1
+CHANGE = {1: [0, 1], 2: [2]}
+HAND = True
+PROBE = 0
+HOMEV = False
+ZP = True
+ZA = []
+KCV = 7
+BMG = 8
 PB = ["P0", "P1"]
-DB = ["D0", "D1"]
+QB = [("D0", "D1"), ("Q0", "Q1")]
 REP = 4
 TIE = 16384
 U = 32 * TIE
@@ -41,7 +42,8 @@ HIGH = 31 * U
 MG = 1.5 * 2.0 ** 23 * 2 * U
 M1 = 1.5 * 2.0 ** 23
 MID = 1520
-KC = {"mid": MID + 16.0, "q": -0.25, "M1": M1, "c0": 18.5 * U, "MG": MG, "nMG": -MG, "n18": -18.0 * U, "V": 17.75 * S, "A": 9.75 * S}
+KC = {"mid": MID + 16.0, "M1": M1, "c0": 18.5 * U, "MG": MG, "nMG": -MG, "V": 17.75 * S, "A": 19.5 * S,
+      }
 
 SCRATCH = {}
 
@@ -50,17 +52,17 @@ def _b(name, cols, dtype, rows=128, where="sbuf"):
     SCRATCH[name] = (where, [rows, cols], dtype)
 
 
-for _n, _c in (("winA", WIN), ("winB", WIN), ("pwb", V), ("bsb", V), ("bb", REP * V), ("cmp", 17 * E), ("Ab", 17 * E),
-               ("dK", 128), ("acc", 2 * E), ("dB", V), ("dS", E), ("rl", V), ("Zh", V), ("eqb", V), ("Jb", 128), ("Cb", E),
-               ("WS", 144), ("WH", 144), ("iB", 128), ("inB", 128), ("iH", 128), ("iU", 128), ("inU", 128), ("i32", 128), ("Wg", 144),
-               ("Jg", 128), ("bo", 128), ("Bm", 2048), ("mk", E), ("qa", 2 * E),
-               ("Gd", 384), ("dlb", E), ("oneB", 384), ("kc", 128 * len(KC)), ("tjb", 48)):
+for _n, _c in (("winA", WIN), ("winB", WIN), ("pwb", V), ("bsb", V), ("bb", REP * V), ("cmp", 16 * E), ("Ab", 16 * E),
+               ("dK", 128), ("dB", V), ("dS", E), ("rl", V), ("Zh", V), ("eqb", V), ("Jb", 128), ("Cb", E),
+               ("WS", 144), ("iB", 128), ("inB", 128), ("iU", 128), ("Wg", 144),
+               ("Bm", 2048), ("kb", 3 * SL), ("iS", 128), ("mk", 2 * E), ("qa", 2 * E), ("bo", 128), ("Jg", 128),
+               ("Gd", 384), ("dlb", E), ("oneB", 512), ("kc", 128 * len(KC)), ("tjb", 48)):
     _b(_n, _c, "bfloat16")
-for _n, _c in (("lo", V), ("cF", 512)):
+for _n, _c in (("lo", V), ("cF", 2 * E), ("iH", 128)):
     _b(_n, _c, "float16")
-for _n, _c in (("W0", V), ("W1", V), ("W2", V), ("kp", 3 * SL), ("nk0", 3 * SL), ("nk", SL), ("o2f", SL), ("Y", E), ("Yt", 128),
-               ("oneF", 128), ("idF", 128), ("iS", 128), ("J0", 256), ("J1", 256), ("K0", 256), ("K1", 256),
-               ("Wd", 144), ("col", 16), ("io8", 32), ("sm", 512), ("ein", 16), ("eout", 16), ("Zb", E), ("Zs", V)):
+for _n, _c in (("W", 3 * V), ("kp", 3 * SL), ("nk0", 3 * SL), ("nk", SL), ("o2f", SL), ("Y", E), ("Yt", 128),
+               ("oneF", 128), ("idF", 128), ("inF", 128), ("id2", 32), ("iS2", 128), ("iN2", 128), ("iSF", 128), ("J0", 256), ("J1", 256),
+               ("Wd", 144), ("col", 16), ("io8", 64), ("sm", 512), ("ein", 16), ("eout", 16), ("Zb", E), ("Zs", V)):
     _b(_n, _c, "float32")
 for _n, _c in (("fdi", V), ("qi", V), ("nxi", 48), ("keyI", V), ("fI", 3 * SL), ("smi", 512), ("pci", 16)):
     _b(_n, _c, "int32")
@@ -68,40 +70,25 @@ for _n, _c in (("off", 3 * SL), ("off2", SL), ("nxu", 48), ("inv", 48), ("lP", 1
     _b(_n, _c, "uint16")
 for _n in ("P0", "P1", "D0", "D1", "Q0", "Q1", "M0", "Mb"):
     _b(_n, 512, "float32", where="psum")
+for _s, _c in enumerate(SCANS):
+    for _n in "XdS":
+        _b("%s%d" % (_n, _s), len(_c) * E, "bfloat16")
 
-
-def scans(q):
-    out = []
-    for s, (w, a) in enumerate(SCANS[q]):
-        end = s == len(SCANS[q]) - 1
-        n = (w is not None) + len(a) + end
-        out.append((n, end) + tuple("%s%d%s" % (c, n, "e" if end else "s" + str(s) * (c != "d")) for c in ("X", "d", "S")))
-        for nm in out[-1][2:]:
-            _b(nm, n * E, "bfloat16")
-    return out
-
-
-TILES = [scans(0), scans(1)]
-NDMA = 24
-SEMAPHORES = ["cV", "cA", "cP", "cG", "arrA", "arrB", "arrE"] + ["d%d" % i for i in range(NDMA)]
+NDMA = 36
+SEMAPHORES = ["cV", "cA", "cP", "cG", "arrA", "arrB", "arrE", "arrF"] + ["d%d" % i for i in range(NDMA)]
 ENG_SEM = {"V": "cV", "A": "cA", "P": "cP", "G": "cG"}
+ENG = "VAPGS"
 OP = AluOpType
 AF = ActivationFunctionType
 CY = 0.83 * 1.2
 PCY = 0.42 * 1.2
 GC = 1.56
-LAT = 120.0
-RATE = 100.0
-SLACK = [40.0, 80.0, 120.0, 160.0]
-NOISE = [0.0, 50.0, 200.0, 500.0]
-PASSES = 100
-MOVES = 8000
-HEAT = 50.0
-FIT, BLIND, EPS, EPS2 = 100.0, 500.0, 0.0003, 0.001
-REFINE = [(120, 60, 10000, 120.0), (130, 50, 8000, 60.0), (120, 60, 8000, 20.0)]
+RATE = 85.0
+PASSES = 60
+REFINE = [(300, 1000, 12000, 30.0, 0.04, 0, 1), (200, 100, 7000, 30.0, 0.003)]
 ORDER = {}
 SEED = 1
-VARIANTS = [(1.0, 1.0, LAT, 1.0), (0.8, 1.3, 80.0, 0.7), (1.2, 1.0, 200.0, 1.5)]
+VARIANTS = [(1.0, 1.05, 200.0, 230.0, 1.0, 1.15), (0.75, 1.1, 160.0, 160.0, 0.8, 1.3), (1.2, 1.0, 130.0, 150.0, 0.85, 1.15)]
 
 
 def R(name, a, b, step=1, p0=0, p1=128):
@@ -130,8 +117,7 @@ def insb(x):
 
 
 def plan(r, core, T, topo, g):
-    tasks = []
-    due, step, loop = [None], [], []
+    tasks, tag, names = [], [None], set()
     queue = {"V": g.vector, "A": g.scalar, "P": g.tensor, "G": g, "S": g.sync}
 
     def ap(x):
@@ -147,12 +133,11 @@ def plan(r, core, T, topo, g):
         return out
 
     def add(eng, fn, reads, writes, cost, lat=0.0, sem=None, ext=None, grp=None):
-        if step:
-            due[0] = step[0]
-            step[0] += step[1]
-        elif not loop:
-            due[0] = None
-        tasks.append({"tag": loop[0] if loop else None, "grp": grp, "eng": eng, "fn": fn, "r": flat(reads), "w": flat(writes), "cost": cost, "lat": lat, "sem": sem, "ext": ext, "due": due[0],
+        name = tag[0]
+        while name and (name, eng) in names:
+            name = (name[0], name[1] + "'")
+        names.add((name, eng))
+        tasks.append({"tag": name, "grp": grp, "eng": eng, "fn": fn, "r": flat(reads), "w": flat(writes), "cost": cost, "lat": lat, "sem": sem, "ext": ext,
                       "ind": any(isinstance(x, tuple) and len(x) == 2 for x in reads)})
 
     def vcost(out, ins, per):
@@ -190,11 +175,11 @@ def plan(r, core, T, topo, g):
         per = 0.5 if is2(out) and is2(d0) and is2(d1) else 1
         add("V", lambda: g.vector.tensor_tensor_scan(ap(out), ap(d0), ap(d1), 0.0, op0, op1), [d0, d1], [out], vcost(out, [d1], per))
 
-    def act(out, a, func=AF.Identity, bias=0.0, scale=1.0, ext=None):
-        cost = 65 + ncols(out) * GC * CY if len(a) == 2 else 40 + max(64, ncols(out)) * CY
+    def act(out, a, func=AF.Identity, bias=0.0, scale=1.0, ext=None, more=0.0):
+        cost = more + (65 + ncols(out) * GC * CY if len(a) == 2 else 40 + max(64, ncols(out)) * CY)
         add("A", lambda: g.scalar.activation(ap(out), ap(a), func, bias=sc(bias), scale=sc(scale)), [a, bias, scale], [out], cost, ext=ext)
 
-    def mm(items, cuts=(), ext=None, more=False, each=False):
+    def mm(items, cuts=(), ext=None, more=False, each=False, hold=False):
         cuts = [0] + list(cuts) + [len(items)]
         grp = len(tasks)
         for p, p1 in zip(cuts, cuts[1:]):
@@ -202,11 +187,11 @@ def plan(r, core, T, topo, g):
                 ins = None
                 for i in range(p, p1):
                     o, l, x = items[i]
-                    ins = g.tensor.matmul(ap(o), ap(l), ap(x), each or (i == 0 and not more), each or i == len(items) - 1)
+                    ins = g.tensor.matmul(ap(o), ap(l), ap(x), each or (i == 0 and not more), each or (i == len(items) - 1 and not hold))
                 return ins
             its = items[p:p1]
-            cost = 40 + sum(max(min(64, ncols(l)), ncols(x)) * (1 if is2(x) else 4) for o, l, x in its) * PCY
-            add("P", fn, [l for o, l, x in its] + [x for o, l, x in its], [o for o, l, x in items], cost, ext=ext, grp=grp)
+            cost = sum(5 + max(min(64, ncols(l)), ncols(x)) * (1 if is2(x) else 4) * PCY for o, l, x in its)
+            add("P", fn, [l for o, l, x in its] + [x for o, l, x in its], [o for o, l, x in items], cost, lat=50.0, ext=ext, grp=grp)
 
     def const(o, name):
         j = list(KC).index(name)
@@ -214,8 +199,6 @@ def plan(r, core, T, topo, g):
 
     def move(out, a):
         add("G", lambda: g.affine_select(ap(out), ap(a), [[0, ncols(a)]], OP.is_equal, 0.0, 0, 0), [a], [out], 170 + 2 * ncols(out) * CY)
-
-    nbank = [0]
 
     def iota(out, pat, base, cm=0):
         if SCRATCH[out[0]][2] == "int32":
@@ -242,15 +225,15 @@ def plan(r, core, T, topo, g):
             return None
         add(eng, fn, reads, writes, 60.0 * len(pairs), lat=1500 + nbytes / 200.0, sem=(s, 16 * len(pairs)), ext=ext)
 
-    def rot(eng, name, dst, rows, nbytes):
+    def rot(eng, name, dst, rows, nbytes, cols=(None, None), ext=None):
         a, b = rows
         d = lambda p0, p1: (lambda: ap(dst[:4] + (p0, p1)))
-        pairs = [(d(0, (N - r) * b), lambda: T[name][r * a:N * a, :])]
+        pairs = [(d(0, (N - r) * b), lambda: T[name][r * a:N * a, cols[0]:cols[1]])]
         if r:
-            pairs.append((d((N - r) * b, N * b), lambda: T[name][0:r * a, :]))
-        dma(eng, pairs, [], [dst], nbytes)
+            pairs.append((d((N - r) * b, N * b), lambda: T[name][0:r * a, cols[0]:cols[1]]))
+        dma(eng, pairs, [], [dst], nbytes, ext)
 
-    def send(src, dsts, rsem):
+    def send(src, dsts, rsem, cost=300.0, times=None, ext=None):
         s = dsem()
         far = [(T.cores[k], x) for k, x in dsts if topo.chip(T.cores[k]) != topo.chip(core)]
         near = [(T.cores[k], x) for k, x in dsts if topo.chip(T.cores[k]) == topo.chip(core)]
@@ -269,7 +252,7 @@ def plan(r, core, T, topo, g):
                                             srcs=[ap(src)], dsts=[ap(x) for c, x in ds]))
             g.remote_dma_fused(tr, local_sem=T.sem[s])
             return None
-        add("G", fn, [src], [], 500.0, lat=2000 + ncols(src) * 256 * len(dsts) / RATE, sem=(s, sum(len(es) for ds, es in sets)))
+        add("G", fn, [src], [], cost, lat=2000 + ncols(src) * 256 * (times or len(dsts)) / (RATE if far else 2 * RATE), sem=(s, sum(len(es) for ds, es in sets)), ext=ext)
         return len(tasks) - 1
 
     def landed(k):
@@ -299,20 +282,41 @@ def plan(r, core, T, topo, g):
     def lev(name, l, o=0):
         return R(name, o + l * E, o + (l + 1) * E)
 
-    step[:] = [0.0, 10.0]
     rot("S", "t0", R("winA", 16, 16 + V), (16, 16), 196608)
     for l in range(3):
         c0, c1 = l * E, (l + 1) * E
-        dma("A", [(lambda c0=c0, c1=c1: T.fdi[:, c0:c1], lambda c0=c0, c1=c1: T.fd[:, c0:c1])], [], [lev("fdi", l)], 196608 * (l + 1))
-        dma("A", [(lambda c0=c0, c1=c1: T.pwb[:, c0:c1], lambda c0=c0, c1=c1: T.pw[:, c0:c1])], [], [lev("pwb", l)], 196608 * (l + 1) + 65536)
-    rot("S", "bs", full("bsb"), (16, 16), 196608)
+        dma("A", [(lambda c0=c0, c1=c1: T.fdi[:, c0:c1], lambda c0=c0, c1=c1: T.fd[:, c0:c1]),
+                  (lambda c0=c0, c1=c1: T.pwb[:, c0:c1], lambda c0=c0, c1=c1: T.pw[:, c0:c1])],
+            [], [lev("fdi", l), lev("pwb", l)], 196608 * (l + 2))
+    rot("S", "bs", full("bsb"), (16, 16), 2 * 196608)
     dma("S", [(lambda: T.qi[0:8, 256:512], lambda: T.cf[:, :]), (lambda: T.qi[0:8, 512:768], lambda: T.cw[:, :])], [], [R("qi", 256, 768)], 16384)
     rot("S", "nx", full("nxi"), (16, 16), 24576)
     rot("S", "dl", R("qi", 0, 256), (1, 3), 24576)
-    step[:] = [2500.0, 0.0]
-    s0 = send(R("winA", 16, 16 + V), [((r + h) % N, R("winA", 16 + h * V, 16 + (h + 1) * V)) for h in (1, 2, 3)], "arrA")
-    step[:] = []
-    extA = ("arrA", three, [s0])
+    nload = len(tasks)
+    for i in range(1, nload):
+        tasks[i]["after"] = [j for j in range(i) if tasks[j]["eng"] == tasks[i]["eng"]]
+    def pair(k):
+        c = T.cores[k % N]
+        far = [(k + h) % N for h in (1, 2, 3) if topo.chip(T.cores[(k + h) % N]) != topo.chip(c)]
+        two = [x for x in far if sum(topo.chip(T.cores[y]) == topo.chip(T.cores[x]) for y in far) == 2]
+        return sorted(two, key=lambda x: topo.die(T.cores[x]) != topo.die(c)) if len(far) == 3 and HAND else []
+
+    block = lambda k, src: R("winA", 16 + (k - src) % N * V, 16 + ((k - src) % N + 1) * V)
+    readers = [(r + h) % N for h in (1, 2, 3)]
+    if pair(r):
+        s0 = send(block(r, r), [(pair(r)[0], block(pair(r)[0], r))], "arrF", 1300.0)
+        s1 = send(block(r, r), [(k, block(k, r)) for k in readers if k not in pair(r)], "arrA", 300.0, 2)
+        tasks[s1]["after"] = [s0]
+    else:
+        s0 = send(block(r, r), [(k, block(k, r)) for k in readers], "arrA", 1300.0)
+        add("G", None, [], [], 0.0)
+    mine = [k for k in range(N) if pair(k)[:1] == [r]]
+    extF = ({"arrF": sum(landed(k) for k in mine)}, [s0])
+    if mine:
+        s2 = send(block(r, mine[0]), [(pair(mine[0])[1], block(pair(mine[0])[1], mine[0]))], "arrA", 300.0, ext=extF)
+    else:
+        add("G", None, [], [], 0.0)
+    extA = (dict(extF[0], arrA=sum(0 if pair(r - h)[:1] == [r] else landed(pair(r - h)[0] if r in pair(r - h) else r - h) for h in (1, 2, 3))), [s0, s0 + 1, s0 + 2])
 
     col = lambda j: R("col", j, j + 1)
     pf, pg, par1, par0, kc, p16x, par1n, par0n = [col(j) for j in range(8)]
@@ -324,7 +328,6 @@ def plan(r, core, T, topo, g):
     ts(par0, par1, -1.0, OP.mult, 1.0, OP.add)
     ts(kc, pf, float(TIE), OP.mult, float(TIE + U), OP.add)
     ts(p16x, pf, 16.0, OP.mult)
-    ts(R("col", 6, 8), R("col", 2, 4), -2.0, OP.mult)
     ms(full("oneF"), 1.0)
     ms(full("oneB"), 1.0)
     for j, nm in enumerate(KC):
@@ -333,17 +336,19 @@ def plan(r, core, T, topo, g):
         else:
             act(R("kc", 128 * j, 128 * j + 128, 1, 0, 1), R("oneF", 0, 128, 1, 0, 1), scale=KC[nm])
     sel(full("idF"), full("oneF"), [[-1, 128]], 0)
-    for nm, val in (("i32", -32.0), ("iB", 1.0), ("iU", float(U)), ("inU", -float(U)), ("iH", 0.5), ("inB", -1.0), ("iS", -S / U)):
-        act(full(nm), full("idF"), scale=val)
-    act(full("dK"), full("idF"), scale=kc)
-    for nm, c in (("K0", par0n), ("K1", par1n), ("J0", par0), ("J1", par1)):
+    act(full("iB"), full("idF"))
+    scaled = (("iH", 511 / 1024), ("iS", -S / U), ("dK", kc), ("inB", -1.0), ("iS2", -2 * S / U), ("iN2", -2.0), ("iSF", -S / U), ("inF", -1.0), ("iU", float(U)))
+    for nm, val in scaled[:IDV]:
+        ts(full(nm), full("iB"), val, OP.mult)
+    for nm, val in scaled[IDV:]:
+        act(full(nm), full("idF"), scale=val, func=AF.Silu if nm == "iU" else AF.Identity, more=1300.0 * (nm == "iU"))
+    for nm, c in (("J0", par0), ("J1", par1)):
         act(R(nm, 0, 128), full("idF"), scale=c)
         act(R(nm, 128, 256), full("idF"), scale=c)
     iota(R("io8", 0, 18), [[1, 18]], 0)
     ms(full("Wd"), 0.0)
     ts(R("Wd", 16, 144, 16), R("io8", 0, 8), pg, OP.is_equal)
     act(full("WS"), full("Wd"), scale=-S)
-    act(full("WH"), full("Wd"), scale=-S / 2)
     ms(R("Wg", 0, 144, 1, 0, 32), 0.0)
     cut = N - r if r else N // 2
     sel(R("Wg", 16, 16 + 16 * cut, 16, 0, 8), R("oneB", 0, cut, 1, 0, 8), [[-1, cut]], -r)
@@ -354,118 +359,118 @@ def plan(r, core, T, topo, g):
     sel(R("Cb", 0, E, 1, 0, 16), R("Cb", 0, E, 1, 0, 16), [[0, 16], [-1, 16]], 0)
     mm([(R("D1", 0, E), R("Jb", 0, 128, 1, 0, 16), R("Cb", 0, E, 1, 0, 16))])
     act(full("Zb"), R("D1", 0, E), scale=BIG)
-    ts(R("lP", 0, 15), R("io8", 0, 15), p16x, OP.add, 256.0, OP.add)
-    ts(R("lP", 15, 16), p16x, 15.0, OP.add)
-    ts(R("lP", 16, 17), p16x, 512.0 + 14, OP.add)
+    iota(R("io8", 20, 35), [[1, 15]], E)
+    iota(R("io8", 35, 37), [[2 * E - 1, 2]], 15)
+    ts(R("lP", 0, 17), R("io8", 20, 37), p16x, OP.add)
     ts(full("lE"), R("oneF", 0, 16), pf, OP.mult)
     cf2 = sm()
-    ts(cf2, R("io8", 0, 16), 16.0, OP.mult, pf, OP.add)
-    ts(cf2, cf2, 16.0 + V + 2 * E, OP.add)
+    iota(R("io8", 40, 56), [[16, 16]], 16 + V + 2 * E)
+    ts(cf2, R("io8", 40, 56), pf, OP.add)
     ms(full("dS"), 0.0)
     ms(R("dS", 0, E, 16), BIG)
-    for n, end, X, d, Sc in {t[3]: t for t in TILES[0] + TILES[1]}.values():
-        for h in range(2):
-            ms(R(d, h * 128 * n, (h + 1) * 128 * n), 0.0)
-        ms(R(d, 0, n * E, n), -512.0)
-        if end:
-            ms(R(X, n - 1, n * E, n), 0.0)
-    if any(x[2] == "Q" for gr in GROUPS for x in gr):
+    for s, cols in enumerate(SCANS):
+        n, d = len(cols), "d%d" % s
+        for j, k in enumerate(cols):
+            if k == "fin":
+                ms(R("X%d" % s, j, n * E, n), 0.0)
+            elif STEP[s] == s:
+                ms(R(d, j, n * E, n), 0.0 if j else -512.0)
+    anyq = any(x[2] == "Q" for parts in GROUPS for x in parts)
+    for a in range(0, BMG * anyq, 4):
+        sel(R("Bm", 128 * a, 128 * a + 512), full("oneB"), [[-1, 4], [-16, 8], [0, 16]], -a)
+    if BMG < 16 and anyq:
         sel(R("Jg", 0, 128, 1, 0, 8), R("oneB", 0, 128, 1, 0, 8), [[-1, 8], [0, 16]], 0)
-        mm([(R("D0", 0, 128), R("Jg", 0, 128, 1, 0, 8), R("Jg", 0, 128, 1, 0, 8))])
-        act(full("bo"), R("D0", 0, 128))
+        mm([(R("D1", 0, 128), R("Jg", 0, 128, 1, 0, 8), R("Jg", 0, 128, 1, 0, 8))])
+        act(full("bo"), R("D1", 0, 128))
         am = sm()
-        ts(am, R("io8", 0, 16), pf, OP.is_equal, -512.0, OP.mult)
-        for a in range(16):
-            if a % 2:
-                ts(R("Bm", 128 * a, 128 * a + 128), full("bo"), R("sm", am[1] + a, am[1] + a + 1), OP.mult)
-            else:
-                act(R("Bm", 128 * a, 128 * a + 128), full("bo"), scale=R("sm", am[1] + a, am[1] + a + 1))
+        ts(am, R("io8", 0, 16), pf, OP.is_equal)
+        for a in range(BMG, 16):
+            ts(R("Bm", 128 * a, 128 * a + 128), full("bo"), R("sm", am[1] + a, am[1] + a + 1), OP.mult)
     ms(R("winA", 0, 16), 0.0)
     ms(R("winB", 0, 16), 0.0)
-    dma("S", [(lambda: T.winB[:, 16:16 + V], lambda: T.bsb[:, :])], [full("bsb")], [R("winB", 16, 16 + V)], 196608, extA)
 
     def Lm(name, a, p1=128):
         return R(name, 16 - a, 144 - a, 1, 0, p1)
 
-    def bcalc(l):
+    def bcalc(l, copy=move):
         o = R("Mb", 0, E)
-        mm([(o, full("iH"), lev("bsb", l)), (o, full("iH"), lev("winA", l, 16)), const(o, "q"), const(o, "M1")])
+        mm([(o, full("iH"), lev("bsb", l)), (o, full("iH"), lev("winA", l, 16)), const(o, "M1")])
         act(brep(l, 0, 1), o, bias=-M1)
         for j in range(1, REP):
-            move(brep(l, j, j + 1), brep(l, 0, 1))
+            copy(brep(l, j, j + 1), brep(l, 0, 1))
 
-    def brep(l, j, j1):
-        return R("bb", (l * REP + j) * E, (l * REP + j1) * E)
+    def brep(l, j, j1, h=None):
+        return R("bb", (l * REP + j) * E + (h or 0), (l * REP + j1) * E, 1 if h is None else 2)
 
-    Ms, tjI, mjI = sm(48), smi(48), smi(48)
+    Ms, ml, tjI, mjI = sm(48), sm(48), smi(48), smi(48)
 
-    def rows(l, kb, tb):
-        W = "W%d" % l
-        x = R(kb, 0, E)
-        step[:] = [ROWS[l], 400.0]
+    def rows(l, kb):
+        W = lambda a, b: R("W", l * V + a, l * V + b)
+        x, tb = R(kb, 0, E), R(kb, E, 2 * E)
         ts(lev("lo", l), lev("fdi", l), -float(MID), OP.add)
-        mm([(x, full("iB"), lev("pwb", l)), (x, full("i32"), lev("lo", l))])
-        act(lev("rl", l), x, func=AF.Relu, bias=nmid)
+        mm([(x, full("iB"), lev("pwb", l)), (x, full("iS"), lev("lo", l))])
+        act(lev("rl", l), x, func=AF.Relu, scale=4096.0, bias=-4096.0 * (128 * MID + 127))
         mm([(x, full("iB"), lev("lo", l)), (x, full("iU"), lev("pwb", l)), (x, full("dK"), R("oneB", 0, E)), const(x, "mid"),
-            (x, full("inU"), lev("rl", l))], [4])
-        add("V", lambda: g.vector.transpose(ap(R(tb, 0, E)), ap(x)), [x], [R(tb, 0, E)], 20 + E * CY)
-        scan(R(W, 0, E), full("dS"), R(tb, 0, E), OP.add, OP.min)
-        tt(R(W, E, 2 * E - 1), R(W, 0, E - 1), R(tb, 1, E), OP.max)
-        scan(R(W, 2 * E, 3 * E), full("dS"), R(W, E, 2 * E), OP.add, OP.min)
-        act(slot("kp", l, 0, 17), (full(W), R("lP", 0, 17)))
-        step[:] = []
+            (x, full("iS"), lev("rl", l))], [4])
+        add("V", lambda: g.vector.transpose(ap(tb), ap(x)), [x], [tb], 20 + E * CY)
+        scan(W(0, E), full("dS"), tb, OP.add, OP.min)
+        tt(W(E, 2 * E - 1), W(0, E - 1), R(kb, E + 1, 2 * E), OP.max)
+        scan(W(2 * E, 3 * E), full("dS"), W(E, 2 * E), OP.add, OP.min)
+        act(slot("kp", l, 0, 17), (W(0, V), R("lP", 0, 17)))
 
     def onto(l, nb):
         def fix(nm, bank, n):
             return [(R(bank, x1, n, 2), R(nm + str(x1), (16 * (x1 + r - g0)) % 128, (16 * (x1 + r - g0)) % 128 + 128),
                      R("kp", l * SL + g0, l * SL + n, 2)) for x1 in (0, 1) for g0 in (0, 1)]
-        kl = R("keyI", l * E, l * E + 240)
-        step[:] = [ONTO[l], 600.0]
-        mm([const(R(nb, 0, SL), "c0")] + fix("K", nb, E) + [const(R(nb, 0, SL), "MG"), const(R(nb, 0, SL), "nMG"), const(R(nb, E, SL), "n18")]
-           + fix("J", nb, SL), [3, 5, 10])
-        if l == 0:
-            step[1] = 300.0
-            cp(kl, R(nb, 0, 240))
-            ts(slot("fI", l, 0, 15), kl, 4095, OP.bitwise_and)
-            cp(slot("off", l, 0, 15), slot("fI", l, 0, 15))
-        step[:] = []
-        act(slot("nk0", l, 0, 16), R(nb, 0, E))
+        mm(fix("J", nb, SL), [1, 2, 3])
+        feeders(l, nb, "kp", 16, WAYS[0][l])
         act(part(Ms, l), R(nb, E, SL))
-        if l:
-            move(kl, slot("nk0", l, 0, 15))
-            ts(slot("fI", l, 0, 15), kl, 4095, OP.bitwise_and)
-            move(slot("off", l, 0, 15), slot("fI", l, 0, 15))
+        o = R(nb, 0, E)
+        mm([const(o, "c0"), (o, full("iN2"), slot("kp", l, 0, 16)), const(o, "MG"), const(o, "nMG"), (o, full("idF"), slot("kp", l, 0, 16))], [2, 4])
+        act(slot("nk0", l, 0, 16), o)
         move(part(mjI, l), slot("nk0", l, 15))
-        ts(part(tjI, l), part(mjI, l), 31 * TIE, OP.bitwise_and)
-        ts(part(full("tjb"), l), part(tjI, l), 4096.0, OP.add)
+        if l != 1:
+            two = lambda x: R(x[0], x[1] + 16 * (l > 0), x[1] + 16 * (l + 1))
+            ts(two(tjI), two(mjI), 31 * TIE, OP.bitwise_and)
+            ts(two(full("tjb")), two(tjI), 4096.0, OP.add)
+            tt(two(ml), two(mjI), two(tjI), OP.subtract)
+
+    def feeders(l, nb, keys, n, way):
+        o, kl, lo = R(nb, 0, 240), R("keyI", l * E, l * E + 240), slot("fI", l, 0, 15)
+        if way == "V":
+            cp(kl, o)
+        act(slot(keys, l, 0, n), R(nb, 0, 16 * n))
+        if way == "G":
+            move(kl, slot(keys, l, 0, 15))
+        ts(lo, kl, 4095, OP.bitwise_and)
+        (cp if way == "V" else move)(slot("off", l, 0, 15), lo)
 
     def inverse(l):
         nxl = R("nxu", 16 * l, 16 * l + 16)
-        step[:] = [INV[l], 0.0]
-        add("A", lambda: g.scalar.activation(ap((lev("Zs", l), nxl)), ap(full("Zb")), AF.Silu), [full("Zb"), nxl] + ([lev("Zs", 0)] if l else []), [lev("Zs", l)],
-            65 + E * 3.8 * CY + (1300 if l == 0 else 0))
-        step[:] = []
+        add("A", lambda: g.scalar.activation(ap((lev("Zs", l), nxl)), ap(full("Zb")), AF.Silu), [full("Zb"), nxl, full("iU")], [lev("Zs", l)],
+            65 + E * 3.8 * CY)
         move(lev("Zh", l), lev("Zs", l))
         mm([(R("Mb", 0, 16), Lm("WS", a), R("Zh", l * E + a, (l + 1) * E, 16)) for a in range(16)])
         ts(R("inv", 16 * l, 16 * l + 16), R("Mb", 0, 16), -1.0 / (BIG * S), OP.mult, -1.0, OP.add)
 
-    for l in range(3):
-        ms(R("W%d" % l, 2 * E - 1, 2 * E), 0.0)
-    nmid = -32.0 * MID - 31
-    rows(0, "P0", "P1")
-    rows(1, "Q0", "Q1")
-    rows(2, "D1", "P0")
-    onto(0, "D0")
-    onto(1, "Q0")
-    onto(2, "Q1")
-    bcalc(0)
-    ts(R("cF", 0, 512, 1, 0, 8), R("qi", 256, 768, 1, 0, 8), -float(MID), OP.add)
-    mm([(R("M0", 32, 64), Lm("Wg", a, 8), R("cF", a, 512, 16, 0, 8)) for a in range(16)])
+    ms(R("W", 2 * E - 1, 3 * V, V), 0.0)
+    for l, bank in enumerate(("P0", "P1", "Q0")):
+        tag[0] = (0, "R%d" % l)
+        rows(l, bank)
+    for l, bank in enumerate(("D0", "Q1", "Q0")):
+        tag[0] = (0, "O%d" % l)
+        onto(l, bank)
+    tag[0] = None
+    bcalc(0, cp)
+    for j in range(PROBE):
+        add("V", lambda: g.vector.memset(ap(full("cmp")), 0.0), [slot("off", 0, 0, 15), brep(0, 0, 4), R("W", 0, 3 * V)], [full("cmp")], 2060.0)
+    ts(R("cF", 0, E, 1, 0, 8), R("qi", 256, 512, 1, 0, 8), -float(MID), OP.add)
+    move(R("cF", E, 2 * E, 1, 0, 8), R("qi", 512, 768, 1, 0, 8))
+    mm([(R("M0", 32, 64), Lm("Wg", a, 8), R("cF", a, 2 * E, 16, 0, 8)) for a in range(16)], [8])
     e0, t1, t2, t3 = sm(), sm(), sm(), sm()
     act(t3, R("M0", 32, 48), func=AF.Relu, scale=-1.0, bias=-float(MID))
     act(t1, t3, scale=18.0 * U + 16 + MID)
-    act(t2, R("M0", 48, 64), scale=-float(U), bias=(17.0 - MID) * U)
-    ts(t2, t2, 16.0 + MID, OP.add)
+    act(t2, R("M0", 48, 64), scale=-float(U), bias=17.0 * U + 16 + MID)
     tt(t1, t1, t2, OP.max)
     tt(e0, R("M0", 32, 48), t1, OP.add)
     move(R("dlb", 0, E, 1, 0, 24), R("qi", 0, E, 1, 0, 24))
@@ -474,20 +479,75 @@ def plan(r, core, T, topo, g):
         mm([(R("Mb", 0, E), R("Gd", 128 * l, 128 * l + 128, 1, 0, 24), R("dlb", 0, E, 1, 0, 24))])
         act(lev("dB", l), R("Mb", 0, E))
         inverse(l)
-        if l < 2:
-            bcalc(l + 1)
 
-    loop.append(None)
-    due[0] = None
-    ej = R("M0", 0, 16)
-    homeI, homeN, neI, ne2 = [smi() for _ in range(4)]
+    for t in tasks[s0 + 3:]:
+        if t["eng"] == "G" and t["w"][0][0] not in ("pci", "idF", "io8", "Cb", "Jb"):
+            t["after"] = [s0]
+    early = [i for i, t in enumerate(tasks) if t["eng"] == "G" and t["w"] and t["w"][0][0] in ("io8", "Cb", "Jb", "Wg", "cF", "nxu", "Gd", "dlb")]
+    tasks.append(tasks[s0 + 2])
+    tasks[s0 + 2] = dict(tasks[s0 + 2], fn=None, r=[], sem=None, ext=None, cost=0.0, lat=0.0)
+    tasks[-1]["after"] = early
+    extA[1][2] = len(tasks) - 1
+    dma("S", [(lambda: T.winB[:, 16:16 + V], lambda: T.pwb[:, :])], [full("pwb")], [R("winB", 16, 16 + V)], 2 * 196608, extA)
+    for l in (1, 2):
+        bcalc(l)
+    ej, ej2, home = R("M0", 0, 16), R("M0", 16, 32), sm()
+    if HOMEV:
+        sel(R("id2", 0, 32, 1, 0, 16), R("oneF", 0, 32, 1, 0, 16), [[0, 2], [-1, 16]], 0)
+    neI, ne2, eI = smi(), smi(), smi()
     nI, cI, tie, lowa, kI, low = [smi(48) for _ in range(6)]
     ntk, Mv, Ma, l2, tsel, selk = [sm(48) for _ in range(6)]
     sends = []
-    extB = ("arrB", 3 * three, sends)
+    extB = ({"arrB": 3 * three}, sends)
     esend = []
-    extE = ("arrE", landed(r - 1), esend)
+    extE = ({"arrE": landed(r - 1)}, esend)
     tj = lambda l: (ej, full("iB"), part(full("tjb"), l))
+    column = {k: R("X%d" % s, j, len(cols) * E, len(cols)) for s, cols in enumerate(SCANS) for j, k in enumerate(cols)}
+
+    both = [lambda x: (x[0], x[1], x[1] + ncols(x) // 2 * x[3]) + x[3:], lambda x: (x[0], x[1] + ncols(x) // 2 * x[3], x[2]) + x[3:]]
+    whole = [lambda x: x]
+
+    def halves(name):
+        return both if name in HALVED else whole
+
+    def result(s, h=None):
+        n = len(SCANS[s])
+        return R("S%d" % s, n - 1 + n * (h or 0), n * E, n if h is None else 2 * n)
+    lastq = ([0] + [x[1] - 1 for parts in GROUPS for x in parts if x[2] == "Q"])[-1]
+
+    def change(levels):
+        w = lambda x: R(x[0], x[1] + 16 * levels[0], x[1] + 16 * levels[-1] + 16)
+        ts(w(tie), w(cI), 31 * TIE, OP.bitwise_and)
+        ts(w(ntk), w(tie), 0.0, OP.is_equal, BIG, OP.mult)
+        tt(w(Mv), w(tie), w(ntk), OP.add)
+        ts(w(lowa), w(nI), U - 1, OP.bitwise_and)
+        ts(w(l2), w(lowa), 2.0, OP.mult, 18.0 * U, OP.add)
+        tt(w(Ma), w(l2), w(nI), OP.subtract)
+        tt(w(Ma), w(Ma), w(Ms), OP.min)
+        tt(w(kI), w(Ma), w(Mv), OP.min)
+        ts(w(low), w(kI), U - 1, OP.bitwise_and)
+        ts(w(l2), w(low), 2.0, OP.mult, 18.0 * U, OP.add)
+        tt(w(mjI), w(l2), w(kI), OP.subtract)
+        ts(w(tjI), w(kI), 31 * TIE, OP.bitwise_and)
+        ts(w(full("tjb")), w(tjI), 8192.0, OP.add)
+        tt(w(ml), w(mjI), w(tjI), OP.subtract)
+        tt(w(tsel), w(cI), w(ntk), OP.add)
+        tt(w(selk), w(mjI), w(tsel), OP.min)
+        tt(w(Mv), w(nI), w(selk), OP.subtract)
+        for l in levels:
+            n = R("lE", 0, 15)
+            eq, dk = [R(nm, l * E, l * E + 240) for nm in ("eqb", "W")]
+            o = R("Q%d" % (l % 2), 0, 240)
+            if l < EQV:
+                tt(eq, (part(selk, l), n), slot("nk0", l, 0, 15), OP.is_equal)
+            else:
+                act(dk, (part(selk, l), n))
+                mm([(o, full("idF"), slot("nk0", l, 0, 15)), (o, full("inF"), dk)], [1])
+                act(eq, o, func=AF.Abs)
+                act(eq, eq, func=AF.Relu, scale=-1.0, bias=1.0)
+            tt(dk, (part(Mv, l), n), eq, OP.mult)
+            mm([(o, full("idF"), slot("nk0", l, 0, 15)), (o, full("idF"), dk)], [1])
+            feeders(l, o[0], "nk0", 15, WAYS[1][l])
 
     for q in range(2):
         win = "winA" if q == 0 else "winB"
@@ -495,117 +555,119 @@ def plan(r, core, T, topo, g):
         for l in range(3):
             last = q == 1 and l == 2
             k0 = 15
-            c = KIND[3 * q + l]
-            where = {k: R(t[2], (w is not None) + j, t[0] * E, t[0]) for t, (w, a) in zip(TILES[c], SCANS[c]) for j, k in enumerate(a)}
-            ne, dE = TILES[c][-1][0], TILES[c][-1][3]
-            base = BASE[3 * q + l]
-            D = DUE[c]
-
-            def at(name, j=0):
-                due[0] = None if name is None else base + (D[name][j] if isinstance(D[name], list) else D[name])
-                loop[0] = name and (c, base, name, j)
+            came = lambda o: (o, R("Yt", 0, 128, 1, 0, 16), R("idF", 0, 16, 1, 0, 16)) if l else (o, full("idF"), full("ein") if q else e0)
             if l == 0:
-                mm([tj(0), (ej, full("idF"), full("ein") if q else e0)], ext=extE if q else None)
-            m = part(mjI, l)
-            at("entry", 0)
-            tt(slot("nk0", l, k0), ej, m, OP.min)
-            at("entry", 1)
-            move(part(nI, l), slot("nk0", l, k0))
-            at("entry", 2)
+                mm([tj(0), came(ej)], ext=extE if q else None)
+            def at(name, lv=3 * q + l):
+                tag[0] = name and (lv, name)
+            at("e0")
+            tt(part(nI, l), ej, part(mjI, l), OP.min)
+            at("e1")
             ts(slot("fI", l, k0), part(nI, l), 4095, OP.bitwise_and)
-            at("entry", 3)
-            move(slot("off", l, k0), slot("fI", l, k0))
+            at("e2")
+            (cp if QUICK else move)(slot("off", l, k0), slot("fI", l, k0))
+            at("e4")
+            move(slot("nk0", l, k0), part(nI, l))
             if not last:
-                at("entry", 4)
-                tt(homeI, ej, m, OP.max)
-                at("entry", 5)
-                ts(homeN, homeI, HIGH + 4095, OP.bitwise_and)
-            at(None)
-            move(R(dE, ne - 1, ne * E, ne), lev("dB", l))
-            nv, na, ng, nq = 0, 0, 0, 0
-            for gi, (ka, kb, who) in enumerate(GROUPS[c]):
-                banks = []
-                if who != "V":
-                    for j in range(ka, kb, 2):
-                        n2 = min(2, kb - j)
-                        bk = R(DB[nbank[0] % len(DB)], 0, n2 * E)
-                        banks.append((j, n2, bk))
-                        nbank[0] += 1
-                        Ab = R("Ab", j * E, (j + n2) * E)
-                        at("gather", na)
-                        act(Ab, (full(win), slot("off", l, j, j + n2)), ext=ext)
-                        at("sub", na)
-                        mm([(bk, full("iB"), Ab), (bk, full("inB"), brep(l, 0, n2))])
-                        at("sign", na)
-                        act(R("cmp", j * E, (j + n2) * E), bk, func=AF.Sign, bias=-0.5)
-                        na += 1
+                at("h")
+                if HOMEV:
+                    tt(home, R("M0", 16, 32), part(ml, l), OP.max)
                 else:
-                    cuts = sorted(set(list(range(ka, min(kb, k0), CUT[gi])) + [min(kb, k0), kb]))
-                    for k, k1 in zip(cuts, cuts[1:]):
-                        at("cmp", nv)
-                        nv += 1
+                    mm([tj(l), came(ej), (ej, full("inF"), slot("nk0", l, k0)), (ej, full("idF"), part(ml, l))])
+            at("dd")
+            move(R("d%d" % (len(SCANS) - 1), len(SCANS[-1]) - 1, len(SCANS[-1]) * E, len(SCANS[-1])), lev("dB", l))
+            nq, ny, ns, done = 0, 0, 0, set()
+            for gi, parts in enumerate(GROUPS):
+                ka, kb = parts[0][0], parts[-1][1]
+                bank = PB[gi % 2]
+                head = []
+                for k, k1, who in parts:
+                    run = [x for x in parts if (x[2] == "V") == (who == "V")]
+                    if k == run[0][0]:
+                        x = R(bank, 16 * k, 16 * run[-1][1])
+                        head += [const(x, "V" if who == "V" else "A"), (x, full("iSF" if who == "V" else "iS2"), slot("nk0", l, k, run[-1][1]))]
+                    if who == "V":
+                        at("c%d" % k)
                         tt(R("cmp", k * E, k1 * E), (full(win), slot("off", l, k, k1)), brep(l, 0, k1 - k), OP.is_gt, ext=ext)
-                c0 = 96 * (gi // len(PB))
-                P = R(PB[gi % len(PB)], c0, c0 + 16 * (kb - ka))
-                it = [const(P, "V" if who == "V" else "A")] + [(P, Lm("WS" if who == "V" else "WH", a), R("cmp", ka * E + a, kb * E, 16)) for a in range(16)]
-                at("count", gi)
-                mm(it[:1] + [(P, full("iS"), slot("nk0", l, ka, kb))] + it[1:], [2])
-                at("o2f", gi)
-                if who == "Q":
-                    ts(R("mk", 16 * ka, 16 * kb), P, 0.0, OP.is_lt)
-                    for j, n2, bk in banks:
-                        at("bcast", nq // 2)
-                        mm([(R(bk[0], a, n2 * E, 16), R("Bm", 128 * a, 128 * a + 128), R("mk", 16 * j, 16 * (j + n2))) for a in range(16)], more=True)
-                        for h in range(n2):
-                            at("qmax", nq)
-                            x = R(bk[0], h * E, (h + 1) * E)
-                            if nq:
-                                tt(lev("qa", nq % 2), x, lev("qa", 1 - nq % 2), OP.max)
-                            else:
-                                ts(lev("qa", 0), x, 0.0, OP.max)
-                            nq += 1
-                    if kb == max(x[1] for x in GROUPS[c] if x[2] == "Q"):
-                        x = R(bk[0], 0, E)
-                        at("qend", 0)
-                        mm([(x, full("iB"), brep(l, 0, 1)), (x, full("iB"), lev("qa", 1 - nq % 2))])
-                        at("qend", 1)
-                        act(where["Q"], x)
+                        continue
+                    for j in range(k, k1, 2):
+                        j1 = min(j + 2, k1)
+                        at("g%d" % j)
+                        act(R("Ab", j * E, j1 * E), (full(win), slot("off", l, j, j1)), ext=ext)
+                        bk = R(YB[ny % len(YB)], 0, (j1 - j) * E)
+                        ny += 1
+                        at("v%d" % j)
+                        mm([(bk, full("inB"), brep(l, 0, j1 - j)), (bk, full("iB"), R("Ab", j * E, j1 * E))], [1])
+                        at("s%d" % j)
+                        act(R("cmp", j * E, j1 * E), bk, func=AF.Sign, bias=-0.5)
+                at("k%d" % ka)
+                P = R(bank, 16 * ka, 16 * kb)
+                order = list(range(0, 16, 2)) + list(range(1, 16, 2))
+                it = [(P, Lm("WS", a), R("cmp", ka * E + a, kb * E, 16)) for a in order]
+                mm(head + it, [len(head), len(head) + 8])
+                again = [k for k, k1, who in parts if who != "Q"]
+                for k, k1, who in parts:
+                    if who == "Q":
+                        mk = R("mk", 16 * k, 16 * k1)
+                        at("m%d" % k)
+                        ts(mk, R(bank, 16 * k, 16 * k1), 0.0, OP.is_lt, -512.0, OP.mult)
+                        for h in (0, 1):
+                            at("B%d" % k + "ab"[h])
+                            mm([(R(QB[nq][h], 0, (k1 - k) * 128), full("iB"), R("Ab", k * E + h, k1 * E, 2))]
+                               + [(R(QB[nq][h], a // 2, (k1 - k) * 128, 8), R("Bm", 128 * a, 128 * a + 128), mk) for a in range(h, 16, 2)], [1])
+                            for j in range(k1 - k):
+                                x, run = R(QB[nq][h], 128 * j, 128 * j + 128), R("qa", 128 * h, 128 * h + 128)
+                                c = column["q"]
+                                o = R(c[0], c[1] + h * c[3], c[2], 2 * c[3]) if k + j == lastq else run
+                                at("q%d" % (k + j) + "ab"[h])
+                                tt(o, x, run if nq or j else result(0, h) if "b" in column else brep(l, 0, 1, h), OP.max)
+                        nq += 1
+                if again:
+                    kr = again[0]
+                    at("o%d" % ka)
+                    tt(R("o2f", 16 * kr, 16 * kb), R(bank, 16 * kr, 16 * kb), slot("fI", l, kr, kb), OP.min)
+                    at("f%d" % ka)
+                    move(R("off2", 16 * kr, 16 * kb), R("o2f", 16 * kr, 16 * kb))
+                    for k in range(kr, kb):
+                        if k in column:
+                            at("x%d" % k)
+                            act(column[k], (full(win), R("off2", 16 * k, 16 * k + 16)), ext=ext)
+                done.update(range(ka, kb))
+                while ns < len(SCANS) and all(lastq in done if k == "q" else k in ("b", "fin") or abs(k) in done for k in SCANS[ns]):
+                    fused = [k for k in SCANS[ns] if k not in ("q", "fin", "b") and k < 0]
+                    for k in SCANS[ns]:
+                        if k == "b":
+                            at("bc")
+                            move(column[k], brep(l, 0, 1))
+                        elif k in fused:
+                            at("w%d" % -k)
+                            for h in halves("w%d" % -k):
+                                tt(h(column[k]), (full(win), h(R("off2", -16 * k, 16 - 16 * k))),
+                                   h(result(ns - 1) if ns and k == fused[-1] else brep(l, 0, 1)), OP.max, ext=ext)
+                    at("S%d" % ns)
+                    for h in halves("S%d" % ns):
+                        scan(h(full("S%d" % ns)), h(full("d%d" % STEP[ns])), h(full("X%d" % ns)), OP.add, OP.max)
+                    ns += 1
+                acc = R("nk", 16 * (WIDE - kb + ka), 16 * WIDE)
+                if last:
+                    continue
+                at("n%d" % ka)
+                if not again and ZP:
+                    P = R("M0", 192 + 64 * nq, 192 + 64 * nq + 16 * (kb - ka))
+                    mm([const(P, "Z"), (P, full("iU"), mk), (P, full("idF"), slot("nk0", l, ka, kb))])
+                elif gi in ZA:
+                    act(R("mk", 16 * ka, 16 * kb), P, func=AF.Relu)
+                    P = R(bank, E + 16 * ka, E + 16 * kb)
+                    at("z%d" % ka)
+                    mm([(P, full("idF"), slot("nk0", l, ka, kb)), (P, full("iB"), R("mk", 16 * ka, 16 * kb))])
                 else:
-                    tt(R("o2f", 16 * ka, 16 * kb), P, slot("fI", l, ka, kb), OP.min)
-                    at("off2", gi)
-                    (move if gi >= QUICK else cp)(R("off2", 16 * ka, 16 * kb), R("o2f", 16 * ka, 16 * kb))
-                at("nk", gi)
-                if not last and gi == 0:
-                    tt(R("nk", 0, 16 * (kb - ka)), P, slot("nk0", l, ka, kb), OP.max)
-                    wide = kb - ka
-                elif not last:
-                    tt(P, P, slot("nk0", l, ka, kb), OP.max)
-                    at("acc", gi)
-                    for j in range(0, kb - ka, wide):
-                        n = 16 * min(wide, kb - ka - j)
-                        tt(R("nk", 0, n), R(P[0], P[1] + 16 * j, P[1] + 16 * j + n), R("nk", 0, n), OP.min)
-                for k in range(ka, kb):
-                    if k in where:
-                        at("again", ng)
-                        ng += 1
-                        act(where[k], (full(win), R("off2", 16 * k, 16 * k + 16)), ext=ext)
-            run, nw = brep(l, 0, 1), 0
-            for s, ((n, end, X, d, Sc), (ws, a)) in enumerate(zip(TILES[c], SCANS[c])):
-                for j, k in enumerate(ws or []):
-                    o = R(X, 0, n * E, n) if k == ws[-1] else lev("acc", j % 2)
-                    at("W", nw)
-                    nw += 1
-                    tt(o, (full(win), R("off2", 16 * k, 16 * k + 16)), run, OP.max, ext=ext)
-                    run = o
-                if ws == []:
-                    at("W" if s else None, nw)
-                    nw += 1
-                    move(R(X, 0, n * E, n), run)
-                at("scan", s)
-                scan(full(Sc), full(d), full(X), OP.add, OP.max)
-                run = R(Sc, n - 1, n * E, n)
-            at("end")
-            ts(lev(win, l, 16), run, 255.0, OP.min)
+                    tt(P if gi else acc, P, slot("nk0", l, ka, kb), OP.max)
+                if gi:
+                    at("a%d" % ka)
+                    tt(acc, P, acc, OP.min)
+            for h in halves("end")[::-1]:
+                at("end" if h is halves("end")[0] else "en")
+                ts(h(lev(win, l, 16)), h(result(len(SCANS) - 1)), 255.0, OP.min)
             at(None)
             if q == 0:
                 sends.append(send(lev("winA", l, 16), [((r + h) % N, lev("winB", l, 16 + h * V)) for h in (1, 2, 3)], "arrB"))
@@ -617,16 +679,15 @@ def plan(r, core, T, topo, g):
                 dma("S", pairs, [lev("winB", l, 16)], [], 65536)
             if last:
                 continue
-            nt = 0
+            wide = WIDE
             while wide > 1:
                 h = wide // 2
                 wide -= h
-                at("tree", nt)
-                nt += 1
+                at("t%d" % h)
                 tt(R("nk", 0, 16 * h), R("nk", 0, 16 * h), R("nk", 16 * wide, 16 * (wide + h)), OP.min)
-            at("tree", 2)
-            tt(part(cI, l), R("nk", 0, 16), homeN, OP.min)
-            at("tree", 3)
+            at("t0")
+            tt(part(cI, l), home if HOMEV else ej, R("nk", 0, 16), OP.min)
+            at("ne")
             if l < 2:
                 ts(neI, part(cI, l), HIGH + 4095, OP.bitwise_and)
             else:
@@ -634,45 +695,22 @@ def plan(r, core, T, topo, g):
                 tt(neI, ne2, cf2, OP.add)
             at("Y")
             tt(full("Y"), (neI, R("inv", 16 * l, 16 * l + 16)), lev("Zs", l), OP.min)
-            at("route", 0)
-            mm([(R("M0", 64 + a, 192, 16, 0, 16), R("Y", a, E, 16), R("Wd", 16, 144, 16)) for a in range(16)], each=True)
-            at("route", 1)
+            at("r")
+            mm([(R("M0", 64 + a, 192, 16, 0, 16), R("Y", a, E, 16), R("Wd", 16, 144, 16)) for a in range(16)], [8], each=True)
+            at("Yt")
             act(R("Yt", 0, 128, 1, 0, 16), R("M0", 64, 192, 1, 0, 16))
-            at("route", 2)
-            mm(([tj(l + 1)] if l < 2 else []) + [(ej, R("Yt", 0, 128, 1, 0, 16), R("idF", 0, 16, 1, 0, 16))])
+            at("ej")
+            if HOMEV and l < 2:
+                mm([tj(l + 1), const(ej2, "e%d" % q), (R("M0", 0, 32), R("Yt", 0, 128, 1, 0, 16), R("id2", 0, 32, 1, 0, 16))])
+            else:
+                mm(([tj(l + 1)] if l < 2 else []) + [(ej, R("Yt", 0, 128, 1, 0, 16), R("idF", 0, 16, 1, 0, 16))])
             at(None)
             if l == 2:
                 act(full("eout"), ej)
                 esend.append(send(full("eout"), [((r + 1) % N, full("ein"))], "arrE"))
-        if q == 0:
-            ts(tie, cI, 31 * TIE, OP.bitwise_and)
-            ts(ntk, tie, 0.0, OP.is_equal, BIG, OP.mult)
-            tt(Mv, tie, ntk, OP.add)
-            ts(lowa, nI, U - 1, OP.bitwise_and)
-            ts(l2, lowa, 2.0, OP.mult, 18.0 * U, OP.add)
-            tt(Ma, l2, nI, OP.subtract)
-            tt(Ma, Ma, Ms, OP.min)
-            tt(kI, Ma, Mv, OP.min)
-            ts(low, kI, U - 1, OP.bitwise_and)
-            ts(l2, low, 2.0, OP.mult, 18.0 * U, OP.add)
-            tt(mjI, l2, kI, OP.subtract)
-            ts(tjI, kI, 31 * TIE, OP.bitwise_and)
-            ts(full("tjb"), tjI, 8192.0, OP.add)
-            tt(tsel, cI, ntk, OP.add)
-            tt(selk, mjI, tsel, OP.min)
-            tt(Mv, nI, selk, OP.subtract)
-            for l in range(3):
-                n = R("lE", 0, 15)
-                eq, dk, kl = [R(nm, l * E, l * E + 240) for nm in ("eqb", "W0", "keyI")]
-                tt(eq, (part(selk, l), n), slot("nk0", l, 0, 15), OP.is_equal)
-                tt(dk, (part(Mv, l), n), eq, OP.mult)
-                o = R("Q%d" % (l % 2), 0, 240)
-                mm([(o, full("idF"), slot("nk0", l, 0, 15)), (o, full("idF"), dk)], [1])
-                act(slot("nk0", l, 0, 15), o)
-                (move if l else cp)(kl, slot("nk0", l, 0, 15) if l else o)
-                ts(slot("fI", l, 0, 15), kl, 4095, OP.bitwise_and)
-                (move if l else cp)(slot("off", l, 0, 15), slot("fI", l, 0, 15))
-    return tasks, queue, [extA, extB, extE]
+            if q == 0 and l in CHANGE:
+                change(CHANGE[l])
+    return tasks, queue, [extA, extB, extE], nload
 
 
 def depend(tasks):
@@ -696,220 +734,154 @@ def depend(tasks):
     return deps
 
 
-def schedule(tasks, deps):
+def edges(tasks, pre, v):
+    fg, fp, far, near, fl, fq = VARIANTS[v]
+    cost = [t["cost"] * (fp if t["eng"] == "P" else fq if t["eng"] == "G" else fg if t["ind"] else 1.0) for t in tasks]
+    gap = [[(j, 0.0 if j in t["free"] or (t["grp"] is not None and tasks[j]["grp"] == t["grp"]) else tasks[j]["lat"] * fl + (near if tasks[j]["eng"] == t["eng"] else far))
+            for j in d] for d, t in zip(pre, tasks)]
+    return cost, gap
+
+
+def replay(tasks, order, cost, gap):
+    free = {e: 0.0 for e in ENG}
+    fin = [0.0] * len(tasks)
+    for i in order:
+        e = tasks[i]["eng"]
+        s = free[e]
+        for j, x in gap[i]:
+            if fin[j] + x > s:
+                s = fin[j] + x
+        free[e] = fin[i] = s + cost[i]
+    return max(f + t["lat"] for f, t in zip(fin, tasks))
+
+
+def place(tasks, order, cost, gap, first):
+    slots = {e: [] for e in ENG}
+    fin = [0.0] * len(tasks)
+    for i in order:
+        s = max([first[i]] + [fin[j] + x for j, x in gap[i]])
+        sl = slots[tasks[i]["eng"]]
+        k = len(sl)
+        while k and sl[k - 1][1] > s:
+            k -= 1
+        while k < len(sl) and sl[k][0] < s + cost[i]:
+            s = max(s, sl[k][1])
+            k += 1
+        sl.insert(k, (s, s + cost[i]))
+        fin[i] = s + cost[i]
+    return fin
+
+
+def sorted_after(key, before):
+    key = list(key)
+    for i in range(len(key)):
+        for j, x in before[i]:
+            key[i] = max(key[i], key[j] + 1e-3)
+    return sorted(range(len(key)), key=lambda i: (key[i], i))
+
+
+def justify(tasks, pre, nload):
     n = len(tasks)
-    pre = [set(d) | set(t["ext"][2] if t["ext"] else []) for d, t in zip(deps, tasks)]
-    succ = [[] for _ in range(n)]
-    for i in range(n):
-        for j in pre[i]:
-            succ[j].append(i)
-    prio = [0.0] * n
-    for i in range(n - 1, -1, -1):
-        prio[i] = tasks[i]["cost"] + tasks[i]["lat"] + max([prio[k] + LAT for k in succ[i]] + [0.0])
-    best = None
     rng = np.random.default_rng(SEED)
+    models = [edges(tasks, pre, v) for v in range(len(VARIANTS))]
+    cost, gap = models[0]
+    back = [[] for _ in range(n)]
+    for i in range(n):
+        for j, x in gap[i]:
+            back[n - 1 - j].append((n - 1 - i, x))
+    rtasks, rcost = tasks[::-1], cost[::-1]
+    rfirst = [t["lat"] for t in rtasks]
+    tail = [0.0] * n
+    for i in range(n):
+        tail[i] = max([rfirst[i]] + [tail[j] + x for j, x in back[i]]) + rcost[i]
+    best = None
     for it in range(PASSES):
-        slack = float(rng.choice(np.array(SLACK)))
-        order, start = sweep(tasks, pre, succ, prio, False, slack)
-        end = sum(replay(tasks, pre, order, v) for v in range(len(VARIANTS)))
+        key = [-x for x in tail[::-1]]
+        if it % 4:
+            key = (np.array(key) + rng.normal(0.0, 40.0 * (it % 4) ** 2, n)).tolist()
+        for i in range(nload):
+            key[i] = -1e9 + i
+        fin = place(tasks, sorted_after(key, gap), cost, gap, [0.0] * n)
+        order = sorted_after([f - c for f, c in zip(fin, cost)], gap)
+        end = sum(replay(tasks, order, c, x) for c, x in models)
         if best is None or end < best[0]:
-            best = (end, order, start)
-        if it % 2:
-            start = best[2]
-        noise = rng.normal(0.0, float(rng.choice(np.array(NOISE))), n)
-        o2, s2 = sweep(tasks, succ, pre, [start[i] + tasks[i]["cost"] + noise[i] for i in range(n)], True, slack)
-        prio = [s2[i] + tasks[i]["cost"] for i in range(n)]
-    cur, order = best[0], best[1]
-    best = (cur, order)
-    pre = [list(p) for p in pre]
-    chain = None
-    for it in range(MOVES):
-        if chain is None or it % 8 == 0:
-            why = [None] * n
-            replay(tasks, pre, order, int(rng.integers(len(VARIANTS))), why)
-            chain, i = [], why[n - 1][2]
-            while why[i][0] is not None:
-                if why[i][1]:
-                    chain.append((i, why[i][0]))
-                i = why[i][0]
-        i, j = chain[int(rng.integers(len(chain)))]
-        a, b = order.index(j), order.index(i)
-        if rng.random() < 0.3:
-            e = tasks[i]["eng"]
-            back = [k for k in range(max(0, a - 12), a) if tasks[order[k]]["eng"] == e]
-            if back:
-                a = back[int(rng.integers(len(back)))]
-        mid = order[a:b]
-        need, front = set(pre[i]), []
-        for k in reversed(mid):
-            if k in need:
-                front.append(k)
-                need.update(pre[k])
-        if order[a] in need:
-            continue
-        fs = set(front)
-        cand = order[:a] + front[::-1] + [i] + [k for k in mid if k not in fs] + order[b + 1:]
-        end = sum(replay(tasks, pre, cand, v) for v in range(len(VARIANTS)))
-        if end < cur + HEAT * (1.0 - it / MOVES) * rng.exponential():
-            cur, order, chain = end, cand, None
-            if end < best[0]:
-                best = (end, cand)
+            best = (end, order, fin)
+        if it % 4 == 3:
+            fin = best[2]
+        tail = place(rtasks, sorted_after([-x for x in fin[::-1]], back), rcost, back, rfirst)
     return best[1]
 
 
-def replay(tasks, pre, order, v, why=None):
-    fg, fp, lat, fl = VARIANTS[v]
-    free = {e: 0.0 for e in "VAPGS"}
-    prev = {e: None for e in "VAPGS"}
-    fin = [0.0] * len(tasks)
-    for i in order:
-        t = tasks[i]
-        e = t["eng"]
-        s = free[e]
-        w = None
-        for j in pre[i]:
-            if fin[j] + lat > s:
-                s = fin[j] + lat
-                w = j
-        if why is not None:
-            why[i] = [prev[e], True, None] if w is None else [w, False, None]
-            prev[e] = i
-        s += t["cost"] * (fp if e == "P" else fg if t["ind"] else 1.0)
-        free[e] = s
-        fin[i] = s + t["lat"] * fl
-    end = max(fin)
-    if why is not None:
-        why[len(tasks) - 1][2] = fin.index(end)
-    return end
-
-
-def sweep(tasks, pre, succ, prio, back, slack):
+def first_order(tasks, pre, nload):
     n = len(tasks)
-    left = [len(p) for p in pre]
-    ready = {e: [] for e in "VAPGS"}
-    at = [tasks[i]["lat"] if back else 0.0 for i in range(n)]
-    for i in range(n):
-        if not left[i]:
-            ready[tasks[i]["eng"]].append(i)
-    free = {e: 0.0 for e in "VAPGS"}
-    order, start = [], [0.0] * n
-    while len(order) < n:
-        best = None
-        for e in "VAPGS":
-            if ready[e]:
-                t0 = max(free[e], min(at[i] for i in ready[e]))
-                if best is None or t0 < best[0]:
-                    best = (t0, e)
-        t0, e = best
-        i = max((k for k in ready[e] if at[k] <= t0 + slack), key=lambda k: (prio[k], -k))
-        t0 = max(t0, at[i])
-        ready[e].remove(i)
-        order.append(i)
-        start[i] = t0
-        free[e] = t0 + tasks[i]["cost"]
-        for k in succ[i]:
-            at[k] = max(at[k], free[e] + tasks[k if back else i]["lat"] + LAT)
-            left[k] -= 1
-            if not left[k]:
-                ready[tasks[k]["eng"]].append(k)
-    return order, start
+    named = {}
+    for i, t in enumerate(tasks):
+        if t["tag"]:
+            named.setdefault(t["tag"], []).append(i)
+    tied = [set(p) for p in pre]
+    free = [set(t["free"]) for t in tasks]
+    for before, names in zip(PREP, ISSUE):
+        chain = [i for x in before.split() for i in named[(0, x)]] + [i for lv in range(-1, 7) for x in names.split() for i in named.get((lv - (x[0] == "|") + (x[0] == "+"), x.strip("|+")), [])]
+        chain = [i for i in chain if tasks[i]["eng"] == ENG[ISSUE.index(names)]]
+        chain.sort(key=lambda i: tasks[i]["tag"][0] // 3)
+        for j, i in zip(chain, chain[1:]):
+            if j not in tied[i] and tasks[i]["tag"][0] // 3 == tasks[j]["tag"][0] // 3:
+                tied[i].add(j)
+                free[i].add(j)
+    perm, done = [], [False] * n
+    while len(perm) < n:
+        for i in range(n):
+            if not done[i] and all(done[j] for j in tied[i]):
+                done[i] = True
+                perm.append(i)
+    at = {i: k for k, i in enumerate(perm)}
+    ts = [dict(tasks[i], free=set(at[j] for j in free[i])) for i in perm]
+    return [perm[k] for k in justify(ts, [set(at[j] for j in tied[i]) for i in perm], nload)]
 
 
-def schedule(tasks, deps):
-    pre = [set(d) | set(t["ext"][2] if t["ext"] else []) for d, t in zip(deps, tasks)]
-    order = bydue(tasks, pre)
-    for span, stride, moves, heat in REFINE:
-        order = refine(tasks, pre, order, span, stride, moves, heat)
-    return order
-
-
-def bydue(tasks, pre):
-    n = len(tasks)
-    succ = [[] for _ in range(n)]
-    for i in range(n):
-        for j in pre[i]:
-            succ[j].append(i)
-    due = [0.0] * n
-    for i in range(n - 1, -1, -1):
-        t = tasks[i]
-        d = min([due[k] - t["cost"] - t["lat"] - LAT for k in succ[i]] + [1e9])
-        due[i] = d if t["due"] is None else min([t["due"]] + [due[k] - 1.0 for k in succ[i]])
-    todo = {e: sorted((i for i in range(n) if tasks[i]["eng"] == e), key=lambda i: (due[i], i)) for e in "VAPGS"}
-    left = [len(p) for p in pre]
-    at = [0.0] * n
-    free = {e: 0.0 for e in "VAPGS"}
-    order = []
-    while len(order) < n:
-        best = None
-        for e in "VAPGS":
-            if not todo[e]:
-                continue
-            m = todo[e][0]
-            pick = m if not left[m] else None
-            if left[m] or at[m] > free[e] + FIT:
-                room = at[m] + FIT if not left[m] else max(at[m], free[e]) + BLIND
-                fill = [k for k in todo[e] if not left[k] and tasks[k]["due"] is None and max(at[k], free[e]) + tasks[k]["cost"] <= room]
-                if fill:
-                    pick = fill[0]
-            if pick is not None:
-                s = max(free[e], at[pick])
-                if best is None or s < best[0]:
-                    best = (s, e, pick)
-        s, e, i = best
-        todo[e].remove(i)
-        order.append(i)
-        free[e] = s + tasks[i]["cost"]
-        for k in succ[i]:
-            at[k] = max(at[k], free[e] + tasks[i]["lat"] + LAT)
-            left[k] -= 1
-    return order
-
-
-def refine(tasks, pre, order, span, stride, moves, heat):
+def refine(tasks, pre, order, span, stride, moves, heat, soon=0.001, first=0, last=None):
     n = len(tasks)
     rng = np.random.default_rng(SEED)
-    eng = ["VAPGS".index(t["eng"]) for t in tasks]
-    hard = [[j for j in d if t["grp"] is None or tasks[j]["grp"] != t["grp"]] for d, t in zip(pre, tasks)]
-    cost = [[t["cost"] * (fp if t["eng"] == "P" else fg if t["ind"] else 1.0) for t in tasks] for fg, fp, lat, fl in VARIANTS]
-    late = [[t["lat"] * fl + lat for t in tasks] for fg, fp, lat, fl in VARIANTS]
-    eps = [0.3 if t["sem"] and t["eng"] == "G" else EPS if t["tag"] is None else EPS2 for t in tasks]
+    eng = [ENG.index(t["eng"]) for t in tasks]
+    models = [edges(tasks, pre, v) for v in range(len(VARIANTS))]
+    eps = [0.3 if t["lat"] and t["eng"] == "G" else 0.001 if t["tag"] and t["tag"][1][0] not in "RO" else soon for t in tasks]
     fin = [[0.0] * n for v in VARIANTS]
     free0 = [[0.0] * 5 for v in VARIANTS]
     order = list(order)
 
     def run(seq, keep=False):
         tot = 0.0
-        for f, c, la, fr, tl, te in zip(fin, cost, late, free0, tail, tend):
+        for f, (c, gp), fr, tl, te in zip(fin, models, free0, tail, tend):
             free = fr if keep else fr[:]
             end = 0.0
             for i in seq:
                 e = eng[i]
                 s = free[e]
-                for j in hard[i]:
-                    if f[j] > s:
-                        s = f[j]
+                for j, x in gp[i]:
+                    if f[j] + x > s:
+                        s = f[j] + x
                 s += c[i]
-                free[e] = s
-                s += la[i]
-                f[i] = s
+                free[e] = f[i] = s
                 tot += eps[i] * s
                 s += tl[i]
                 if s > end:
                     end = s
             tot += max([end] + [x + y for x, y in zip(free, te)])
         return tot
-    for a0 in range(0, max(n - span, 0) + stride, stride):
+    budget = moves
+    for a0 in range(0, max(n - span, 0) + stride, stride)[:last]:
+        moves = budget if a0 >= first * stride else 0
         seq = order[a0:a0 + span]
         m = len(seq)
-        tail, tend = [[0.0] * n for v in VARIANTS], [[0.0] * 5 for v in VARIANTS]
-        for c, la, tl, te in zip(cost, late, tail, tend):
+        tail, tend = [[t["lat"] for t in tasks] for v in VARIANTS], [[0.0] * 5 for v in VARIANTS]
+        for (c, gp), tl, te in zip(models, tail, tend):
             for i in order[:a0 + span - 1:-1]:
-                te[eng[i]] = c[i] + max(la[i] + tl[i], te[eng[i]])
-                for j in hard[i]:
-                    tl[j] = max(tl[j], te[eng[i]])
+                te[eng[i]] = c[i] + max(tl[i], te[eng[i]])
+                for j, x in gp[i]:
+                    tl[j] = max(tl[j], te[eng[i]] + x)
         cur = run(seq)
         best = (cur, seq)
-        pos, far, way, warm = rng.integers(m, size=moves).tolist(), rng.exponential(1.4, moves).tolist(), rng.random(moves).tolist(), rng.exponential(1.0, moves).tolist()
+        pos, far, way, warm = rng.integers(m, size=moves).tolist(), (rng.exponential(1.2, moves) * rng.choice(np.array([1, 1, 1, 5]), moves)).tolist(), rng.random(moves).tolist(), rng.exponential(1.0, moves).tolist()
         for it in range(moves):
             a = b = pos[it]
             i = seq[b]
@@ -942,14 +914,36 @@ def refine(tasks, pre, order, span, stride, moves, heat):
     return order
 
 
+def schedule(tasks, nload):
+    pre = [set(d) | set(t["ext"][1] if t["ext"] else []) for d, t in zip(depend(tasks), tasks)]
+    bank = {}
+    for i, t in enumerate(tasks):
+        t["free"] = set(t.get("after", [])) - pre[i]
+        pre[i] |= t["free"]
+        if t["eng"] == "P":
+            j = bank.get(t["w"][0][0])
+            if j is not None and j not in pre[i]:
+                pre[i].add(j)
+                t["free"].add(j)
+            bank[t["w"][0][0]] = i
+    return improve(tasks, pre, nload)
+
+
+def improve(tasks, pre, nload):
+    order = first_order(tasks, pre, nload)
+    for x in REFINE:
+        order = refine(tasks, pre, order, *x)
+    return order
+
+
 def rank_program(g, core, T, topo):
     r = T.rank_of(core)
     if r is None:
         return
-    tasks, queue, exts = plan(r, core, T, topo, g)
+    tasks, queue, exts, nload = plan(r, core, T, topo, g)
     deps = depend(tasks)
     if "all" not in ORDER:
-        ORDER["all"] = schedule(*[(t, depend(t)) for t in [plan(1, T.cores[1], T, topo, g)[0]]][0])
+        ORDER["all"] = schedule(plan(1, T.cores[1], T, topo, g)[0], nload)
     order = ORDER["all"]
     hard = [[j for j in d if t["grp"] is None or tasks[j]["grp"] != t["grp"]] for d, t in zip(deps, tasks)]
     needed = set(j for d in hard for j in d)
@@ -970,16 +964,16 @@ def rank_program(g, core, T, topo):
         for j in hard[i]:
             want[mark[j][0]] = max(want.get(mark[j][0], 0), mark[j][1])
         if t["ext"]:
-            want[t["ext"][0]] = t["ext"][1]
+            want.update(t["ext"][0])
         for s, v in want.items():
             if seen[e].get(s, 0) < v:
                 queue[e].wait_ge(T.sem[s], v)
                 seen[e][s] = v
-        ins = t["fn"]()
+        ins = t["fn"] and t["fn"]()
         if t["sem"] is None and i in mark:
             ins.then_inc(T.sem[mark[i][0]], 1)
     ends = {}
-    for s, v in list(mark.values()) + [(x[0], x[1]) for x in exts]:
+    for s, v in list(mark.values()) + [y for x in exts for y in x[0].items()]:
         ends[s] = max(ends.get(s, 0), v)
     for s, v in ends.items():
         if max(seen[e].get(s, 0) for e in seen) < v:

import numpy as np
from concourse.bass import DstId, RemoteDMATransfer
from concourse.mybir import AluOpType, ActivationFunctionType

N = 8
E = 256
V = 768
WIN = 16 + 4 * V
SL = 272
GROUPS = [[(0, 4, "V")], [(4, 6, "V"), (6, 8, "V")], [(8, 10, "Y"), (10, 12, "Y")], [(12, 14, "V"), (14, 15, "V"), (15, 16, "V")]]
SCANS = [[-7, 0, 1, 2, 3, 4], [-6, 5, 8, 9, 10, 11], [-15, 12, 13, 14, "fin"]]
QUICK = False
ISSUE = ["|ne c0 |Y c4 o0 c6 n0 c12 o4 e0 c14 e1 n4 o8 w7 a4 c15 n8 S0 a8 o12 w6 n12 S1' a12 S1 t2 w15' t1 w15 S2' S2 t0 en end",
         "g8 g10 s8 s10 |Yt x0 x1 x2 x3 x4 x5 x8 x9 x10 x11 x12 x13 x14",
         "v8' k0' k0'' v10' |r |r' k4' k4'' |ej k8 k8' k8'' +v10 +v8 k12 k12' k12'' h +k0 +k4",
         "dd f0 f4 e4 e2 f8 f12"]
PREP = ["R0 R1 R0' R0'' R2 R0''' R0'''' R1' R1'' R1''' R2' R1'''' R2'' O0 R2''' O0' R2'''' O0''", "R0 R1 R2 R0' R1' O0 R2'",
        "R0 R0' R0'' R1 R2 R1' R1'' R2' R2'' O0 O0' O0'' O0'''", ""]
WIDE = GROUPS[0][-1][1] - GROUPS[0][0][0]
YB = ["D0", "D1"]
IDV = 8
STEP = [min(j for j, y in enumerate(SCANS) if j == s or (len(x) == len(y) and "fin" not in x + y)) for s, x in enumerate(SCANS)]
WAYS = ["VGG", "VGG"]
HALVED = ["S1", "w15", "S2", "end"]
EQV = 1
CHANGE = {1: [0, 1], 2: [2]}
HAND = True
PROBE = 0
HOMEV = False
ZP = True
ZA = []
KCV = 7
BMG = 8
PB = ["P0", "P1"]
QB = [("D0", "D1"), ("Q0", "Q1")]
REP = 4
TIE = 16384
U = 32 * TIE
S = 128.0 * U
BIG = 32.0 * U
HIGH = 31 * U
MG = 1.5 * 2.0 ** 23 * 2 * U
M1 = 1.5 * 2.0 ** 23
MID = 1520
KC = {"mid": MID + 16.0, "M1": M1, "c0": 18.5 * U, "MG": MG, "nMG": -MG, "V": 17.75 * S, "A": 19.5 * S,
      }

SCRATCH = {}


def _b(name, cols, dtype, rows=128, where="sbuf"):
    SCRATCH[name] = (where, [rows, cols], dtype)


for _n, _c in (("winA", WIN), ("winB", WIN), ("pwb", V), ("bsb", V), ("bb", REP * V), ("cmp", 16 * E), ("Ab", 16 * E),
               ("dK", 128), ("dB", V), ("dS", E), ("rl", V), ("Zh", V), ("eqb", V), ("Jb", 128), ("Cb", E),
               ("WS", 144), ("iB", 128), ("inB", 128), ("iU", 128), ("Wg", 144),
               ("Bm", 2048), ("kb", 3 * SL), ("iS", 128), ("mk", 2 * E), ("qa", 2 * E), ("bo", 128), ("Jg", 128),
               ("Gd", 384), ("dlb", E), ("oneB", 512), ("kc", 128 * len(KC)), ("tjb", 48)):
    _b(_n, _c, "bfloat16")
for _n, _c in (("lo", V), ("cF", 2 * E), ("iH", 128)):
    _b(_n, _c, "float16")
for _n, _c in (("W", 3 * V), ("kp", 3 * SL), ("nk0", 3 * SL), ("nk", SL), ("o2f", SL), ("Y", E), ("Yt", 128),
               ("oneF", 128), ("idF", 128), ("inF", 128), ("id2", 32), ("iS2", 128), ("iN2", 128), ("iSF", 128), ("J0", 256), ("J1", 256),
               ("Wd", 144), ("col", 16), ("io8", 64), ("sm", 512), ("ein", 16), ("eout", 16), ("Zb", E), ("Zs", V)):
    _b(_n, _c, "float32")
for _n, _c in (("fdi", V), ("qi", V), ("nxi", 48), ("keyI", V), ("fI", 3 * SL), ("smi", 512), ("pci", 16)):
    _b(_n, _c, "int32")
for _n, _c in (("off", 3 * SL), ("off2", SL), ("nxu", 48), ("inv", 48), ("lP", 18), ("lE", 16)):
    _b(_n, _c, "uint16")
for _n in ("P0", "P1", "D0", "D1", "Q0", "Q1", "M0", "Mb"):
    _b(_n, 512, "float32", where="psum")
for _s, _c in enumerate(SCANS):
    for _n in "XdS":
        _b("%s%d" % (_n, _s), len(_c) * E, "bfloat16")

NDMA = 36
SEMAPHORES = ["cV", "cA", "cP", "cG", "arrA", "arrB", "arrE", "arrF"] + ["d%d" % i for i in range(NDMA)]
ENG_SEM = {"V": "cV", "A": "cA", "P": "cP", "G": "cG"}
ENG = "VAPGS"
OP = AluOpType
AF = ActivationFunctionType
CY = 0.83 * 1.2
PCY = 0.42 * 1.2
GC = 1.56
RATE = 85.0
PASSES = 60
REFINE = [(300, 1000, 12000, 30.0, 0.04, 0, 1), (200, 100, 7000, 30.0, 0.003)]
ORDER = {}
SEED = 1
VARIANTS = [(1.0, 1.05, 200.0, 230.0, 1.0, 1.15), (0.75, 1.1, 160.0, 160.0, 0.8, 1.3), (1.2, 1.0, 130.0, 150.0, 0.85, 1.15)]


def R(name, a, b, step=1, p0=0, p1=128):
    return (name, a, b, step, p0, p1)


def ncols(x):
    return len(range(x[1], x[2], x[3]))


def bits(x):
    if x[3] == 1:
        return ((1 << (x[2] - x[1])) - 1) << x[1]
    m = 0
    for j in range(x[1], x[2], x[3]):
        m |= 1 << j
    return m


def is2(x):
    return SCRATCH[x[0]][2] in ("bfloat16", "uint16", "float16")


def insb(x):
    return SCRATCH[x[0]][0] == "sbuf"


def plan(r, core, T, topo, g):
    tasks, tag, names = [], [None], set()
    queue = {"V": g.vector, "A": g.scalar, "P": g.tensor, "G": g, "S": g.sync}

    def ap(x):
        if len(x) == 2:
            return ap(x[0]).indirect(ap(x[1]))
        return T[x[0]][x[4]:x[5], x[1]:x[2]:x[3]]

    def flat(xs):
        out = []
        for x in xs:
            if isinstance(x, tuple):
                out.extend(list(x) if len(x) == 2 else [x])
        return out

    def add(eng, fn, reads, writes, cost, lat=0.0, sem=None, ext=None, grp=None):
        name = tag[0]
        while name and (name, eng) in names:
            name = (name[0], name[1] + "'")
        names.add((name, eng))
        tasks.append({"tag": name, "grp": grp, "eng": eng, "fn": fn, "r": flat(reads), "w": flat(writes), "cost": cost, "lat": lat, "sem": sem, "ext": ext,
                      "ind": any(isinstance(x, tuple) and len(x) == 2 for x in reads)})

    def vcost(out, ins, per):
        x = ins[0]
        if len(x) == 2:
            return 50 + ncols(out) * GC * CY
        if len(out) == 2:
            return 50 + ncols(x) * 3.8 * CY
        return 20 + max(64, ncols(out) * per) * CY

    def sc(s):
        return ap(s) if isinstance(s, tuple) else s

    def tt(out, a, b, op, ext=None):
        per = 2 if len(a) == 2 or (insb(a) and insb(b)) else 1
        add("V", lambda: g.vector.tensor_tensor(ap(out), ap(a), ap(b), op), [a, b], [out], vcost(out, [a], per), ext=ext)

    def ts(out, a, s1, op0, s2=None, op1=None, ext=None):
        per = 0.5 if is2(out) and is2(a) else 1
        if op1 is None:
            fn = lambda: g.vector.tensor_scalar(ap(out), ap(a), sc(s1), None, op0)
        else:
            fn = lambda: g.vector.tensor_scalar(ap(out), ap(a), sc(s1), sc(s2), op0, op1)
        add("V", fn, [a, s1, s2], [out], vcost(out, [a], per), ext=ext)

    def cp(out, a):
        per = 0.5 if len(out) > 2 and is2(out) and is2(a) else 1
        rd = [a] + ([out[1]] if len(out) == 2 else [])
        add("V", lambda: g.vector.tensor_copy(ap(out), ap(a)), rd, [out[0] if len(out) == 2 else out], vcost(out, [a], per))

    def ms(out, val):
        add("V", lambda: g.vector.memset(ap(out), val), [], [out], vcost(out, [out], 0.5 if is2(out) else 1))

    def scan(out, d0, d1, op0, op1):
        per = 0.5 if is2(out) and is2(d0) and is2(d1) else 1
        add("V", lambda: g.vector.tensor_tensor_scan(ap(out), ap(d0), ap(d1), 0.0, op0, op1), [d0, d1], [out], vcost(out, [d1], per))

    def act(out, a, func=AF.Identity, bias=0.0, scale=1.0, ext=None, more=0.0):
        cost = more + (65 + ncols(out) * GC * CY if len(a) == 2 else 40 + max(64, ncols(out)) * CY)
        add("A", lambda: g.scalar.activation(ap(out), ap(a), func, bias=sc(bias), scale=sc(scale)), [a, bias, scale], [out], cost, ext=ext)

    def mm(items, cuts=(), ext=None, more=False, each=False, hold=False):
        cuts = [0] + list(cuts) + [len(items)]
        grp = len(tasks)
        for p, p1 in zip(cuts, cuts[1:]):
            def fn(p=p, p1=p1):
                ins = None
                for i in range(p, p1):
                    o, l, x = items[i]
                    ins = g.tensor.matmul(ap(o), ap(l), ap(x), each or (i == 0 and not more), each or (i == len(items) - 1 and not hold))
                return ins
            its = items[p:p1]
            cost = sum(5 + max(min(64, ncols(l)), ncols(x)) * (1 if is2(x) else 4) * PCY for o, l, x in its)
            add("P", fn, [l for o, l, x in its] + [x for o, l, x in its], [o for o, l, x in items], cost, lat=50.0, ext=ext, grp=grp)

    def const(o, name):
        j = list(KC).index(name)
        return (o, R("kc", 128 * j, 128 * j + 128, 1, 0, 1), R("oneB", 0, ncols(o), 1, 0, 1))

    def move(out, a):
        add("G", lambda: g.affine_select(ap(out), ap(a), [[0, ncols(a)]], OP.is_equal, 0.0, 0, 0), [a], [out], 170 + 2 * ncols(out) * CY)

    def iota(out, pat, base, cm=0):
        if SCRATCH[out[0]][2] == "int32":
            fn = lambda: g.iota(ap(out), pat, base, cm)
        else:
            fn = lambda: g.iota(ap(out), pat, base, cm, allow_small_or_imprecise_dtypes=True)
        add("G", fn, [], [out], 130 + 2 * ncols(out) * CY)

    def sel(out, a, pat, base):
        add("G", lambda: g.affine_select(ap(out), ap(a), pat, OP.is_equal, 0.0, base, 1), [a], [out], 170 + 2 * ncols(out) * CY)

    nd = [0]

    def dsem():
        nd[0] += 1
        return "d%d" % (nd[0] - 1)

    def dma(eng, pairs, reads, writes, nbytes, ext=None):
        s = dsem()

        def fn():
            for o, i in pairs:
                queue[eng].dma_start(o(), i()).then_inc(T.sem[s], 16)
            return None
        add(eng, fn, reads, writes, 60.0 * len(pairs), lat=1500 + nbytes / 200.0, sem=(s, 16 * len(pairs)), ext=ext)

    def rot(eng, name, dst, rows, nbytes, cols=(None, None), ext=None):
        a, b = rows
        d = lambda p0, p1: (lambda: ap(dst[:4] + (p0, p1)))
        pairs = [(d(0, (N - r) * b), lambda: T[name][r * a:N * a, cols[0]:cols[1]])]
        if r:
            pairs.append((d((N - r) * b, N * b), lambda: T[name][0:r * a, cols[0]:cols[1]]))
        dma(eng, pairs, [], [dst], nbytes, ext)

    def send(src, dsts, rsem, cost=300.0, times=None, ext=None):
        s = dsem()
        far = [(T.cores[k], x) for k, x in dsts if topo.chip(T.cores[k]) != topo.chip(core)]
        near = [(T.cores[k], x) for k, x in dsts if topo.chip(T.cores[k]) == topo.chip(core)]
        out = topo.engines(core, T.cores[(r + 2) % N])
        sets = []
        if far:
            sets.append((far, out))
        if near:
            sets.append((near, [e for e in topo.engines(core, near[0][0]) if e not in out]))

        def fn():
            tr = []
            for ds, es in sets:
                ids = [DstId(rid=topo.addr(c)[0], pnc=topo.addr(c)[1]) for c, x in ds]
                tr.append(RemoteDMATransfer(dst_ids=ids, dma_engine_mask=sum(1 << e for e in es), remote_sem=T.sem[rsem],
                                            srcs=[ap(src)], dsts=[ap(x) for c, x in ds]))
            g.remote_dma_fused(tr, local_sem=T.sem[s])
            return None
        add("G", fn, [src], [], cost, lat=2000 + ncols(src) * 256 * (times or len(dsts)) / (RATE if far else 2 * RATE), sem=(s, sum(len(es) for ds, es in sets)), ext=ext)
        return len(tasks) - 1

    def landed(k):
        c = T.cores[k % N]
        out = topo.engines(c, T.cores[(k + 2) % N])
        return len(out) if topo.chip(c) != topo.chip(core) else len(topo.engines(c, core)) - len(out)

    three = sum(landed(r - h) for h in (1, 2, 3))
    used = {"sm": 0, "smi": 0}

    def sm(n=16, name="sm"):
        used[name] += n
        return R(name, used[name] - n, used[name])

    def smi(n=16):
        return sm(n, "smi")

    def part(x, l):
        return R(x[0], x[1] + 16 * l, x[1] + 16 * l + 16)

    def slot(name, l, k, k1=None):
        return R(name, l * SL + 16 * k, l * SL + 16 * (k + 1 if k1 is None else k1))

    def full(name):
        return R(name, 0, SCRATCH[name][1][1])

    def lev(name, l, o=0):
        return R(name, o + l * E, o + (l + 1) * E)

    rot("S", "t0", R("winA", 16, 16 + V), (16, 16), 196608)
    for l in range(3):
        c0, c1 = l * E, (l + 1) * E
        dma("A", [(lambda c0=c0, c1=c1: T.fdi[:, c0:c1], lambda c0=c0, c1=c1: T.fd[:, c0:c1]),
                  (lambda c0=c0, c1=c1: T.pwb[:, c0:c1], lambda c0=c0, c1=c1: T.pw[:, c0:c1])],
            [], [lev("fdi", l), lev("pwb", l)], 196608 * (l + 2))
    rot("S", "bs", full("bsb"), (16, 16), 2 * 196608)
    dma("S", [(lambda: T.qi[0:8, 256:512], lambda: T.cf[:, :]), (lambda: T.qi[0:8, 512:768], lambda: T.cw[:, :])], [], [R("qi", 256, 768)], 16384)
    rot("S", "nx", full("nxi"), (16, 16), 24576)
    rot("S", "dl", R("qi", 0, 256), (1, 3), 24576)
    nload = len(tasks)
    for i in range(1, nload):
        tasks[i]["after"] = [j for j in range(i) if tasks[j]["eng"] == tasks[i]["eng"]]
    def pair(k):
        c = T.cores[k % N]
        far = [(k + h) % N for h in (1, 2, 3) if topo.chip(T.cores[(k + h) % N]) != topo.chip(c)]
        two = [x for x in far if sum(topo.chip(T.cores[y]) == topo.chip(T.cores[x]) for y in far) == 2]
        return sorted(two, key=lambda x: topo.die(T.cores[x]) != topo.die(c)) if len(far) == 3 and HAND else []

    block = lambda k, src: R("winA", 16 + (k - src) % N * V, 16 + ((k - src) % N + 1) * V)
    readers = [(r + h) % N for h in (1, 2, 3)]
    if pair(r):
        s0 = send(block(r, r), [(pair(r)[0], block(pair(r)[0], r))], "arrF", 1300.0)
        s1 = send(block(r, r), [(k, block(k, r)) for k in readers if k not in pair(r)], "arrA", 300.0, 2)
        tasks[s1]["after"] = [s0]
    else:
        s0 = send(block(r, r), [(k, block(k, r)) for k in readers], "arrA", 1300.0)
        add("G", None, [], [], 0.0)
    mine = [k for k in range(N) if pair(k)[:1] == [r]]
    extF = ({"arrF": sum(landed(k) for k in mine)}, [s0])
    if mine:
        s2 = send(block(r, mine[0]), [(pair(mine[0])[1], block(pair(mine[0])[1], mine[0]))], "arrA", 300.0, ext=extF)
    else:
        add("G", None, [], [], 0.0)
    extA = (dict(extF[0], arrA=sum(0 if pair(r - h)[:1] == [r] else landed(pair(r - h)[0] if r in pair(r - h) else r - h) for h in (1, 2, 3))), [s0, s0 + 1, s0 + 2])

    col = lambda j: R("col", j, j + 1)
    pf, pg, par1, par0, kc, p16x, par1n, par0n = [col(j) for j in range(8)]
    iota(R("pci", 0, 1), [[0, 1]], 0, 1)
    ts(R("pci", 4, 5), R("pci", 0, 1), 15, OP.bitwise_and)
    ts(R("pci", 5, 6), R("pci", 0, 1), 4, OP.logical_shift_right)
    ts(R("pci", 6, 7), R("pci", 0, 1), 4, OP.logical_shift_right, 1, OP.bitwise_and)
    cp(R("col", 0, 3), R("pci", 4, 7))
    ts(par0, par1, -1.0, OP.mult, 1.0, OP.add)
    ts(kc, pf, float(TIE), OP.mult, float(TIE + U), OP.add)
    ts(p16x, pf, 16.0, OP.mult)
    ms(full("oneF"), 1.0)
    ms(full("oneB"), 1.0)
    for j, nm in enumerate(KC):
        if j < KCV:
            ms(R("kc", 128 * j, 128 * j + 128, 1, 0, 1), KC[nm])
        else:
            act(R("kc", 128 * j, 128 * j + 128, 1, 0, 1), R("oneF", 0, 128, 1, 0, 1), scale=KC[nm])
    sel(full("idF"), full("oneF"), [[-1, 128]], 0)
    act(full("iB"), full("idF"))
    scaled = (("iH", 511 / 1024), ("iS", -S / U), ("dK", kc), ("inB", -1.0), ("iS2", -2 * S / U), ("iN2", -2.0), ("iSF", -S / U), ("inF", -1.0), ("iU", float(U)))
    for nm, val in scaled[:IDV]:
        ts(full(nm), full("iB"), val, OP.mult)
    for nm, val in scaled[IDV:]:
        act(full(nm), full("idF"), scale=val, func=AF.Silu if nm == "iU" else AF.Identity, more=1300.0 * (nm == "iU"))
    for nm, c in (("J0", par0), ("J1", par1)):
        act(R(nm, 0, 128), full("idF"), scale=c)
        act(R(nm, 128, 256), full("idF"), scale=c)
    iota(R("io8", 0, 18), [[1, 18]], 0)
    ms(full("Wd"), 0.0)
    ts(R("Wd", 16, 144, 16), R("io8", 0, 8), pg, OP.is_equal)
    act(full("WS"), full("Wd"), scale=-S)
    ms(R("Wg", 0, 144, 1, 0, 32), 0.0)
    cut = N - r if r else N // 2
    sel(R("Wg", 16, 16 + 16 * cut, 16, 0, 8), R("oneB", 0, cut, 1, 0, 8), [[-1, cut]], -r)
    sel(R("Wg", 16 + 16 * cut, 144, 16, 0, 8), R("oneB", 0, N - cut, 1, 0, 8), [[-1, N - cut]], -((cut + r) % N))
    sel(R("Gd", 0, 384, 1, 0, 24), R("oneB", 0, 384, 1, 0, 24), [[-1, 3], [-3, 8], [0, 16]], 0)
    sel(R("Jb", 0, 128, 1, 0, 16), R("oneB", 0, 128, 1, 0, 16), [[0, 8], [-1, 16]], 0)
    iota(R("Cb", 0, E, 1, 0, 16), [[1, 16], [0, 16]], 1)
    sel(R("Cb", 0, E, 1, 0, 16), R("Cb", 0, E, 1, 0, 16), [[0, 16], [-1, 16]], 0)
    mm([(R("D1", 0, E), R("Jb", 0, 128, 1, 0, 16), R("Cb", 0, E, 1, 0, 16))])
    act(full("Zb"), R("D1", 0, E), scale=BIG)
    iota(R("io8", 20, 35), [[1, 15]], E)
    iota(R("io8", 35, 37), [[2 * E - 1, 2]], 15)
    ts(R("lP", 0, 17), R("io8", 20, 37), p16x, OP.add)
    ts(full("lE"), R("oneF", 0, 16), pf, OP.mult)
    cf2 = sm()
    iota(R("io8", 40, 56), [[16, 16]], 16 + V + 2 * E)
    ts(cf2, R("io8", 40, 56), pf, OP.add)
    ms(full("dS"), 0.0)
    ms(R("dS", 0, E, 16), BIG)
    for s, cols in enumerate(SCANS):
        n, d = len(cols), "d%d" % s
        for j, k in enumerate(cols):
            if k == "fin":
                ms(R("X%d" % s, j, n * E, n), 0.0)
            elif STEP[s] == s:
                ms(R(d, j, n * E, n), 0.0 if j else -512.0)
    anyq = any(x[2] == "Q" for parts in GROUPS for x in parts)
    for a in range(0, BMG * anyq, 4):
        sel(R("Bm", 128 * a, 128 * a + 512), full("oneB"), [[-1, 4], [-16, 8], [0, 16]], -a)
    if BMG < 16 and anyq:
        sel(R("Jg", 0, 128, 1, 0, 8), R("oneB", 0, 128, 1, 0, 8), [[-1, 8], [0, 16]], 0)
        mm([(R("D1", 0, 128), R("Jg", 0, 128, 1, 0, 8), R("Jg", 0, 128, 1, 0, 8))])
        act(full("bo"), R("D1", 0, 128))
        am = sm()
        ts(am, R("io8", 0, 16), pf, OP.is_equal)
        for a in range(BMG, 16):
            ts(R("Bm", 128 * a, 128 * a + 128), full("bo"), R("sm", am[1] + a, am[1] + a + 1), OP.mult)
    ms(R("winA", 0, 16), 0.0)
    ms(R("winB", 0, 16), 0.0)

    def Lm(name, a, p1=128):
        return R(name, 16 - a, 144 - a, 1, 0, p1)

    def bcalc(l, copy=move):
        o = R("Mb", 0, E)
        mm([(o, full("iH"), lev("bsb", l)), (o, full("iH"), lev("winA", l, 16)), const(o, "M1")])
        act(brep(l, 0, 1), o, bias=-M1)
        for j in range(1, REP):
            copy(brep(l, j, j + 1), brep(l, 0, 1))

    def brep(l, j, j1, h=None):
        return R("bb", (l * REP + j) * E + (h or 0), (l * REP + j1) * E, 1 if h is None else 2)

    Ms, ml, tjI, mjI = sm(48), sm(48), smi(48), smi(48)

    def rows(l, kb):
        W = lambda a, b: R("W", l * V + a, l * V + b)
        x, tb = R(kb, 0, E), R(kb, E, 2 * E)
        ts(lev("lo", l), lev("fdi", l), -float(MID), OP.add)
        mm([(x, full("iB"), lev("pwb", l)), (x, full("iS"), lev("lo", l))])
        act(lev("rl", l), x, func=AF.Relu, scale=4096.0, bias=-4096.0 * (128 * MID + 127))
        mm([(x, full("iB"), lev("lo", l)), (x, full("iU"), lev("pwb", l)), (x, full("dK"), R("oneB", 0, E)), const(x, "mid"),
            (x, full("iS"), lev("rl", l))], [4])
        add("V", lambda: g.vector.transpose(ap(tb), ap(x)), [x], [tb], 20 + E * CY)
        scan(W(0, E), full("dS"), tb, OP.add, OP.min)
        tt(W(E, 2 * E - 1), W(0, E - 1), R(kb, E + 1, 2 * E), OP.max)
        scan(W(2 * E, 3 * E), full("dS"), W(E, 2 * E), OP.add, OP.min)
        act(slot("kp", l, 0, 17), (W(0, V), R("lP", 0, 17)))

    def onto(l, nb):
        def fix(nm, bank, n):
            return [(R(bank, x1, n, 2), R(nm + str(x1), (16 * (x1 + r - g0)) % 128, (16 * (x1 + r - g0)) % 128 + 128),
                     R("kp", l * SL + g0, l * SL + n, 2)) for x1 in (0, 1) for g0 in (0, 1)]
        mm(fix("J", nb, SL), [1, 2, 3])
        feeders(l, nb, "kp", 16, WAYS[0][l])
        act(part(Ms, l), R(nb, E, SL))
        o = R(nb, 0, E)
        mm([const(o, "c0"), (o, full("iN2"), slot("kp", l, 0, 16)), const(o, "MG"), const(o, "nMG"), (o, full("idF"), slot("kp", l, 0, 16))], [2, 4])
        act(slot("nk0", l, 0, 16), o)
        move(part(mjI, l), slot("nk0", l, 15))
        if l != 1:
            two = lambda x: R(x[0], x[1] + 16 * (l > 0), x[1] + 16 * (l + 1))
            ts(two(tjI), two(mjI), 31 * TIE, OP.bitwise_and)
            ts(two(full("tjb")), two(tjI), 4096.0, OP.add)
            tt(two(ml), two(mjI), two(tjI), OP.subtract)

    def feeders(l, nb, keys, n, way):
        o, kl, lo = R(nb, 0, 240), R("keyI", l * E, l * E + 240), slot("fI", l, 0, 15)
        if way == "V":
            cp(kl, o)
        act(slot(keys, l, 0, n), R(nb, 0, 16 * n))
        if way == "G":
            move(kl, slot(keys, l, 0, 15))
        ts(lo, kl, 4095, OP.bitwise_and)
        (cp if way == "V" else move)(slot("off", l, 0, 15), lo)

    def inverse(l):
        nxl = R("nxu", 16 * l, 16 * l + 16)
        add("A", lambda: g.scalar.activation(ap((lev("Zs", l), nxl)), ap(full("Zb")), AF.Silu), [full("Zb"), nxl, full("iU")], [lev("Zs", l)],
            65 + E * 3.8 * CY)
        move(lev("Zh", l), lev("Zs", l))
        mm([(R("Mb", 0, 16), Lm("WS", a), R("Zh", l * E + a, (l + 1) * E, 16)) for a in range(16)])
        ts(R("inv", 16 * l, 16 * l + 16), R("Mb", 0, 16), -1.0 / (BIG * S), OP.mult, -1.0, OP.add)

    ms(R("W", 2 * E - 1, 3 * V, V), 0.0)
    for l, bank in enumerate(("P0", "P1", "Q0")):
        tag[0] = (0, "R%d" % l)
        rows(l, bank)
    for l, bank in enumerate(("D0", "Q1", "Q0")):
        tag[0] = (0, "O%d" % l)
        onto(l, bank)
    tag[0] = None
    bcalc(0, cp)
    for j in range(PROBE):
        add("V", lambda: g.vector.memset(ap(full("cmp")), 0.0), [slot("off", 0, 0, 15), brep(0, 0, 4), R("W", 0, 3 * V)], [full("cmp")], 2060.0)
    ts(R("cF", 0, E, 1, 0, 8), R("qi", 256, 512, 1, 0, 8), -float(MID), OP.add)
    move(R("cF", E, 2 * E, 1, 0, 8), R("qi", 512, 768, 1, 0, 8))
    mm([(R("M0", 32, 64), Lm("Wg", a, 8), R("cF", a, 2 * E, 16, 0, 8)) for a in range(16)], [8])
    e0, t1, t2, t3 = sm(), sm(), sm(), sm()
    act(t3, R("M0", 32, 48), func=AF.Relu, scale=-1.0, bias=-float(MID))
    act(t1, t3, scale=18.0 * U + 16 + MID)
    act(t2, R("M0", 48, 64), scale=-float(U), bias=17.0 * U + 16 + MID)
    tt(t1, t1, t2, OP.max)
    tt(e0, R("M0", 32, 48), t1, OP.add)
    move(R("dlb", 0, E, 1, 0, 24), R("qi", 0, E, 1, 0, 24))
    move(full("nxu"), full("nxi"))
    for l in range(3):
        mm([(R("Mb", 0, E), R("Gd", 128 * l, 128 * l + 128, 1, 0, 24), R("dlb", 0, E, 1, 0, 24))])
        act(lev("dB", l), R("Mb", 0, E))
        inverse(l)

    for t in tasks[s0 + 3:]:
        if t["eng"] == "G" and t["w"][0][0] not in ("pci", "idF", "io8", "Cb", "Jb"):
            t["after"] = [s0]
    early = [i for i, t in enumerate(tasks) if t["eng"] == "G" and t["w"] and t["w"][0][0] in ("io8", "Cb", "Jb", "Wg", "cF", "nxu", "Gd", "dlb")]
    tasks.append(tasks[s0 + 2])
    tasks[s0 + 2] = dict(tasks[s0 + 2], fn=None, r=[], sem=None, ext=None, cost=0.0, lat=0.0)
    tasks[-1]["after"] = early
    extA[1][2] = len(tasks) - 1
    dma("S", [(lambda: T.winB[:, 16:16 + V], lambda: T.pwb[:, :])], [full("pwb")], [R("winB", 16, 16 + V)], 2 * 196608, extA)
    for l in (1, 2):
        bcalc(l)
    ej, ej2, home = R("M0", 0, 16), R("M0", 16, 32), sm()
    if HOMEV:
        sel(R("id2", 0, 32, 1, 0, 16), R("oneF", 0, 32, 1, 0, 16), [[0, 2], [-1, 16]], 0)
    neI, ne2, eI = smi(), smi(), smi()
    nI, cI, tie, lowa, kI, low = [smi(48) for _ in range(6)]
    ntk, Mv, Ma, l2, tsel, selk = [sm(48) for _ in range(6)]
    sends = []
    extB = ({"arrB": 3 * three}, sends)
    esend = []
    extE = ({"arrE": landed(r - 1)}, esend)
    tj = lambda l: (ej, full("iB"), part(full("tjb"), l))
    column = {k: R("X%d" % s, j, len(cols) * E, len(cols)) for s, cols in enumerate(SCANS) for j, k in enumerate(cols)}

    both = [lambda x: (x[0], x[1], x[1] + ncols(x) // 2 * x[3]) + x[3:], lambda x: (x[0], x[1] + ncols(x) // 2 * x[3], x[2]) + x[3:]]
    whole = [lambda x: x]

    def halves(name):
        return both if name in HALVED else whole

    def result(s, h=None):
        n = len(SCANS[s])
        return R("S%d" % s, n - 1 + n * (h or 0), n * E, n if h is None else 2 * n)
    lastq = ([0] + [x[1] - 1 for parts in GROUPS for x in parts if x[2] == "Q"])[-1]

    def change(levels):
        w = lambda x: R(x[0], x[1] + 16 * levels[0], x[1] + 16 * levels[-1] + 16)
        ts(w(tie), w(cI), 31 * TIE, OP.bitwise_and)
        ts(w(ntk), w(tie), 0.0, OP.is_equal, BIG, OP.mult)
        tt(w(Mv), w(tie), w(ntk), OP.add)
        ts(w(lowa), w(nI), U - 1, OP.bitwise_and)
        ts(w(l2), w(lowa), 2.0, OP.mult, 18.0 * U, OP.add)
        tt(w(Ma), w(l2), w(nI), OP.subtract)
        tt(w(Ma), w(Ma), w(Ms), OP.min)
        tt(w(kI), w(Ma), w(Mv), OP.min)
        ts(w(low), w(kI), U - 1, OP.bitwise_and)
        ts(w(l2), w(low), 2.0, OP.mult, 18.0 * U, OP.add)
        tt(w(mjI), w(l2), w(kI), OP.subtract)
        ts(w(tjI), w(kI), 31 * TIE, OP.bitwise_and)
        ts(w(full("tjb")), w(tjI), 8192.0, OP.add)
        tt(w(ml), w(mjI), w(tjI), OP.subtract)
        tt(w(tsel), w(cI), w(ntk), OP.add)
        tt(w(selk), w(mjI), w(tsel), OP.min)
        tt(w(Mv), w(nI), w(selk), OP.subtract)
        for l in levels:
            n = R("lE", 0, 15)
            eq, dk = [R(nm, l * E, l * E + 240) for nm in ("eqb", "W")]
            o = R("Q%d" % (l % 2), 0, 240)
            if l < EQV:
                tt(eq, (part(selk, l), n), slot("nk0", l, 0, 15), OP.is_equal)
            else:
                act(dk, (part(selk, l), n))
                mm([(o, full("idF"), slot("nk0", l, 0, 15)), (o, full("inF"), dk)], [1])
                act(eq, o, func=AF.Abs)
                act(eq, eq, func=AF.Relu, scale=-1.0, bias=1.0)
            tt(dk, (part(Mv, l), n), eq, OP.mult)
            mm([(o, full("idF"), slot("nk0", l, 0, 15)), (o, full("idF"), dk)], [1])
            feeders(l, o[0], "nk0", 15, WAYS[1][l])

    for q in range(2):
        win = "winA" if q == 0 else "winB"
        ext = extA if q == 0 else extB
        for l in range(3):
            last = q == 1 and l == 2
            k0 = 15
            came = lambda o: (o, R("Yt", 0, 128, 1, 0, 16), R("idF", 0, 16, 1, 0, 16)) if l else (o, full("idF"), full("ein") if q else e0)
            if l == 0:
                mm([tj(0), came(ej)], ext=extE if q else None)
            def at(name, lv=3 * q + l):
                tag[0] = name and (lv, name)
            at("e0")
            tt(part(nI, l), ej, part(mjI, l), OP.min)
            at("e1")
            ts(slot("fI", l, k0), part(nI, l), 4095, OP.bitwise_and)
            at("e2")
            (cp if QUICK else move)(slot("off", l, k0), slot("fI", l, k0))
            at("e4")
            move(slot("nk0", l, k0), part(nI, l))
            if not last:
                at("h")
                if HOMEV:
                    tt(home, R("M0", 16, 32), part(ml, l), OP.max)
                else:
                    mm([tj(l), came(ej), (ej, full("inF"), slot("nk0", l, k0)), (ej, full("idF"), part(ml, l))])
            at("dd")
            move(R("d%d" % (len(SCANS) - 1), len(SCANS[-1]) - 1, len(SCANS[-1]) * E, len(SCANS[-1])), lev("dB", l))
            nq, ny, ns, done = 0, 0, 0, set()
            for gi, parts in enumerate(GROUPS):
                ka, kb = parts[0][0], parts[-1][1]
                bank = PB[gi % 2]
                head = []
                for k, k1, who in parts:
                    run = [x for x in parts if (x[2] == "V") == (who == "V")]
                    if k == run[0][0]:
                        x = R(bank, 16 * k, 16 * run[-1][1])
                        head += [const(x, "V" if who == "V" else "A"), (x, full("iSF" if who == "V" else "iS2"), slot("nk0", l, k, run[-1][1]))]
                    if who == "V":
                        at("c%d" % k)
                        tt(R("cmp", k * E, k1 * E), (full(win), slot("off", l, k, k1)), brep(l, 0, k1 - k), OP.is_gt, ext=ext)
                        continue
                    for j in range(k, k1, 2):
                        j1 = min(j + 2, k1)
                        at("g%d" % j)
                        act(R("Ab", j * E, j1 * E), (full(win), slot("off", l, j, j1)), ext=ext)
                        bk = R(YB[ny % len(YB)], 0, (j1 - j) * E)
                        ny += 1
                        at("v%d" % j)
                        mm([(bk, full("inB"), brep(l, 0, j1 - j)), (bk, full("iB"), R("Ab", j * E, j1 * E))], [1])
                        at("s%d" % j)
                        act(R("cmp", j * E, j1 * E), bk, func=AF.Sign, bias=-0.5)
                at("k%d" % ka)
                P = R(bank, 16 * ka, 16 * kb)
                order = list(range(0, 16, 2)) + list(range(1, 16, 2))
                it = [(P, Lm("WS", a), R("cmp", ka * E + a, kb * E, 16)) for a in order]
                mm(head + it, [len(head), len(head) + 8])
                again = [k for k, k1, who in parts if who != "Q"]
                for k, k1, who in parts:
                    if who == "Q":
                        mk = R("mk", 16 * k, 16 * k1)
                        at("m%d" % k)
                        ts(mk, R(bank, 16 * k, 16 * k1), 0.0, OP.is_lt, -512.0, OP.mult)
                        for h in (0, 1):
                            at("B%d" % k + "ab"[h])
                            mm([(R(QB[nq][h], 0, (k1 - k) * 128), full("iB"), R("Ab", k * E + h, k1 * E, 2))]
                               + [(R(QB[nq][h], a // 2, (k1 - k) * 128, 8), R("Bm", 128 * a, 128 * a + 128), mk) for a in range(h, 16, 2)], [1])
                            for j in range(k1 - k):
                                x, run = R(QB[nq][h], 128 * j, 128 * j + 128), R("qa", 128 * h, 128 * h + 128)
                                c = column["q"]
                                o = R(c[0], c[1] + h * c[3], c[2], 2 * c[3]) if k + j == lastq else run
                                at("q%d" % (k + j) + "ab"[h])
                                tt(o, x, run if nq or j else result(0, h) if "b" in column else brep(l, 0, 1, h), OP.max)
                        nq += 1
                if again:
                    kr = again[0]
                    at("o%d" % ka)
                    tt(R("o2f", 16 * kr, 16 * kb), R(bank, 16 * kr, 16 * kb), slot("fI", l, kr, kb), OP.min)
                    at("f%d" % ka)
                    move(R("off2", 16 * kr, 16 * kb), R("o2f", 16 * kr, 16 * kb))
                    for k in range(kr, kb):
                        if k in column:
                            at("x%d" % k)
                            act(column[k], (full(win), R("off2", 16 * k, 16 * k + 16)), ext=ext)
                done.update(range(ka, kb))
                while ns < len(SCANS) and all(lastq in done if k == "q" else k in ("b", "fin") or abs(k) in done for k in SCANS[ns]):
                    fused = [k for k in SCANS[ns] if k not in ("q", "fin", "b") and k < 0]
                    for k in SCANS[ns]:
                        if k == "b":
                            at("bc")
                            move(column[k], brep(l, 0, 1))
                        elif k in fused:
                            at("w%d" % -k)
                            for h in halves("w%d" % -k):
                                tt(h(column[k]), (full(win), h(R("off2", -16 * k, 16 - 16 * k))),
                                   h(result(ns - 1) if ns and k == fused[-1] else brep(l, 0, 1)), OP.max, ext=ext)
                    at("S%d" % ns)
                    for h in halves("S%d" % ns):
                        scan(h(full("S%d" % ns)), h(full("d%d" % STEP[ns])), h(full("X%d" % ns)), OP.add, OP.max)
                    ns += 1
                acc = R("nk", 16 * (WIDE - kb + ka), 16 * WIDE)
                if last:
                    continue
                at("n%d" % ka)
                if not again and ZP:
                    P = R("M0", 192 + 64 * nq, 192 + 64 * nq + 16 * (kb - ka))
                    mm([const(P, "Z"), (P, full("iU"), mk), (P, full("idF"), slot("nk0", l, ka, kb))])
                elif gi in ZA:
                    act(R("mk", 16 * ka, 16 * kb), P, func=AF.Relu)
                    P = R(bank, E + 16 * ka, E + 16 * kb)
                    at("z%d" % ka)
                    mm([(P, full("idF"), slot("nk0", l, ka, kb)), (P, full("iB"), R("mk", 16 * ka, 16 * kb))])
                else:
                    tt(P if gi else acc, P, slot("nk0", l, ka, kb), OP.max)
                if gi:
                    at("a%d" % ka)
                    tt(acc, P, acc, OP.min)
            for h in halves("end")[::-1]:
                at("end" if h is halves("end")[0] else "en")
                ts(h(lev(win, l, 16)), h(result(len(SCANS) - 1)), 255.0, OP.min)
            at(None)
            if q == 0:
                sends.append(send(lev("winA", l, 16), [((r + h) % N, lev("winB", l, 16 + h * V)) for h in (1, 2, 3)], "arrB"))
                bcalc(l)
            else:
                y = lambda p0, p1, l=l: (lambda: T.yt[p0:p1, l * E:(l + 1) * E])
                w = lambda p0, p1, l=l: (lambda: T.winB[p0:p1, 16 + l * E:16 + (l + 1) * E])
                pairs = [(y(16 * r, 128), w(0, 128 - 16 * r))] + ([(y(0, 16 * r), w(128 - 16 * r, 128))] if r else [])
                dma("S", pairs, [lev("winB", l, 16)], [], 65536)
            if last:
                continue
            wide = WIDE
            while wide > 1:
                h = wide // 2
                wide -= h
                at("t%d" % h)
                tt(R("nk", 0, 16 * h), R("nk", 0, 16 * h), R("nk", 16 * wide, 16 * (wide + h)), OP.min)
            at("t0")
            tt(part(cI, l), home if HOMEV else ej, R("nk", 0, 16), OP.min)
            at("ne")
            if l < 2:
                ts(neI, part(cI, l), HIGH + 4095, OP.bitwise_and)
            else:
                ts(ne2, part(cI, l), HIGH, OP.bitwise_and)
                tt(neI, ne2, cf2, OP.add)
            at("Y")
            tt(full("Y"), (neI, R("inv", 16 * l, 16 * l + 16)), lev("Zs", l), OP.min)
            at("r")
            mm([(R("M0", 64 + a, 192, 16, 0, 16), R("Y", a, E, 16), R("Wd", 16, 144, 16)) for a in range(16)], [8], each=True)
            at("Yt")
            act(R("Yt", 0, 128, 1, 0, 16), R("M0", 64, 192, 1, 0, 16))
            at("ej")
            if HOMEV and l < 2:
                mm([tj(l + 1), const(ej2, "e%d" % q), (R("M0", 0, 32), R("Yt", 0, 128, 1, 0, 16), R("id2", 0, 32, 1, 0, 16))])
            else:
                mm(([tj(l + 1)] if l < 2 else []) + [(ej, R("Yt", 0, 128, 1, 0, 16), R("idF", 0, 16, 1, 0, 16))])
            at(None)
            if l == 2:
                act(full("eout"), ej)
                esend.append(send(full("eout"), [((r + 1) % N, full("ein"))], "arrE"))
            if q == 0 and l in CHANGE:
                change(CHANGE[l])
    return tasks, queue, [extA, extB, extE], nload


def depend(tasks):
    hist = {}
    deps = []
    for i, t in enumerate(tasks):
        d = set()
        acc = [(x[0], bits(x), False) for x in t["r"]] + [(x[0], bits(x), True) for x in t["w"]]
        for name, m, wr in acc:
            ps = SCRATCH[name][0] == "psum"
            for j, m2, wr2 in hist.get(name, []):
                if j != i and ((ps and tasks[j]["eng"] != t["eng"]) or ((m & m2) and (wr or wr2))):
                    d.add(j)
        for name, m, wr in acc:
            h = hist.setdefault(name, [])
            if wr:
                ps = SCRATCH[name][0] == "psum"
                h[:] = [(j, m2 & ~m, w2) for j, m2, w2 in h if j == i or ((m2 & ~m) and not (ps and tasks[j]["eng"] != t["eng"]))]
            h.append((i, m, wr))
        deps.append(d)
    return deps


def edges(tasks, pre, v):
    fg, fp, far, near, fl, fq = VARIANTS[v]
    cost = [t["cost"] * (fp if t["eng"] == "P" else fq if t["eng"] == "G" else fg if t["ind"] else 1.0) for t in tasks]
    gap = [[(j, 0.0 if j in t["free"] or (t["grp"] is not None and tasks[j]["grp"] == t["grp"]) else tasks[j]["lat"] * fl + (near if tasks[j]["eng"] == t["eng"] else far))
            for j in d] for d, t in zip(pre, tasks)]
    return cost, gap


def replay(tasks, order, cost, gap):
    free = {e: 0.0 for e in ENG}
    fin = [0.0] * len(tasks)
    for i in order:
        e = tasks[i]["eng"]
        s = free[e]
        for j, x in gap[i]:
            if fin[j] + x > s:
                s = fin[j] + x
        free[e] = fin[i] = s + cost[i]
    return max(f + t["lat"] for f, t in zip(fin, tasks))


def place(tasks, order, cost, gap, first):
    slots = {e: [] for e in ENG}
    fin = [0.0] * len(tasks)
    for i in order:
        s = max([first[i]] + [fin[j] + x for j, x in gap[i]])
        sl = slots[tasks[i]["eng"]]
        k = len(sl)
        while k and sl[k - 1][1] > s:
            k -= 1
        while k < len(sl) and sl[k][0] < s + cost[i]:
            s = max(s, sl[k][1])
            k += 1
        sl.insert(k, (s, s + cost[i]))
        fin[i] = s + cost[i]
    return fin


def sorted_after(key, before):
    key = list(key)
    for i in range(len(key)):
        for j, x in before[i]:
            key[i] = max(key[i], key[j] + 1e-3)
    return sorted(range(len(key)), key=lambda i: (key[i], i))


def justify(tasks, pre, nload):
    n = len(tasks)
    rng = np.random.default_rng(SEED)
    models = [edges(tasks, pre, v) for v in range(len(VARIANTS))]
    cost, gap = models[0]
    back = [[] for _ in range(n)]
    for i in range(n):
        for j, x in gap[i]:
            back[n - 1 - j].append((n - 1 - i, x))
    rtasks, rcost = tasks[::-1], cost[::-1]
    rfirst = [t["lat"] for t in rtasks]
    tail = [0.0] * n
    for i in range(n):
        tail[i] = max([rfirst[i]] + [tail[j] + x for j, x in back[i]]) + rcost[i]
    best = None
    for it in range(PASSES):
        key = [-x for x in tail[::-1]]
        if it % 4:
            key = (np.array(key) + rng.normal(0.0, 40.0 * (it % 4) ** 2, n)).tolist()
        for i in range(nload):
            key[i] = -1e9 + i
        fin = place(tasks, sorted_after(key, gap), cost, gap, [0.0] * n)
        order = sorted_after([f - c for f, c in zip(fin, cost)], gap)
        end = sum(replay(tasks, order, c, x) for c, x in models)
        if best is None or end < best[0]:
            best = (end, order, fin)
        if it % 4 == 3:
            fin = best[2]
        tail = place(rtasks, sorted_after([-x for x in fin[::-1]], back), rcost, back, rfirst)
    return best[1]


def first_order(tasks, pre, nload):
    n = len(tasks)
    named = {}
    for i, t in enumerate(tasks):
        if t["tag"]:
            named.setdefault(t["tag"], []).append(i)
    tied = [set(p) for p in pre]
    free = [set(t["free"]) for t in tasks]
    for before, names in zip(PREP, ISSUE):
        chain = [i for x in before.split() for i in named[(0, x)]] + [i for lv in range(-1, 7) for x in names.split() for i in named.get((lv - (x[0] == "|") + (x[0] == "+"), x.strip("|+")), [])]
        chain = [i for i in chain if tasks[i]["eng"] == ENG[ISSUE.index(names)]]
        chain.sort(key=lambda i: tasks[i]["tag"][0] // 3)
        for j, i in zip(chain, chain[1:]):
            if j not in tied[i] and tasks[i]["tag"][0] // 3 == tasks[j]["tag"][0] // 3:
                tied[i].add(j)
                free[i].add(j)
    perm, done = [], [False] * n
    while len(perm) < n:
        for i in range(n):
            if not done[i] and all(done[j] for j in tied[i]):
                done[i] = True
                perm.append(i)
    at = {i: k for k, i in enumerate(perm)}
    ts = [dict(tasks[i], free=set(at[j] for j in free[i])) for i in perm]
    return [perm[k] for k in justify(ts, [set(at[j] for j in tied[i]) for i in perm], nload)]


def refine(tasks, pre, order, span, stride, moves, heat, soon=0.001, first=0, last=None):
    n = len(tasks)
    rng = np.random.default_rng(SEED)
    eng = [ENG.index(t["eng"]) for t in tasks]
    models = [edges(tasks, pre, v) for v in range(len(VARIANTS))]
    eps = [0.3 if t["lat"] and t["eng"] == "G" else 0.001 if t["tag"] and t["tag"][1][0] not in "RO" else soon for t in tasks]
    fin = [[0.0] * n for v in VARIANTS]
    free0 = [[0.0] * 5 for v in VARIANTS]
    order = list(order)

    def run(seq, keep=False):
        tot = 0.0
        for f, (c, gp), fr, tl, te in zip(fin, models, free0, tail, tend):
            free = fr if keep else fr[:]
            end = 0.0
            for i in seq:
                e = eng[i]
                s = free[e]
                for j, x in gp[i]:
                    if f[j] + x > s:
                        s = f[j] + x
                s += c[i]
                free[e] = f[i] = s
                tot += eps[i] * s
                s += tl[i]
                if s > end:
                    end = s
            tot += max([end] + [x + y for x, y in zip(free, te)])
        return tot
    budget = moves
    for a0 in range(0, max(n - span, 0) + stride, stride)[:last]:
        moves = budget if a0 >= first * stride else 0
        seq = order[a0:a0 + span]
        m = len(seq)
        tail, tend = [[t["lat"] for t in tasks] for v in VARIANTS], [[0.0] * 5 for v in VARIANTS]
        for (c, gp), tl, te in zip(models, tail, tend):
            for i in order[:a0 + span - 1:-1]:
                te[eng[i]] = c[i] + max(tl[i], te[eng[i]])
                for j, x in gp[i]:
                    tl[j] = max(tl[j], te[eng[i]] + x)
        cur = run(seq)
        best = (cur, seq)
        pos, far, way, warm = rng.integers(m, size=moves).tolist(), (rng.exponential(1.2, moves) * rng.choice(np.array([1, 1, 1, 5]), moves)).tolist(), rng.random(moves).tolist(), rng.exponential(1.0, moves).tolist()
        for it in range(moves):
            a = b = pos[it]
            i = seq[b]
            hops, d = 1 + int(far[it]), -1 if way[it] < 0.5 else 1
            while hops and 0 <= a + d < m:
                a += d
                hops -= eng[seq[a]] == eng[i]
            if hops:
                continue
            tied, along, rest = set(pre[i]) if d < 0 else {i}, [], []
            for k in seq[b + d:a:d]:
                if (k in tied) if d < 0 else (pre[k] & tied):
                    along.append(k)
                    tied.update(pre[k] if d < 0 else [k])
                else:
                    rest.append(k)
            if (seq[a] in tied) if d < 0 else (pre[seq[a]] & tied):
                continue
            if d < 0:
                cand = seq[:a] + along[::-1] + [i, seq[a]] + rest[::-1] + seq[b + 1:]
            else:
                cand = seq[:b] + rest + [seq[a], i] + along + seq[a + 1:]
            c = run(cand)
            if c < cur + heat * (1.0 - it / moves) * warm[it]:
                cur, seq = c, cand
                if c < best[0]:
                    best = (c, cand)
        order[a0:a0 + span] = best[1]
        run(best[1][:stride], True)
    return order


def schedule(tasks, nload):
    pre = [set(d) | set(t["ext"][1] if t["ext"] else []) for d, t in zip(depend(tasks), tasks)]
    bank = {}
    for i, t in enumerate(tasks):
        t["free"] = set(t.get("after", [])) - pre[i]
        pre[i] |= t["free"]
        if t["eng"] == "P":
            j = bank.get(t["w"][0][0])
            if j is not None and j not in pre[i]:
                pre[i].add(j)
                t["free"].add(j)
            bank[t["w"][0][0]] = i
    return improve(tasks, pre, nload)


def improve(tasks, pre, nload):
    order = first_order(tasks, pre, nload)
    for x in REFINE:
        order = refine(tasks, pre, order, *x)
    return order


def rank_program(g, core, T, topo):
    r = T.rank_of(core)
    if r is None:
        return
    tasks, queue, exts, nload = plan(r, core, T, topo, g)
    deps = depend(tasks)
    if "all" not in ORDER:
        ORDER["all"] = schedule(plan(1, T.cores[1], T, topo, g)[0], nload)
    order = ORDER["all"]
    hard = [[j for j in d if t["grp"] is None or tasks[j]["grp"] != t["grp"]] for d, t in zip(deps, tasks)]
    needed = set(j for d in hard for j in d)
    count = {e: 0 for e in ENG_SEM}
    mark = {}
    for i in order:
        t = tasks[i]
        if t["sem"] is not None:
            mark[i] = t["sem"]
        elif i in needed:
            count[t["eng"]] += 1
            mark[i] = (ENG_SEM[t["eng"]], count[t["eng"]])
    seen = {e: {} for e in queue}
    for i in order:
        t = tasks[i]
        e = t["eng"]
        want = {}
        for j in hard[i]:
            want[mark[j][0]] = max(want.get(mark[j][0], 0), mark[j][1])
        if t["ext"]:
            want.update(t["ext"][0])
        for s, v in want.items():
            if seen[e].get(s, 0) < v:
                queue[e].wait_ge(T.sem[s], v)
                seen[e][s] = v
        ins = t["fn"] and t["fn"]()
        if t["sem"] is None and i in mark:
            ins.then_inc(T.sem[mark[i][0]], 1)
    ends = {}
    for s, v in list(mark.values()) + [y for x in exts for y in x[0].items()]:
        ends[s] = max(ends.get(s, 0), v)
    for s, v in ends.items():
        if max(seen[e].get(s, 0) for e in seen) < v:
            g.wait_ge(T.sem[s], v)
